import numpy as np, ml_dtypes
CORES = [3,7,11,15,131,135,139,143]
N = 8
BF = ml_dtypes.bfloat16
def gentries(a):
    return np.ascontiguousarray(a.reshape(8, 16, -1).transpose(0, 2, 1)).reshape(8, -1)
def gtable(e):
    e = np.asarray(e); return np.ascontiguousarray(e.reshape(8, -1, 16).transpose(0, 2, 1)).reshape(128, -1).astype(np.int32)
def f(rng, *shape):
    return (rng.standard_normal(shape, dtype=np.float32) * np.exp2(rng.integers(-2, 3, shape[:-1] + (1,)))).astype(BF)
def wide(rng, *shape):
    v = f(rng, *shape).astype(np.float32); k = shape[:-2] + (1, shape[-1])
    return (v * np.exp2(rng.integers(-6, 7, k)) * (rng.random(k) > 0.0625)).astype(BF)
F, P, KD, GEN, LG, RO = 2048, 1536, 2, 8, 3, 2
S, H = F + 2 * P, F // 2
def pointers(pl, b):
    return np.concatenate([np.broadcast_to(np.arange(F), (N, 8, F)), 2 * pl + b], axis=2)
def rise(q):
    for i in range(LG): q = np.take_along_axis(q, q, 2)
    return q
def alleles(rng):
    u = rng.random((N, 8, 16, F), dtype=np.float32)
    return np.floor(16 * u * np.sqrt(u)) * np.exp2(rng.integers(-2, 3, (N, 8, 16, 1))).astype(np.float32)
def generations(rng):
    e = rng.choice(np.array([0.7, 1.0, 1.4]), (N, 8, 1))
    return np.minimum(1 + (GEN * rng.random((N, 8, P)) ** e).astype(np.int64), GEN)
def pedigree(rng, gl, near):
    pl = np.zeros((N, 8, 2 * P), np.int64)
    for r in range(N):
        for g in range(8):
            k = gl[r, g]; o = np.argsort(k, kind="stable"); ids = np.concatenate([np.arange(H), H + o])
            under = np.searchsorted(k[o], np.arange(GEN + 2)); kk = np.repeat(k, 2)
            top = H + under[kk]; low = np.where(kk == 1, 0, H + under[kk - 1])
            low = np.where((rng.random(2 * P) < near) & (low < top), low, 0)
            pl[r, g] = ids[low + (rng.random(2 * P) * (top - low)).astype(np.int64)]
    return pl
def kids(rng, pl):
    kl = rng.integers(F, S, (N, 8, KD, P))
    for r in range(N):
        for g in range(8):
            v = pl[r, g]; o = np.lexsort((rng.random(2 * P), v)); at = np.searchsorted(v[o], H + np.arange(P + 1))
            for k in range(KD):
                kl[r, g, k] = np.where(at[:-1] + k < at[1:], F + o[np.minimum(at[:-1] + k, 2 * P - 1)], kl[r, g, k])
    return kl
def phenotypes(rng, al, pl, tb):
    a = rise(pointers(pl, tb))[:, :, F:].reshape(N, 8, 1, P, 2)
    y = np.maximum(np.take_along_axis(al, a[..., 0], 3), np.take_along_axis(al, a[..., 1], 3))
    return np.where(rng.random(y.shape) < 0.0625, np.take_along_axis(al, rng.integers(0, F, y.shape), 3), y)
def start(rng, tb):
    return tb ^ (rng.random((1, 8, 2 * P)) < 0.2).astype(np.int64) ^ (rng.random((N, 8, 2 * P)) < 0.1).astype(np.int64)
def pack(al, y, pl, b, kl, gl):
    return {"fa": np.ascontiguousarray(al.reshape(N, 128, F)).astype(BF), "ph": np.ascontiguousarray(y.reshape(N, 128, P)).astype(BF),
            "par": np.stack([gtable(a) for a in pl]), "sw": np.stack([gtable(a) for a in b]),
            "kd": np.stack([gtable(a.reshape(8, -1)) for a in kl]), "gen": np.ascontiguousarray(gl).astype(np.int32)}
def finish(rng, al, gl, pl, kl):
    tb = rng.integers(0, 2, (N, 8, 2 * P)); y = phenotypes(rng, al, pl, tb)
    return pack(al, y, pl, start(rng, tb), kl, gl)
def own():
    return F + 2 * np.arange(P)[None, :] + np.arange(KD)[:, None] % 2
def setup_inputs(rng):
    al = alleles(rng); gl = generations(rng); pl = pedigree(rng, gl, 0.85)
    return finish(rng, al, gl, pl, kids(rng, pl))
def setup_inputs_deep(rng):
    al = alleles(rng); gl = np.tile(GEN - np.arange(P) * GEN // P, (N, 8, 1)); gl[:, 1::2] = rng.permuted(gl[:, 1::2], axis=2)
    pl = pedigree(rng, gl, 1.0); one = np.repeat(gl[:, 0], 2, axis=1) == 1
    pl[:, 0] = np.where(one, rng.choice(np.array([0, H - 1]), one.shape), pl[:, 0])
    return finish(rng, al, gl, pl, kids(rng, pl))
def setup_inputs_full(rng):
    h = H // 2; up = rng.integers(0, 2, (N, 8, H)); v = rng.integers(0, 4, (N, 8, 16, H, 2))
    tall = up[:, :, None, :h, None] == np.arange(2)
    v[:, :, :, :h] = np.where(tall, rng.integers(10, 16, (N, 8, 16, h, 2)), rng.integers(4, 10, (N, 8, 16, h, 2)))
    unit = np.exp2(rng.integers(-2, 3, (N, 8, 16, 1))).astype(np.float32); al = v.reshape(N, 8, 16, F).astype(np.float32) * unit
    e = rng.integers(0, 2, (8, P)); pl = rng.integers(h, H, (N, 8, P, 2)); tb = rng.integers(0, 2, (N, 8, P, 2)); b = tb.copy()
    gl = np.full((N, 8, P), 2); kl = rng.integers(F, S, (N, 8, KD, P)); near = np.zeros((8, P), bool); weak = np.zeros((N, 8, P), bool)
    top = min(GEN, 8); n = -(-P // (2 ** top - 1)); size = [P - n * (2 ** (top - 1) - 1)] + [n * 2 ** (top - i) for i in range(2, top + 1)]
    for g in range(8):
        o = rng.permutation(P); band = np.split(o, np.add.accumulate(size)[:-1]); hit = o
        if g % 2 == 0:
            hit = band[0][:size[0] // 2]; rest = band[0][size[0] // 2:]; near[g, hit] = rng.random(len(hit)) < 0.5
            for i in range(top): gl[:, g, band[i]] = i + 1
        for r in range(N):
            x = rng.integers(0, h, len(hit)); pl[r, g, hit, e[g, hit]] = x; tb[r, g, hit, e[g, hit]] = up[r, g, x]; b[r, g, hit, e[g, hit]] = 1 - up[r, g, x]
            if g % 2: continue
            kid = band[1]; s = e[g, kid]
            x = rng.permutation(np.concatenate([hit, rng.choice(hit, len(kid) - len(hit))])); z = rng.permutation(np.concatenate([rest, rng.choice(rest, len(kid) - len(rest))]))
            pl[r, g, kid, s] = H + x; tb[r, g, kid, s] = e[g, x]; b[r, g, kid, s] = e[g, x]; pl[r, g, kid, 1 - s] = H + z; weak[r, g, kid] = near[g, x]
            for i in range(2, top): pl[r, g, band[i]] = H + rng.permutation(band[i - 1]).reshape(-1, 2)
            w = pl[r, g].reshape(-1); far = np.flatnonzero(w >= H); one = F + 2 * np.arange(P); one[w[far] - H] = F + far; kl[r, g] = one
    pl = pl.reshape(N, 8, 2 * P); tb = tb.reshape(N, 8, 2 * P); b = b.reshape(N, 8, 2 * P)
    def seen(c):
        a = rise(pointers(pl, c))[:, :, F:].reshape(N, 8, 1, P, 2)
        return np.maximum(np.take_along_axis(al, a[..., 0], 3), np.take_along_axis(al, a[..., 1], 3))
    y = np.where(near[None, :, None, :], seen(b), seen(tb))
    off = weak[:, :, None, :] & (np.argsort(rng.random((N, 8, 16, P)), axis=2) >= 16 // (KD - 1))
    return pack(al, np.where(off, 16 * unit, y), pl, b, kl, gl)
def setup_inputs_ties(rng):
    al = alleles(rng); al[..., 1:H // 2:2] = al[..., 0:H // 2:2]
    lot = np.argsort(rng.random((8, P)), axis=1); mz = lot < P // 8; mx = lot < 5 * P // 8
    gl = generations(rng); gl[:, mz] = 2
    pl = pedigree(rng, gl, 0.85); v = pl.reshape(N, 8, P, 2)
    v[..., 0] = np.where(mz, rng.integers(0, H // 4, (N, 8, P)), v[..., 0]); v[..., 1] = np.where(mx, v[..., 0], v[..., 1])
    kl = np.where(mx[:, None, :], own(), kids(rng, pl))
    tb = rng.integers(0, 2, (N, 8, 2 * P)); w = tb.reshape(N, 8, P, 2)
    w[..., 0] = np.where(mx, 0, w[..., 0]); w[..., 1] = np.where(mx, 1, w[..., 1])
    y = phenotypes(rng, al, pl, tb); b = np.ascontiguousarray(start(rng, tb)); w = b.reshape(N, 8, P, 2)
    w[..., 1] = np.where(mx, w[..., 0], w[..., 1])
    return pack(al, y, pl, b, kl, gl)
def setup_inputs_kids(rng):
    al = alleles(rng); gl = generations(rng); gl[:, 3] = 2; gl[:, 3, 0] = 1; gl[:, 3, P - 1] = 1; gl[:, 7] = 1
    pl = pedigree(rng, gl, 0.85); two = np.repeat(gl[:, 3], 2, axis=1) == 2; one = np.repeat(gl[:, 5], 2, axis=1) == 1
    pl[:, 3] = np.where(two, rng.choice(np.array([H, H + P - 1]), two.shape), pl[:, 3])
    pl[:, 5] = np.where(one, rng.choice(np.array([0, H - 1]), one.shape), pl[:, 5])
    kl = kids(rng, pl); kl[:, 0::2] = kl[:, 0::2, :1].copy()
    kl[:, 1] = np.where(rng.random((N, KD, P)) < 0.5, own(), rng.choice(np.array([F, S - 1]), (N, KD, P)))
    return finish(rng, al, gl, pl, kl)
def setup_inputs_spread(rng):
    al = wide(rng, N, 128, F).astype(np.float32).reshape(N, 8, 16, F) * np.exp2(rng.integers(-40, 41, (N, 8, 16, 1))).astype(np.float32)
    gl = generations(rng); pl = pedigree(rng, gl, 0.6)
    return finish(rng, al, gl, pl, kids(rng, pl))
def check_inputs(d):
    bad = []
    for k in ("fa", "ph"):
        if not np.all(np.isfinite(d[k].astype(np.float32))): bad.append("finite numbers in " + k)
    low = len(bad)
    for k, lo, hi in (("par", 0, S // 2 - 1), ("sw", 0, 1), ("kd", F, S - 1), ("gen", 1, GEN)):
        if np.min(d[k]) < lo or np.max(d[k]) > hi: bad.append("range of " + k)
    if len(bad) == low:
        gl = d["gen"].astype(np.int64); pl = np.stack([gentries(a) for a in d["par"]]).astype(np.int64)
        age = np.concatenate([np.zeros((N, 8, H), np.int64), gl], axis=2)
        if np.any(np.take_along_axis(age, pl, 2) >= np.repeat(gl, 2, axis=2)): bad.append("generations of parents")
    return bad
def reference(fa, ph, par, sw, kd, gen):
    al = fa.astype(np.float32).reshape(N, 8, 16, F); y = np.repeat(ph.astype(np.float32).reshape(N, 8, 16, P), 2, axis=3)
    pl = np.stack([gentries(a) for a in par]).astype(np.int64); b = np.stack([gentries(a) for a in sw]).astype(np.int64)
    kl = np.stack([gentries(a) for a in kd]).astype(np.int64).reshape(N, 8, KD, P); gl = np.repeat(gen.astype(np.int64), 2, axis=2)
    first = np.broadcast_to(np.arange(F), (N, 8, F)); slot = np.arange(F, S).reshape(P, 2); even = np.arange(2 * P) % 2 == 0
    def match(a, other):
        u = np.take_along_axis(al, a[:, :, None, :], 3); v = np.take_along_axis(al, other[:, :, None, :], 3)
        return np.add.reduce(y == np.maximum(u, v), axis=2, dtype=np.int64)
    for t in range(1, RO + 1):
        q = pointers(pl, b); a = rise(q)
        alt = np.concatenate([first, np.take_along_axis(a, q[:, :, F:] ^ 1, 2)], axis=2)
        alt2 = np.take_along_axis(alt, q[:, :, F:], 2)
        mine = a[:, :, F:]; other = np.ascontiguousarray(mine.reshape(N, 8, P, 2)[..., ::-1]).reshape(N, 8, 2 * P)
        base = match(mine, other)
        g0 = match(alt[:, :, F:], other) - base; g1 = match(alt2, other) - base
        vote = g0.reshape(N, 8, P, 2)
        for k in range(KD):
            up = np.take_along_axis(q, kl[:, :, k], 2); gk = np.take_along_axis(g1, kl[:, :, k] - F, 2)
            vote = vote + np.where(up[..., None] == slot, gk[..., None], 0)
        vote = np.add.reduce(vote, axis=0)
        mate = np.ascontiguousarray(vote[..., ::-1]).reshape(8, 2 * P); vote = vote.reshape(8, 2 * P)
        go = (vote > 0) & ((vote > mate) | ((vote == mate) & even))
        b = np.where(go[None] & (gl % 2 == t % 2), 1 - b, b)
    a = rise(pointers(pl, b))[:, :, F:]
    return {"ya": np.stack([gtable(e) for e in a]).astype(np.float32), "ys": np.stack([gtable(e) for e in b]).astype(np.float32)}

@@ -1,0 +1,425 @@
+from concourse.bass import DstId, RemoteDMATransfer
+from concourse.mybir import AluOpType as A, AxisListType, ActivationFunctionType as AF
+
+NF, NP, NS, KC = 2048, 1536, 3072, 96
+BF, F32, I32, U16 = "bfloat16", "float32", "int32", "uint16"
+ZW = 144
+ZA1, ZP, ZA, ZG, ZSP, ZSM = range(6)
+
+
+def _sb(n, d):
+    return ("sbuf", [128, n], d)
+
+
+SCRATCH = {
+    "tab": _sb(5120, BF), "wb": _sb(8192, BF), "w4": _sb(NS, BF), "xb": _sb(8192, BF), "xc": _sb(NS, BF),
+    "phs": _sb(NP, BF), "yp": _sb(NP, BF), "mx": _sb(NP + NS, BF), "m1": _sb(NS, BF),
+    "sg": _sb(NP + NS, BF), "ne": _sb(NP + NS, BF), "ne1": _sb(NS, BF), "gw": _sb(NS, BF), "go": _sb(NS, BF),
+    "pari": _sb(192, I32), "swi": _sb(192, I32), "kdi": _sb(192, I32), "geni": _sb(KC, I32), "gen1": _sb(KC, I32),
+    "genf": _sb(KC, F32), "genb": _sb(KC, BF), "g8": _sb(NP, BF),
+    "ta": _sb(192, F32), "tb": _sb(192, F32), "tc": _sb(192, F32), "mu": _sb(192, F32), "td": _sb(192, F32), "te": _sb(192, F32),
+    "q0": _sb(192, F32), "q1": _sb(192, F32), "q2": _sb(192, F32), "dl": _sb(192, F32), "qhi": _sb(192, F32), "qsum": _sb(192, F32),
+    "big": _sb(384, F32), "thr": _sb(192, F32), "yso": _sb(192, F32), "yao": _sb(192, F32),
+    "uq": _sb(192, U16), "u2": _sb(192, U16), "u4": _sb(192, U16), "u4c": _sb(192, U16), "up": _sb(384, U16), "uk": _sb(192, U16),
+    "tg0": _sb(192, F32), "tgt": _sb(192, F32), "mk": _sb(384, F32), "ck": _sb(384, BF),
+    "vs0": _sb(192, BF), "vs1": _sb(192, BF), "vs2": _sb(KC, BF),
+    "land0": _sb(8 * 192, BF), "land1": _sb(8 * 192, BF), "land2": _sb(8 * KC, BF),
+    "i1": _sb(8, I32), "i2": _sb(8, I32), "rt": _sb(8, F32), "cs": _sb(16, F32), "j8": _sb(8, F32), "hc": _sb(8, F32),
+    "lo": _sb(256, BF), "zz": _sb(6 * ZW, BF), "z8": _sb(ZW, BF), "idn": _sb(4 * 128 + ZW, BF),
+    "ps": ("psum", [128, 4096], F32),
+}
+QUEUES = ["v", "s", "t", "g"]
+NDMA = 24
+SEMAPHORES = ["c_" + q for q in QUEUES] + ["d%d" % i for i in range(NDMA)] + ["arr0", "arr1", "arr2", "sent"]
+
+SPLIT = {"a0": (48, 48), "a": (46, 44), "b": (46, 48), "c": (40, 46), "d": (42, 44), "e": (40, 32), "f": (44, 44), "g": (42, 50)}
+MATCH = ("M.0 M.1 M.2 d.1 n.0 M.6 M.8 sg.1 M.7 d.2 sg.2 ab.1 d.6 M.3 ab.2 d.8 n.7 sg.6 ab.6 Z sg.8 n.3 ab.8 M.4 M.5 G.4 C.4 n.4 G.5 C.5 "
+         "n.5 G.6 M1.0 C.6 G.7 G.0 C.7 C.0 G.1 C.1 G.2 M1.1 G.3 B.0 C.2 C.3 B.1 K.0 n1.0 n1.1 M1.2 n1.2 V.0 U.0 K.1 U.1 K.2 V.1 U.2 "
+         "M1.3 mk.0 ck.0 K.3 n1.3 AD.0 U.3 mk.1 ck.1 V.2 AD.1").split()
+
+
+def rank_program(g, core, T, topo):
+    rank = T.rank_of(core)
+    if rank is None:
+        return
+    Q = {"v": g.vector, "s": g.scalar, "t": g.tensor, "g": g, "y": g.sync}
+    cnt = {q: 0 for q in QUEUES}
+    known = {q: {} for q in Q}
+    recs = {}
+    ndma = [0]
+
+    def R(name, lo, hi, step=1, p=128):
+        return (name, lo, hi, step, p)
+
+    def ap(r):
+        return T[r[0]][0:r[4], r[1]:r[2]:r[3]] if r[3] > 1 else T[r[0]][0:r[4], r[1]:r[2]]
+
+    def need(q, tok):
+        if known[q].get(tok[0], 0) < tok[1]:
+            Q[q].wait_ge(T.sem[tok[0]], tok[1])
+            known[q][tok[0]] = tok[1]
+            for k, v in tok[2].items():
+                if known[q].get(k, 0) < v:
+                    known[q][k] = v
+
+    def op(q, fn, reads, writes, dma=False):
+        deps = {}
+        for rs, w in ((reads, False), (writes, True)):
+            for r in rs:
+                for (lo, hi, tok, eq, ew) in recs.get(r[0], []):
+                    hit = lo < r[2] and r[1] < hi and (w or ew)
+                    if r[0] == "ps":
+                        if eq != q:
+                            hit = lo // 512 <= (r[2] - 1) // 512 and r[1] // 512 <= (hi - 1) // 512
+                        elif q == "t":
+                            hit = False
+                    if hit and deps.get(tok[0], (0, 0))[1] < tok[1]:
+                        deps[tok[0]] = tok
+        for tok in sorted(deps.values(), key=lambda t: t[0] == "c_" + q):
+            need(q, tok)
+        ins = fn()
+        if dma:
+            name = "d%d" % ndma[0]
+            ndma[0] += 1
+            ins.then_inc(T.sem[name], 16)
+            tok = (name, 16, dict(known[q]))
+        else:
+            cnt[q] += 1
+            ins.then_inc(T.sem["c_" + q], 1)
+            tok = ("c_" + q, cnt[q], dict(known[q]))
+        for rs, w in ((reads, False), (writes, True)):
+            for r in rs:
+                l = recs.setdefault(r[0], [])
+                if w and r[3] == 1 and r[0] != "ps":
+                    l[:] = [x for x in l if not (r[1] <= x[0] and x[1] <= r[2])]
+                l.append((r[1], r[2], tok, "dma" if dma else q, w))
+        return tok
+
+    def ts(out, in0, s1, s2, o0, o1=None):
+        rd = [in0] + [s for s in (s1, s2) if isinstance(s, tuple)]
+        a1, a2 = [ap(s) if isinstance(s, tuple) else s for s in (s1, s2)]
+        if o1 is None:
+            return op("v", lambda: g.vector.tensor_scalar(ap(out), ap(in0), a1, None, o0), rd, [out])
+        return op("v", lambda: g.vector.tensor_scalar(ap(out), ap(in0), a1, a2, o0, o1), rd, [out])
+
+    def tt(out, a, b, o):
+        return op("v", lambda: g.vector.tensor_tensor(ap(out), ap(a), ap(b), o), [a, b], [out])
+
+    def cp(out, a):
+        return op("v", lambda: g.vector.tensor_copy(ap(out), ap(a)), [a], [out])
+
+    def act(out, a, f, bias=None, scale=None):
+        kw = {}
+        if bias is not None:
+            kw["bias"] = ap(bias)
+        if scale is not None:
+            kw["scale"] = ap(scale)
+        return op("s", lambda: g.scalar.activation(ap(out), ap(a), f, **kw), [a] + [x for x in (bias, scale) if x], [out])
+
+    def gather(q, out, win, off, other=None):
+        src = lambda: ap(win).indirect(ap(off))
+        if other is not None:
+            return op("v", lambda: g.vector.tensor_tensor(ap(out), src(), ap(other), A.max), [win, off, other], [out])
+        if q == "v":
+            return op("v", lambda: g.vector.tensor_copy(ap(out), src()), [win, off], [out])
+        return op("s", lambda: g.scalar.activation(ap(out), src(), AF.Copy), [win, off], [out])
+
+    def mm(items, start=True, stop=True):
+        def fn():
+            for n, (o, l, r) in enumerate(items):
+                ins = g.tensor.matmul(ap(o), ap(l), ap(r), start and n == 0, stop and n == len(items) - 1)
+            return ins
+        return op("t", fn, [x for it in items for x in it[1:]], [it[0] for it in items])
+
+    def iota(out, pat, base, cm, small=True):
+        kw = {"allow_small_or_imprecise_dtypes": True} if small else {}
+        return op("g", lambda: g.iota(ap(out), pat, base, cm, **kw), [], [out])
+
+    def asel(out, a, pat, cmp, fill, base, cm):
+        return op("g", lambda: g.affine_select(ap(out), ap(a), pat, cmp, fill, base, cm), [a], [out])
+
+    def dma(q, out, in_, reads, writes):
+        return op(q, lambda: Q[q].dma_start(out, in_), reads, writes, dma=True)
+
+    def PS(b, lo, hi):
+        return R("ps", 512 * b + lo, 512 * b + hi)
+
+    def Z(s, i):
+        return R("zz", s * ZW + 15 - i, s * ZW + 143 - i)
+
+    def ID(k):
+        return R("idn", 128 * k, 128 * k + 128)
+
+    def col(name, k):
+        return R(name, k, k + 1)
+
+    def wrap(out, s, src, lo, n):
+        return [(out, Z(s, i), R(src, lo + i, lo + 16 * n, 16)) for i in range(16)]
+
+    H = [lambda n, e=e: R(n, KC * e, KC * e + KC) for e in range(2)]
+    W = lambda n: R(n, 0, 192)
+
+    for e in range(2):
+        dma("y", ap(H[e]("pari")), T.par[e::2, :], [], [H[e]("pari")])
+        dma("s", ap(H[e]("swi")), T.sw[e::2, :], [], [H[e]("swi")])
+    dma("y", ap(R("xb", NS, NS + NF)), T.fa[:], [], [R("xb", NS, NS + NF)])
+    dma("y", T.phs[:], T.ph[:], [], [R("phs", 0, NP)])
+    dma("y", T.kdi[:], T.kd[:], [], [W("kdi")])
+    dma("y", T.geni[:], T.gen[:], [], [R("geni", 0, KC)])
+
+    iota(R("i1", 0, 8), [[-1, 8]], 16, 1, False)
+    iota(R("j8", 0, 8), [[1, 8]], 0, 0)
+    iota(R("lo", 0, 256), [[1, 256]], 0, 0)
+    ts(R("i2", 0, 8), R("i1", 0, 8), 15, None, A.bitwise_and)
+    ts(R("rt", 0, 8), R("i2", 0, 8), 0.0, None, A.is_equal)
+    cp(col("cs", 9), col("i2", 0))
+    red = lambda o, a: op("v", lambda: g.vector.tensor_reduce(ap(o), ap(a), AxisListType.X, A.add), [a], [o])
+    red(col("cs", 0), R("rt", 0, 5, 2))
+    ts(col("cs", 2), col("rt", 0), 12.0, None, A.mult)
+    red(col("cs", 1), R("rt", 1, 4, 2))
+    ts(col("cs", 3), col("rt", 4), 8.0, None, A.mult)
+    ts(R("hc", 0, 8), R("j8", 0, 8), col("cs", 0), col("cs", 2), A.mult, A.add)
+    ts(col("cs", 4), col("rt", 4), 14.0, None, A.mult)
+    ts(col("cs", 5), col("rt", 2), 14.0, col("cs", 3), A.mult, A.add)
+    ts(col("cs", 6), col("rt", 2), 8.0, col("cs", 4), A.mult, A.add)
+    ts(col("cs", 7), col("rt", 0), -12.0, col("cs", 5), A.mult, A.add)
+    ts(col("cs", 8), col("rt", 0), -6.0, col("cs", 6), A.mult, A.add)
+    for j in range(8):
+        o = R("wb", NS + 256 * j, NS + 256 * j + 256)
+        if j >= 3:
+            ts(o, R("lo", 0, 256), col("cs", 1), col("hc", j), A.mult, A.add)
+        else:
+            act(o, R("lo", 0, 256), AF.Identity, col("hc", j), col("cs", 1))
+    act(R("tab", NF + NP, NF + NS), R("wb", NS, NS + NP), AF.Identity, col("cs", 8))
+    act(R("tab", NF, NF + NP), R("wb", NS, NS + NP), AF.Identity, col("cs", 7))
+
+    ts(W("mu"), W("pari"), 1024.0, 1535.0, A.is_ge, A.mult)
+    ts(W("ta"), W("pari"), 2.0, None, A.mult)
+    ts(W("tb"), W("pari"), 1792.0, -1535.0, A.is_ge, A.mult)
+    ts(W("mu"), W("mu"), 1.0, None, A.add)
+    tt(W("td"), W("ta"), W("tb"), A.add)
+    tt(W("te"), W("mu"), W("swi"), A.mult)
+    ts(R("tab", 0, NF, 2), R("wb", NS, NS + NF, 2), col("rt", 3), None, A.add)
+    tt(W("q0"), W("td"), W("te"), A.add)
+    ts(R("tab", 1, NF, 2), R("wb", NS + 1, NS + NF, 2), col("rt", 3), None, A.subtract)
+    cp(W("uq"), W("q0"))
+
+    iota(R("zz", 0, 6 * ZW), [[0, 6 * ZW]], 0, 0)
+    iota(R("idn", 512, 512 + ZW), [[0, ZW]], 0, 0)
+    iota(W("tg0"), [[NP, 2], [16, KC]], 0, 0)
+    zc = lambda s: R("zz", s * ZW + 15, s * ZW + 143, 16)
+    for n in range(2):
+        for s, rows in ((ZA1, (0, 1)), (ZP, (2, 3)), (ZA, (4, 1))):
+            asel(zc(s), zc(s), [[-16, 8]], A.not_equal, (256.0, 1.0)[n], -rows[n], 1)
+        for s, v in ((ZSP, 1.0), (ZSM, -1.0)):
+            asel(zc(s), zc(s), [[16, 8]], A.is_gt, (v, 0.0)[n], 16 * n, -1)
+    asel(zc(ZG), zc(ZG), [[-16, 8]], A.not_equal, 1.0, -2, 1)
+    for k, v in enumerate((1.0, 0.5, -0.5)):
+        asel(ID(k), ID(4), [[-1, 128]], A.not_equal, v, 0, 1)
+    for b in range(2):
+        asel(R("yp", b, NP, 2), R("phs", 768 * b, 768 * b + 768), [[0, 768]], A.is_ge, 0.0, 0, 0)
+    asel(ID(3), ID(0), [[0, 8], [-1, 16]], A.is_ge, 0.0, 1, 0)
+    asel(R("z8", 0, ZW, 1, 8), R("idn", 512, 512 + ZW, 1, 8), [[1, ZW]], A.not_equal, 1.0, -15, -16)
+
+    def late():
+        ts(W("uk"), W("kdi"), -float(NF), None, A.add)
+        ts(W("tgt"), W("tg0"), col("cs", 9), None, A.add)
+
+    def stage(win, off, dst, lo, split, zs, take, before, mid=None, after=None):
+        a, b = split
+
+        def part(q, c0, c1):
+            gather(q, R(dst, lo + 16 * c0, lo + 16 * c1), win, R(off, c0, c1))
+            if after:
+                after(16 * c0, 16 * c1)
+        part("v", 0, a)
+        part("s", a, KC)
+        if zs is not None:
+            mm(wrap(PS(3, 0, KC), zs, dst, lo, KC))
+        if before:
+            before()
+        if mid:
+            mid()
+        part("v", KC, KC + b)
+        part("s", KC + b, 192)
+        if zs is None:
+            return None
+        mm(wrap(PS(4, 0, KC), zs, dst, lo + NP, KC))
+        take(0)
+        return lambda: take(1)
+
+    WA, WA1, PB = R("wb", NS, 8192), R("wb", 0, NS + NF), NS + NF
+    to = lambda name: (lambda h: cp(H[h](name), PS(3 + h, 0, KC)))
+
+    def take4(h):
+        ts(H[h]("u4c"), PS(3 + h, 0, KC), -float(NS), 0.0, A.add, A.max)
+        cp(H[h]("u4"), PS(3 + h, 0, KC))
+
+    near = [c for c in T.cores if c != core and c in topo.cores_of(core)]
+    far = [c for c in T.cores if c not in topo.cores_of(core)]
+    far_mask = topo.mask(core, far[0])
+    near_mask = topo.mask(core, near[0]) & ~far_mask
+    n_eng = len(topo.engines(core, far[0]))
+    sent = [0]
+
+    def exchange(n, w):
+        vs, land = R("vs%d" % n, 0, w), T["land%d" % n][:, w * rank:w * rank + w]
+        for (lo, hi, tok, eq, ew) in recs[vs[0]]:
+            need("g", tok)
+        tr = []
+        for cs, m in ((far, far_mask), (near, near_mask)):
+            ids = [DstId(rid=topo.addr(c, core)[0], pnc=topo.addr(c, core)[1]) for c in cs]
+            tr.append(RemoteDMATransfer(dst_ids=ids, dma_engine_mask=m, remote_sem=T.sem["arr%d" % n], srcs=[ap(vs)], dsts=[land] * len(cs)))
+        g.remote_dma_fused(tr, local_sem=T.sem.sent)
+        sent[0] += 2 * n_eng
+
+    def match(t):
+        XW, bank = R("xb", NS, 8192), {}
+        last = [x for x in MATCH if x[0] in "BV" or x == "AD.0"][-1]
+
+        def mx(dst, off, lo, n):
+            z = (lo + NP) % NS
+            gather("v", dst, XW, R("up", off + lo // 16, off + (lo + n) // 16), R("xc", z, z + n))
+        for step in MATCH:
+            k, c = (step.split(".") + ["0"])[:2]
+            c = int(c)
+            ch = lambda n, w=512: R(n, w * c, w * c + w)
+            y = 512 * (c % 3)
+            if k == "M":
+                if c < 3:
+                    tt(ch("mx"), PS(5 + c, 0, 512), R("xb", PB + NP + y, PB + NP + y + 512), A.max)
+                else:
+                    mx(ch("mx"), 192, 512 * (c - 3), 512)
+            elif k == "M1":
+                mx(ch("m1", 768), 0, 768 * c, 768)
+            elif k == "d":
+                bank[c] = PS(3 + len(bank) % 2, 0, 512)
+                mm([(bank[c], ID(1), ch("mx")), (bank[c], ID(2), R("yp", y, y + 512))])
+            elif k == "sg":
+                act(ch("sg"), bank[c], AF.Sign)
+            elif k == "ab":
+                act(ch("ne"), ch("sg"), AF.Abs)
+            elif k == "n":
+                tt(ch("ne"), PS(0, y, y + 512), ch("mx"), A.not_equal)
+            elif k == "n1":
+                y = 768 * (c % 2)
+                tt(ch("ne1", 768), PS(0, y, y + 768), ch("m1", 768), A.not_equal)
+            elif k == "G":
+                lo, b = 768 * (c // 2), c % 2
+                o = PS(5 + b, 0, 384)
+                mm([(o, ID(3), R("wb", PB + lo + b, PB + lo + 768, 2)), (o, Z(ZSP, 2), R("ne", lo % NP + b, lo % NP + 768, 2)),
+                    (o, Z(ZSM, 2), R("ne", NP + lo + b, NP + lo + 768, 2))])
+            elif k == "C":
+                e, h, b = c // 4, c // 2 % 2, c % 2
+                lo = 2 * (768 * b + 384 * h) + e
+                act(R("gw", lo, lo + 767, 2), PS(5 + b, 0, 384), AF.Copy)
+            elif k == "Z":
+                if t == 0:
+                    mm(wrap(PS(7, 0, KC), ZSP, "ne", 0, KC))
+                    act(H[0]("vs2"), PS(7, 0, KC), AF.Copy)
+                    exchange(2, KC)
+                mm([(PS(7, 0, 192), ID(4), W("yp"))], True, False)
+            elif k == "B":
+                if t:
+                    mm(wrap(PS(7, KC * c, KC * c + KC), ZSP, "ne", 0, KC), False, step == last)
+            elif k == "V":
+                c0, n = ((0, KC), (KC, 48), (KC + 48, 48))[c]
+                mm(wrap(PS(7, c0, c0 + n), ZSM, "ne1", 16 * c0, n), False, step == last)
+            elif k == "K":
+                gather("s", ch("go", 768), R("gw", 0, NS), ch("uk", 48))
+            elif k == "U":
+                kk, b = c // 2, c % 2
+                for n, zs in enumerate((ZA1, ZG)):
+                    mm([(PS(3 + 2 * kk + n, 0, KC), Z(zs, 2 * a + b), R("go", 768 * c + a, 768 * c + 768, 8)) for a in range(8)], b == 0, b == 1)
+            elif k == "mk":
+                for e in range(2):
+                    tt(R("mk", 192 * c + KC * e, 192 * c + KC * e + KC), PS(3 + 2 * c, 0, KC), H[e]("tgt"), A.is_equal)
+            elif k == "ck":
+                for e in range(2):
+                    lo = 192 * c + KC * e
+                    tt(R("ck", lo, lo + KC), PS(4 + 2 * c, 0, KC), R("mk", lo, lo + KC), A.mult)
+            elif k == "AD":
+                if c == 0:
+                    mm([(PS(7, 0, 192), ID(0), ch("ck", 192))], False, step == last)
+                else:
+                    tt(W("vs%d" % t), PS(7, 0, 192), ch("ck", 192), A.add)
+
+    def decide(t):
+        P = lambda b, e: PS(b, KC * e, KC * e + KC)
+        others = [r for r in range(len(T.cores)) if r != rank]
+        mm([(PS(3, 0, 192), ID(0), W("vs%d" % t))], True, False)
+        if t == 0:
+            need("t", ("arr2", n_eng * len(others), {}))
+            mm([(P(3, e), ID(0), x) for e in range(2) for x in [H[0]("vs2")] + [R("land2", KC * r, KC * r + KC) for r in others]], False, False)
+        need("t", ("arr%d" % t, n_eng * len(others), {}))
+        mm([(PS(3, 0, 192), ID(0), R("land%d" % t, 192 * r, 192 * r + 192)) for r in others], False, True)
+        qn = "q%d" % (t + 1)
+        for e in range(2):
+            tt(H[e]("thr"), P(3, 1 - e), R("big", 192 * t + KC * e, 192 * t + KC * e + KC), A.max)
+        for e in range(2):
+            tt(P(4, e), P(3, e), H[e]("thr"), (A.is_ge, A.is_gt)[e])
+        for e in range(2):
+            tt(P(5, e), P(4, e), H[e]("dl"), A.mult)
+        for e in range(2):
+            tt(H[e](qn), P(5, e), H[e]("q%d" % t), A.add)
+        for e in range(2):
+            cp(H[e]("uq"), H[e](qn))
+
+    for t in range(3):
+        mid = None
+        if t == 2:
+            def mid():
+                tt(W("yso"), W("q2"), W("qhi"), A.is_equal)
+                for e in range(2):
+                    dma("y", T.ys[e::2, :], ap(H[e]("yso")), [H[e]("yso")], [])
+        stage(R("tab", 0, 5120), "uq", "wb", PB, SPLIT["a" if t else "a0"], None, None, None, mid)
+        rest = stage(WA, "uq", "wb", 0, SPLIT["b"], ZA1, to("u2"), None)
+        if t == 2:
+            rest = stage(WA1, "u2", "wb", PB, SPLIT["f"], ZA, to("u4"), rest)
+
+            def put(h):
+                cp(H[h]("yao"), PS(3 + h, 0, KC))
+                dma("y", T.ya[h::2, :], ap(H[h]("yao")), [H[h]("yao")], [])
+            stage(WA, "u4", "w4", 0, SPLIT["g"], ZA, put, rest)()
+            break
+        rest = stage(WA1, "u2", "w4", 0, SPLIT["c"], ZA1, take4, rest)
+
+        def partners():
+            mm(wrap(PS(3, 0, 192), ZP, "wb", PB, 192))
+            mm(wrap(PS(3, 192, 384), ZP, "wb", 0, 192))
+            if t == 0:
+                for b in range(3):
+                    mm([(PS(b, 0, 512), ID(0), R("yp", 512 * b, 512 * b + 512))])
+                late()
+        stage(R("xb", NS, NS + NF), "u4c", "xb", 0, SPLIT["d"], None, None, rest, partners)
+
+        def hold():
+            for b in range(3):
+                mm([(PS(5 + b, 0, 512), ID(0), R("xb", PB + 512 * b, PB + 512 * b + 512))])
+            cp(R("up", 0, 384), PS(3, 0, 384))
+
+        def twin(lo, hi):
+            dma("y", ap(R("xc", lo, hi)), ap(R("xb", PB + lo, PB + hi)), [R("xb", PB + lo, PB + hi)], [R("xc", lo, hi)])
+        stage(R("xb", 0, NS + NF), "u4", "xb", PB, SPLIT["e"], None, None, None, hold, twin)
+        match(t)
+        exchange(t, 192)
+        if t == 0:
+            ts(R("gen1", 0, KC), R("geni", 0, KC), 1, None, A.bitwise_and)
+            tt(W("qhi"), W("td"), W("mu"), A.add)
+            cp(R("genf", 0, KC), R("gen1", 0, KC))
+            tt(W("qsum"), W("td"), W("qhi"), A.add)
+            cp(R("genb", 0, KC), R("genf", 0, KC))
+            dma("y", T.g8[0:8, :], T.genb[:], [R("genb", 0, KC)], [R("g8", 0, NP)])
+            mm([(PS(4, 0, KC), R("z8", 15 - i, 143 - i, 1, 8), R("g8", 768 * (i % 2) + i // 2, 768 * (i % 2) + 768, 8, 8)) for i in range(16)])
+        ts(W("tc"), W("q%d" % t), -2.0, None, A.mult)
+        tt(W("dl"), W("qsum"), W("tc"), A.add)
+        if t == 0:
+            for n, (m, c) in enumerate(((-999.0, 1000.0), (-1000.0, 1000.0), (999.0, 1.0), (1000.0, 0.0))):
+                ts(R("big", KC * n, KC * n + KC), PS(4, 0, KC), m, c, A.mult, A.add)
+        decide(t)
+
+    g.wait_ge(T.sem.sent, sent[0])
+    for q in QUEUES:
+        need("g", ("c_" + q, cnt[q], {}))
+    for n in range(ndma[0]):
+        need("g", ("d%d" % n, 16, {}))

@@ -23,19 +23,19 @@ SCRATCH = {
     "uq": _sb(192, U16), "u2": _sb(192, U16), "u4": _sb(192, U16), "u4c": _sb(192, U16), "up": _sb(384, U16), "uk": _sb(192, U16),
     "tg0": _sb(192, F32), "tgt": _sb(192, F32), "mk": _sb(384, F32), "ck": _sb(384, BF),
     "vs0": _sb(192, BF), "vs1": _sb(192, BF), "vs2": _sb(KC, BF),
-    "land0": _sb(8 * 192, BF), "land1": _sb(8 * 192, BF), "land2": _sb(8 * KC, BF),
-    "i1": _sb(8, I32), "i2": _sb(8, I32), "rt": _sb(8, F32), "cs": _sb(16, F32), "j8": _sb(8, F32), "hc": _sb(8, F32),
+    "land0": _sb(5 * 192, BF), "land1": _sb(5 * 192, BF), "land2": _sb(8 * KC, BF),
+    "i1": _sb(8, I32), "i2": _sb(8, I32), "rt": _sb(8, F32), "cs": _sb(16, F32), "ct": _sb(16, F32), "j8": _sb(8, F32), "hc": _sb(8, F32),
     "lo": _sb(256, BF), "zz": _sb(6 * ZW, BF), "z8": _sb(ZW, BF), "idn": _sb(4 * 128 + ZW, BF),
     "ps": ("psum", [128, 4096], F32),
 }
 QUEUES = ["v", "s", "t", "g"]
-NDMA = 24
-SEMAPHORES = ["c_" + q for q in QUEUES] + ["d%d" % i for i in range(NDMA)] + ["arr0", "arr1", "arr2", "sent"]
+NDMA = 28
+SEMAPHORES = ["c_" + q for q in QUEUES] + ["d%d" % i for i in range(NDMA)] + ["arr0", "arr1", "arr2", "sib0", "sib1", "sent"]
 
-SPLIT = {"a0": (48, 48), "a": (46, 44), "b": (46, 48), "c": (40, 46), "d": (42, 44), "e": (40, 32), "f": (44, 44), "g": (42, 50)}
-MATCH = ("M.0 M.1 M.2 d.1 n.0 M.6 M.8 sg.1 M.7 d.2 sg.2 ab.1 d.6 M.3 ab.2 d.8 n.7 sg.6 ab.6 Z sg.8 n.3 ab.8 M.4 M.5 G.4 C.4 n.4 G.5 C.5 "
-         "n.5 G.6 M1.0 C.6 G.7 G.0 C.7 C.0 G.1 C.1 G.2 M1.1 G.3 B.0 C.2 C.3 B.1 K.0 n1.0 n1.1 M1.2 n1.2 V.0 U.0 K.1 U.1 K.2 V.1 U.2 "
-         "M1.3 mk.0 ck.0 K.3 n1.3 AD.0 U.3 mk.1 ck.1 V.2 AD.1").split()
+SPLIT = {"b": (46, 48), "c": (44, 44), "d": (44, 50), "f": (44, 46), "g": (42, 50)}
+MATCH = ("Xv.3 X.0 H.0 Xv.2 X.1 UP M.0 X.4 H.1 X.5 M.1 n.0 H.2 M.2 d.1 M.3 d.2 M.6 M.4 sg.1 sg.2 n.3 n.4 L.0 ab.1 M.7 ab.2 d.6 sg.6 ab.6 "
+         "M.5 n.7 Z G.0 C.0 G.1 M.8 C.1 G.4 G.5 C.4 n.5 C.5 L.1 n.8 G.2 G.3 G.6 C.2 M1.0 C.3 G.7 C.6 C.7 M1.1 K.0 B.1 n1.0 K.1 B.0 n1.1 "
+         "V.0 K.2 M1.2 U.0 U.1 n1.2 V.1 M1.3 U.2 mk.0 ck.0 AD.0 K.3 U.3 n1.3 mk.1 ck.1 V.2 AD.1").split()
 
 
 def rank_program(g, core, T, topo):
@@ -113,8 +113,8 @@ def rank_program(g, core, T, topo):
         if bias is not None:
             kw["bias"] = ap(bias)
         if scale is not None:
-            kw["scale"] = ap(scale)
-        return op("s", lambda: g.scalar.activation(ap(out), ap(a), f, **kw), [a] + [x for x in (bias, scale) if x], [out])
+            kw["scale"] = ap(scale) if isinstance(scale, tuple) else scale
+        return op("s", lambda: g.scalar.activation(ap(out), ap(a), f, **kw), [a] + [x for x in (bias, scale) if isinstance(x, tuple)], [out])
 
     def gather(q, out, win, off, other=None):
         src = lambda: ap(win).indirect(ap(off))
@@ -177,21 +177,17 @@ def rank_program(g, core, T, topo):
     red(col("cs", 0), R("rt", 0, 5, 2))
     ts(col("cs", 2), col("rt", 0), 12.0, None, A.mult)
     red(col("cs", 1), R("rt", 1, 4, 2))
-    ts(col("cs", 3), col("rt", 4), 8.0, None, A.mult)
     ts(R("hc", 0, 8), R("j8", 0, 8), col("cs", 0), col("cs", 2), A.mult, A.add)
-    ts(col("cs", 4), col("rt", 4), 14.0, None, A.mult)
-    ts(col("cs", 5), col("rt", 2), 14.0, col("cs", 3), A.mult, A.add)
-    ts(col("cs", 6), col("rt", 2), 8.0, col("cs", 4), A.mult, A.add)
-    ts(col("cs", 7), col("rt", 0), -12.0, col("cs", 5), A.mult, A.add)
-    ts(col("cs", 8), col("rt", 0), -6.0, col("cs", 6), A.mult, A.add)
+    for o, r, m, b in ((3, 4, 8.0, None), (4, 4, 14.0, None), (5, 2, 14.0, 3), (6, 2, 8.0, 4), (7, 0, -12.0, 5), (8, 0, -6.0, 6)):
+        act(col("ct", o), col("rt", r), AF.Identity, None if b is None else col("ct", b), m)
     for j in range(8):
         o = R("wb", NS + 256 * j, NS + 256 * j + 256)
         if j >= 3:
             ts(o, R("lo", 0, 256), col("cs", 1), col("hc", j), A.mult, A.add)
         else:
             act(o, R("lo", 0, 256), AF.Identity, col("hc", j), col("cs", 1))
-    act(R("tab", NF + NP, NF + NS), R("wb", NS, NS + NP), AF.Identity, col("cs", 8))
-    act(R("tab", NF, NF + NP), R("wb", NS, NS + NP), AF.Identity, col("cs", 7))
+    act(R("tab", NF + NP, NF + NS), R("wb", NS, NS + NP), AF.Identity, col("ct", 8))
+    act(R("tab", NF, NF + NP), R("wb", NS, NS + NP), AF.Identity, col("ct", 7))
 
     ts(W("mu"), W("pari"), 1024.0, 1535.0, A.is_ge, A.mult)
     ts(W("ta"), W("pari"), 2.0, None, A.mult)
@@ -221,17 +217,19 @@ def rank_program(g, core, T, topo):
     asel(ID(3), ID(0), [[0, 8], [-1, 16]], A.is_ge, 0.0, 1, 0)
     asel(R("z8", 0, ZW, 1, 8), R("idn", 512, 512 + ZW, 1, 8), [[1, ZW]], A.not_equal, 1.0, -15, -16)
 
-    def late():
-        ts(W("uk"), W("kdi"), -float(NF), None, A.add)
-        ts(W("tgt"), W("tg0"), col("cs", 9), None, A.add)
+    def late(c):
+        if c == 0:
+            ts(R("gen1", 0, KC), R("geni", 0, KC), 1, None, A.bitwise_and)
+            ts(W("uk"), W("kdi"), -float(NF), None, A.add)
+            cp(R("genf", 0, KC), R("gen1", 0, KC))
+        else:
+            act(R("genb", 0, KC), R("genf", 0, KC), AF.Copy)
+            act(W("tgt"), W("tg0"), AF.Identity, col("cs", 9))
+            dma("y", T.g8[0:8, :], T.genb[:], [R("genb", 0, KC)], [R("g8", 0, NP)])
 
-    def stage(win, off, dst, lo, split, zs, take, before, mid=None, after=None):
+    def stage(win, off, dst, lo, split, zs, take, before, mid=None):
         a, b = split
-
-        def part(q, c0, c1):
-            gather(q, R(dst, lo + 16 * c0, lo + 16 * c1), win, R(off, c0, c1))
-            if after:
-                after(16 * c0, 16 * c1)
+        part = lambda q, c0, c1: gather(q, R(dst, lo + 16 * c0, lo + 16 * c1), win, R(off, c0, c1))
         part("v", 0, a)
         part("s", a, KC)
         if zs is not None:
@@ -257,24 +255,38 @@ def rank_program(g, core, T, topo):
 
     near = [c for c in T.cores if c != core and c in topo.cores_of(core)]
     far = [c for c in T.cores if c not in topo.cores_of(core)]
+    line = [c for c in T.cores if topo.die(c) == topo.die(core)]
+    me = line.index(core)
     far_mask = topo.mask(core, far[0])
     near_mask = topo.mask(core, near[0]) & ~far_mask
-    n_eng = len(topo.engines(core, far[0]))
+    n_eng, n_all = len(topo.engines(core, far[0])), len(topo.engines(core, near[0]))
     sent = [0]
+    ids = lambda cs: [DstId(rid=topo.addr(c, core)[0], pnc=topo.addr(c, core)[1]) for c in cs]
+    slot = lambda t, n: R("land%d" % t, 192 * n, 192 * n + 192)
 
-    def exchange(n, w):
-        vs, land = R("vs%d" % n, 0, w), T["land%d" % n][:, w * rank:w * rank + w]
+    def send_base():
+        vs, land = H[0]("vs2"), T.land2[:, KC * rank:KC * rank + KC]
         for (lo, hi, tok, eq, ew) in recs[vs[0]]:
             need("g", tok)
-        tr = []
-        for cs, m in ((far, far_mask), (near, near_mask)):
-            ids = [DstId(rid=topo.addr(c, core)[0], pnc=topo.addr(c, core)[1]) for c in cs]
-            tr.append(RemoteDMATransfer(dst_ids=ids, dma_engine_mask=m, remote_sem=T.sem["arr%d" % n], srcs=[ap(vs)], dsts=[land] * len(cs)))
-        g.remote_dma_fused(tr, local_sem=T.sem.sent)
+        g.remote_dma_fused([RemoteDMATransfer(dst_ids=ids(cs), dma_engine_mask=m, remote_sem=T.sem.arr2, srcs=[ap(vs)], dsts=[land] * len(cs))
+                            for cs, m in ((far, far_mask), (near, near_mask))], local_sem=T.sem.sent)
         sent[0] += 2 * n_eng
 
+    def exchange(t):
+        vs = W("vs%d" % t)
+        for (lo, hi, tok, eq, ew) in recs[vs[0]]:
+            need("g", tok)
+        cs = [c for c in line if c != core]
+        g.remote_dma_fused([RemoteDMATransfer(dst_ids=ids(cs), dma_engine_mask=far_mask, remote_sem=T.sem["arr%d" % t], srcs=[ap(vs)],
+                                              dsts=[ap(slot(t, me))] * len(cs))], local_sem=T.sem.sent)
+        need("g", ("arr%d" % t, n_eng * len(cs), {}))
+        g.remote_dma_fused([RemoteDMATransfer(dst_ids=ids(near), dma_engine_mask=topo.mask(core, near[0]), remote_sem=T.sem["sib%d" % t],
+                                              srcs=[ap(vs)] + [ap(slot(t, n)) for n in range(len(line)) if n != me],
+                                              dsts=[ap(slot(t, len(line)))], alu_op=1)], local_sem=T.sem.sent)
+        sent[0] += n_eng + n_all
+
     def match(t):
-        XW, bank = R("xb", NS, 8192), {}
+        XW, bank, ring = R("xb", NS, 8192), {}, {}
         last = [x for x in MATCH if x[0] in "BV" or x == "AD.0"][-1]
 
         def mx(dst, off, lo, n):
@@ -285,7 +297,18 @@ def rank_program(g, core, T, topo):
             c = int(c)
             ch = lambda n, w=512: R(n, w * c, w * c + w)
             y = 512 * (c % 3)
-            if k == "M":
+            if k in ("X", "Xv"):
+                o = R("xb", PB + 512 * c, PB + 512 * c + 512)
+                gather("s" if k == "X" else "v", o, R("xb", 0, NS + NF), ch("u4", 32))
+                dma("y", ap(ch("xc")), ap(o), [o], [ch("xc")])
+            elif k == "H":
+                mm([(PS(5 + c, 0, 512), ID(0), R("xb", PB + y, PB + y + 512))])
+            elif k == "UP":
+                cp(R("up", 0, 384), PS(7, 0, 384))
+            elif k == "L":
+                if t == 0:
+                    late(c)
+            elif k == "M":
                 if c < 3:
                     tt(ch("mx"), PS(5 + c, 0, 512), R("xb", PB + NP + y, PB + NP + y + 512), A.max)
                 else:
@@ -306,18 +329,18 @@ def rank_program(g, core, T, topo):
                 tt(ch("ne1", 768), PS(0, y, y + 768), ch("m1", 768), A.not_equal)
             elif k == "G":
                 lo, b = 768 * (c // 2), c % 2
-                o = PS(5 + b, 0, 384)
+                o = ring[c] = PS((5, 6, 3, 4)[len(ring) % 4], 0, 384)
                 mm([(o, ID(3), R("wb", PB + lo + b, PB + lo + 768, 2)), (o, Z(ZSP, 2), R("ne", lo % NP + b, lo % NP + 768, 2)),
                     (o, Z(ZSM, 2), R("ne", NP + lo + b, NP + lo + 768, 2))])
             elif k == "C":
                 e, h, b = c // 4, c // 2 % 2, c % 2
                 lo = 2 * (768 * b + 384 * h) + e
-                act(R("gw", lo, lo + 767, 2), PS(5 + b, 0, 384), AF.Copy)
+                act(R("gw", lo, lo + 767, 2), ring[c], AF.Copy)
             elif k == "Z":
                 if t == 0:
                     mm(wrap(PS(7, 0, KC), ZSP, "ne", 0, KC))
                     act(H[0]("vs2"), PS(7, 0, KC), AF.Copy)
-                    exchange(2, KC)
+                    send_base()
                 mm([(PS(7, 0, 192), ID(4), W("yp"))], True, False)
             elif k == "B":
                 if t:
@@ -351,8 +374,10 @@ def rank_program(g, core, T, topo):
         if t == 0:
             need("t", ("arr2", n_eng * len(others), {}))
             mm([(P(3, e), ID(0), x) for e in range(2) for x in [H[0]("vs2")] + [R("land2", KC * r, KC * r + KC) for r in others]], False, False)
-        need("t", ("arr%d" % t, n_eng * len(others), {}))
-        mm([(PS(3, 0, 192), ID(0), R("land%d" % t, 192 * r, 192 * r + 192)) for r in others], False, True)
+        need("t", ("arr%d" % t, n_eng * (len(line) - 1), {}))
+        mm([(PS(3, 0, 192), ID(0), slot(t, n)) for n in range(len(line)) if n != me], False, False)
+        need("t", ("sib%d" % t, n_all, {}))
+        mm([(PS(3, 0, 192), ID(0), slot(t, len(line)))], False, True)
         qn = "q%d" % (t + 1)
         for e in range(2):
             tt(H[e]("thr"), P(3, 1 - e), R("big", 192 * t + KC * e, 192 * t + KC * e + KC), A.max)
@@ -366,13 +391,10 @@ def rank_program(g, core, T, topo):
             cp(H[e]("uq"), H[e](qn))
 
     for t in range(3):
-        mid = None
-        if t == 2:
-            def mid():
-                tt(W("yso"), W("q2"), W("qhi"), A.is_equal)
-                for e in range(2):
-                    dma("y", T.ys[e::2, :], ap(H[e]("yso")), [H[e]("yso")], [])
-        stage(R("tab", 0, 5120), "uq", "wb", PB, SPLIT["a" if t else "a0"], None, None, None, mid)
+        for e, q in enumerate("sv"):
+            gather(q, R("wb", PB + NP * e, PB + NP * e + NP), R("tab", 0, 5120), H[e]("uq"))
+        if t < 2:
+            mm(wrap(PS(7, 0, 192), ZP, "wb", PB, 192))
         rest = stage(WA, "uq", "wb", 0, SPLIT["b"], ZA1, to("u2"), None)
         if t == 2:
             rest = stage(WA1, "u2", "wb", PB, SPLIT["f"], ZA, to("u4"), rest)
@@ -380,36 +402,25 @@ def rank_program(g, core, T, topo):
             def put(h):
                 cp(H[h]("yao"), PS(3 + h, 0, KC))
                 dma("y", T.ya[h::2, :], ap(H[h]("yao")), [H[h]("yao")], [])
+                if h == 0:
+                    tt(W("yso"), W("q2"), W("qhi"), A.is_equal)
+                    for e in range(2):
+                        dma("s", T.ys[e::2, :], ap(H[e]("yso")), [H[e]("yso")], [])
             stage(WA, "u4", "w4", 0, SPLIT["g"], ZA, put, rest)()
             break
         rest = stage(WA1, "u2", "w4", 0, SPLIT["c"], ZA1, take4, rest)
 
         def partners():
-            mm(wrap(PS(3, 0, 192), ZP, "wb", PB, 192))
-            mm(wrap(PS(3, 192, 384), ZP, "wb", 0, 192))
+            mm(wrap(PS(7, 192, 384), ZP, "wb", 0, 192))
             if t == 0:
                 for b in range(3):
                     mm([(PS(b, 0, 512), ID(0), R("yp", 512 * b, 512 * b + 512))])
-                late()
         stage(R("xb", NS, NS + NF), "u4c", "xb", 0, SPLIT["d"], None, None, rest, partners)
-
-        def hold():
-            for b in range(3):
-                mm([(PS(5 + b, 0, 512), ID(0), R("xb", PB + 512 * b, PB + 512 * b + 512))])
-            cp(R("up", 0, 384), PS(3, 0, 384))
-
-        def twin(lo, hi):
-            dma("y", ap(R("xc", lo, hi)), ap(R("xb", PB + lo, PB + hi)), [R("xb", PB + lo, PB + hi)], [R("xc", lo, hi)])
-        stage(R("xb", 0, NS + NF), "u4", "xb", PB, SPLIT["e"], None, None, None, hold, twin)
         match(t)
-        exchange(t, 192)
+        exchange(t)
         if t == 0:
-            ts(R("gen1", 0, KC), R("geni", 0, KC), 1, None, A.bitwise_and)
             tt(W("qhi"), W("td"), W("mu"), A.add)
-            cp(R("genf", 0, KC), R("gen1", 0, KC))
             tt(W("qsum"), W("td"), W("qhi"), A.add)
-            cp(R("genb", 0, KC), R("genf", 0, KC))
-            dma("y", T.g8[0:8, :], T.genb[:], [R("genb", 0, KC)], [R("g8", 0, NP)])
             mm([(PS(4, 0, KC), R("z8", 15 - i, 143 - i, 1, 8), R("g8", 768 * (i % 2) + i // 2, 768 * (i % 2) + 768, 8, 8)) for i in range(16)])
         ts(W("tc"), W("q%d" % t), -2.0, None, A.mult)
         tt(W("dl"), W("qsum"), W("tc"), A.add)

@@ -1,10 +1,13 @@
 from concourse.bass import DstId, RemoteDMATransfer
-from concourse.mybir import AluOpType as A, AxisListType, ActivationFunctionType as AF
+from concourse.mybir import AluOpType as A, ActivationFunctionType as AF
 
-NF, NP, NS, KC = 2048, 1536, 3072, 96
+NF, NP, NS, NW, NC = 2048, 1536, 3072, 5120, 192
 BF, F32, I32, U16 = "bfloat16", "float32", "int32", "uint16"
 ZW = 144
-ZA1, ZP, ZA, ZG, ZSP, ZSM = range(6)
+ZA, ZC, ZSP, ZSM, ZU, ZB = range(6)
+I1, IH, IMH, I01, I2, IM, IK, IKK, ID64, IODD, ISW, I0 = range(12)
+TAB, W1 = 0, NW
+FS, XS, FA, X1 = 0, NF, NW, NW + NF
 
 
 def _sb(n, d):
@@ -12,30 +15,31 @@ def _sb(n, d):
 
 
 SCRATCH = {
-    "tab": _sb(5120, BF), "wb": _sb(8192, BF), "w4": _sb(NS, BF), "xb": _sb(8192, BF), "xc": _sb(NS, BF),
-    "phs": _sb(NP, BF), "yp": _sb(NP, BF), "mx": _sb(NP + NS, BF), "m1": _sb(NS, BF),
-    "sg": _sb(NP + NS, BF), "ne": _sb(NP + NS, BF), "ne1": _sb(NS, BF), "gw": _sb(NS, BF), "go": _sb(NS, BF),
-    "pari": _sb(192, I32), "swi": _sb(192, I32), "kdi": _sb(192, I32), "geni": _sb(KC, I32), "gen1": _sb(KC, I32),
-    "genf": _sb(KC, F32), "genb": _sb(KC, BF), "g8": _sb(NP, BF),
-    "ta": _sb(192, F32), "tb": _sb(192, F32), "tc": _sb(192, F32), "mu": _sb(192, F32), "td": _sb(192, F32), "te": _sb(192, F32),
-    "q0": _sb(192, F32), "q1": _sb(192, F32), "q2": _sb(192, F32), "dl": _sb(192, F32), "qhi": _sb(192, F32), "qsum": _sb(192, F32),
-    "big": _sb(384, F32), "thr": _sb(192, F32), "yso": _sb(192, F32), "yao": _sb(192, F32),
-    "uq": _sb(192, U16), "u2": _sb(192, U16), "u4": _sb(192, U16), "u4c": _sb(192, U16), "up": _sb(384, U16), "uk": _sb(192, U16),
-    "tg0": _sb(192, F32), "tgt": _sb(192, F32), "mk": _sb(384, F32), "ck": _sb(384, BF),
-    "vs0": _sb(192, BF), "vs1": _sb(192, BF), "vs2": _sb(KC, BF),
-    "land0": _sb(5 * 192, BF), "land1": _sb(5 * 192, BF), "land2": _sb(8 * KC, BF),
-    "i1": _sb(8, I32), "i2": _sb(8, I32), "rt": _sb(8, F32), "cs": _sb(16, F32), "ct": _sb(16, F32), "j8": _sb(8, F32), "hc": _sb(8, F32),
-    "lo": _sb(256, BF), "zz": _sb(6 * ZW, BF), "z8": _sb(ZW, BF), "idn": _sb(4 * 128 + ZW, BF),
+    "wb": _sb(2 * NW, BF), "tb": _sb(1024, BF), "w4": _sb(NS, BF), "xb": _sb(2 * NW, BF), "xc": _sb(NS, BF), "phs": _sb(NP, BF),
+    "mb": _sb(NP, BF), "m2": _sb(NS, BF), "m1": _sb(NS, BF), "nb": _sb(NP, BF), "n2": _sb(NS, BF), "n1": _sb(NS, BF),
+    "sb": _sb(NP, BF), "s1": _sb(NS, BF), "s2": _sb(NS, BF), "gw": _sb(NS, BF), "go": _sb(NS, BF), "ck": _sb(4 * NC, BF),
+    "pari": _sb(NC, I32), "swi": _sb(NC, I32), "kdi": _sb(NC, I32), "geni": _sb(96, I32), "gen1": _sb(96, I32), "genb": _sb(96, BF),
+    "g8": _sb(NP, BF), "par2": _sb(NC, F32), "q0": _sb(NC, F32), "q1": _sb(NC, F32), "q2": _sb(NC, F32), "b1": _sb(NC, F32), "b2": _sb(NC, F32),
+    "big": _sb(NC, F32), "thr": _sb(NC, F32), "tg0": _sb(NC, F32), "tg": _sb(NC, F32), "rd": _sb(NC, F32), "stay": _sb(NC, F32), "yao": _sb(NC, F32),
+    "uq": _sb(NC, U16), "u2": _sb(NC, U16), "u4": _sb(NC, U16), "u4c": _sb(NC, U16), "uk": _sb(NC, U16), "ur": _sb(NC, U16),
+    "vs0": _sb(NC, BF), "vs1": _sb(NC, BF), "vs2": _sb(NC, BF),
+    "land0": _sb(5 * NC, BF), "land1": _sb(5 * NC, BF), "land2": _sb(8 * NC, BF),
+    "i1": _sb(4, I32), "i2": _sb(4, I32), "rt": _sb(4, F32), "cs": _sb(4, F32), "hc": _sb(12, F32),
+    "one": _sb(256, BF), "lo": _sb(256, BF), "lx": _sb(256, BF), "zz": _sb(6 * ZW, BF), "z8": _sb(ZW, BF), "idn": _sb(11 * 128 + ZW, BF),
     "ps": ("psum", [128, 4096], F32),
 }
 QUEUES = ["v", "s", "t", "g"]
-NDMA = 28
+NDMA = 24
 SEMAPHORES = ["c_" + q for q in QUEUES] + ["d%d" % i for i in range(NDMA)] + ["arr0", "arr1", "arr2", "sib0", "sib1", "sent"]
 
-SPLIT = {"b": (46, 48), "c": (44, 44), "d": (44, 50), "f": (44, 46), "g": (42, 50)}
-MATCH = ("Xv.3 X.0 H.0 Xv.2 X.1 UP M.0 X.4 H.1 X.5 M.1 n.0 H.2 M.2 d.1 M.3 d.2 M.6 M.4 sg.1 sg.2 n.3 n.4 L.0 ab.1 M.7 ab.2 d.6 sg.6 ab.6 "
-         "M.5 n.7 Z G.0 C.0 G.1 M.8 C.1 G.4 G.5 C.4 n.5 C.5 L.1 n.8 G.2 G.3 G.6 C.2 M1.0 C.3 G.7 C.6 C.7 M1.1 K.0 B.1 n1.0 K.1 B.0 n1.1 "
-         "V.0 K.2 M1.2 U.0 U.1 n1.2 V.1 M1.3 U.2 mk.0 ck.0 AD.0 K.3 U.3 n1.3 mk.1 ck.1 V.2 AD.1").split()
+CUTS = (0, 64, 128, 192)
+FIRST = (96, 96, 96)
+SHARE = {"p2": 32, "p4": 30, "x1": 30, "n1": 30, "n2": 30, "n4": 32, "r": 90}
+LEAD = 1
+SBLK, GSELF = 3, 1536
+MATCH = ("L.0 L.1 X.1 X.3 X.5 Xv.0 X.4 T.0 Xv.2 T.1 H.0 H.1 M.0 M.1 T.2 d.b11 sg.b11 n.b01 ab.b11 A2.0 H.2 A2.1 d.201 T.3 T.4 sg.201 ab.201 A2.2 M.2 "
+         "T.5 d.211 A2.3 d.221 n.b21 n.231 sg.211 sg.221 A2.4 G.0 Z ab.211 ab.221 A2.5 G.3 n.241 n.251 Y C.31 G.1 C.02 A1.0 A1.3 G.2 G.4 C.21 C.41 "
+         "A1.1 A1.5 G.5 A1.2 C.51 K.0 K.1 U0.1 U0.0 U.0 U.1 A1.4 n.122 n.102 V.1 K.2 n.142 cl.0 U.2 V.0 K.3 U.3 V.2 cl.1 AD.0 AD.1 E").split()
 
 
 def rank_program(g, core, T, topo):
@@ -66,8 +70,8 @@ def rank_program(g, core, T, topo):
         deps = {}
         for rs, w in ((reads, False), (writes, True)):
             for r in rs:
-                for (lo, hi, tok, eq, ew) in recs.get(r[0], []):
-                    hit = lo < r[2] and r[1] < hi and (w or ew)
+                for (lo, hi, tok, eq, ew, st) in recs.get(r[0], []):
+                    hit = lo < r[2] and r[1] < hi and (w or ew) and not (st == r[3] and (lo - r[1]) % st)
                     if r[0] == "ps":
                         if eq != q:
                             hit = lo // 512 <= (r[2] - 1) // 512 and r[1] // 512 <= (hi - 1) // 512
@@ -92,7 +96,10 @@ def rank_program(g, core, T, topo):
                 l = recs.setdefault(r[0], [])
                 if w and r[3] == 1 and r[0] != "ps":
                     l[:] = [x for x in l if not (r[1] <= x[0] and x[1] <= r[2])]
-                l.append((r[1], r[2], tok, "dma" if dma else q, w))
+                elif r[0] == "ps":
+                    l[:] = [x for x in l if not (x[3] == q and r[1] // 512 <= x[0] // 512 and (x[1] - 1) // 512 <= (r[2] - 1) // 512
+                                                 and (q == "t" or known[q].get(x[2][0], 0) >= x[2][1]))]
+                l.append((r[1], r[2], tok, "dma" if dma else q, w, r[3]))
         return tok
 
     def ts(out, in0, s1, s2, o0, o1=None):
@@ -138,11 +145,14 @@ def rank_program(g, core, T, topo):
     def asel(out, a, pat, cmp, fill, base, cm):
         return op("g", lambda: g.affine_select(ap(out), ap(a), pat, cmp, fill, base, cm), [a], [out])
 
+    def gcopy(out, a):
+        return asel(out, a, [[0, len(range(a[1], a[2], a[3]))]], A.is_ge, 0.0, 0, 0)
+
     def dma(q, out, in_, reads, writes):
         return op(q, lambda: Q[q].dma_start(out, in_), reads, writes, dma=True)
 
-    def PS(b, lo, hi):
-        return R("ps", 512 * b + lo, 512 * b + hi)
+    def PS(b, lo, hi, step=1):
+        return R("ps", 512 * b + lo, 512 * b + hi, step)
 
     def Z(s, i):
         return R("zz", s * ZW + 15 - i, s * ZW + 143 - i)
@@ -153,105 +163,119 @@ def rank_program(g, core, T, topo):
     def col(name, k):
         return R(name, k, k + 1)
 
-    def wrap(out, s, src, lo, n):
-        return [(out, Z(s, i), R(src, lo + i, lo + 16 * n, 16)) for i in range(16)]
+    def wrap(out, s, src, lo, n, flip=0):
+        return [(out, Z(s, i ^ flip), R(src, lo + i, lo + 16 * n, 16)) for i in range(16)]
 
-    H = [lambda n, e=e: R(n, KC * e, KC * e + KC) for e in range(2)]
-    W = lambda n: R(n, 0, 192)
+    W = lambda n, lo=0, hi=NC: R(n, lo, hi)
+    H = lambda n, h: R(n, 96 * h, 96 * h + 96)
+    win = lambda base: R("wb", base, base + NW)
 
-    for e in range(2):
-        dma("y", ap(H[e]("pari")), T.par[e::2, :], [], [H[e]("pari")])
-        dma("s", ap(H[e]("swi")), T.sw[e::2, :], [], [H[e]("swi")])
-    dma("y", ap(R("xb", NS, NS + NF)), T.fa[:], [], [R("xb", NS, NS + NF)])
+    dma("y", T.pari[:], T.par[:], [], [W("pari")])
+    dma("s", T.swi[:], T.sw[:], [], [W("swi")])
+    dma("y", ap(R("xb", FA, FA + NF)), T.fa[:], [], [R("xb", FA, FA + NF)])
+    dma("y", T.geni[:], T.gen[:], [], [R("geni", 0, 96)])
     dma("y", T.phs[:], T.ph[:], [], [R("phs", 0, NP)])
     dma("y", T.kdi[:], T.kd[:], [], [W("kdi")])
-    dma("y", T.geni[:], T.gen[:], [], [R("geni", 0, KC)])
 
-    iota(R("i1", 0, 8), [[-1, 8]], 16, 1, False)
-    iota(R("j8", 0, 8), [[1, 8]], 0, 0)
-    iota(R("lo", 0, 256), [[1, 256]], 0, 0)
-    ts(R("i2", 0, 8), R("i1", 0, 8), 15, None, A.bitwise_and)
-    ts(R("rt", 0, 8), R("i2", 0, 8), 0.0, None, A.is_equal)
-    cp(col("cs", 9), col("i2", 0))
-    red = lambda o, a: op("v", lambda: g.vector.tensor_reduce(ap(o), ap(a), AxisListType.X, A.add), [a], [o])
-    red(col("cs", 0), R("rt", 0, 5, 2))
-    ts(col("cs", 2), col("rt", 0), 12.0, None, A.mult)
-    red(col("cs", 1), R("rt", 1, 4, 2))
-    ts(R("hc", 0, 8), R("j8", 0, 8), col("cs", 0), col("cs", 2), A.mult, A.add)
-    for o, r, m, b in ((3, 4, 8.0, None), (4, 4, 14.0, None), (5, 2, 14.0, 3), (6, 2, 8.0, 4), (7, 0, -12.0, 5), (8, 0, -6.0, 6)):
-        act(col("ct", o), col("rt", r), AF.Identity, None if b is None else col("ct", b), m)
-    for j in range(8):
-        o = R("wb", NS + 256 * j, NS + 256 * j + 256)
-        if j >= 3:
-            ts(o, R("lo", 0, 256), col("cs", 1), col("hc", j), A.mult, A.add)
-        else:
-            act(o, R("lo", 0, 256), AF.Identity, col("hc", j), col("cs", 1))
-    act(R("tab", NF + NP, NF + NS), R("wb", NS, NS + NP), AF.Identity, col("ct", 8))
-    act(R("tab", NF, NF + NP), R("wb", NS, NS + NP), AF.Identity, col("ct", 7))
+    iota(R("i1", 0, 4), [[-1, 4]], 16, 1, False)
+    op("v", lambda: g.vector.memset(T.one[:], 1.0), [], [R("one", 0, 256)])
+    ts(R("i2", 0, 3, 2), R("i1", 0, 3, 2), 15, None, A.bitwise_and)
+    ts(col("i2", 1), col("i1", 1), 14, None, A.bitwise_and)
+    op("v", lambda: g.vector.tensor_tensor_scan(T.lo[:], T.one[:], T.one[:], -1.0, A.add, A.mult), [R("one", 0, 256)], [R("lo", 0, 256)])
+    ts(R("rt", 0, 3), R("i2", 0, 3), 0.0, None, A.is_equal)
+    ts(R("hc", 0, 12), R("lo", 0, 12), col("rt", 0), None, A.mult)
+    ts(R("lx", 0, 256, 2), R("lo", 0, 256, 2), col("rt", 2), None, A.add)
+    ts(R("lx", 1, 256, 2), R("lo", 1, 256, 2), col("rt", 2), None, A.subtract)
+    tab = lambda lo, hi: R("wb", TAB + lo, TAB + hi)
+    block = lambda o, src, j: ts(o, R(src, 0, 256), col("rt", 1), col("hc", j), A.mult, A.add)
+    persons = lambda n: act(tab(NF + 1024 * n, NF + 1024 * n + 1024), R("tb", 0, 1024), AF.Identity, col("hc", 4 * n))
+    for j in range(8 - SBLK, 8):
+        act(tab(256 * j, 256 * j + 256), R("lo", 0, 256), AF.Identity, col("hc", j), col("rt", 1))
+    block(tab(0, 256), "lo", 0)
+    for j in range(4):
+        block(R("tb", 256 * j, 256 * j + 256), "lx", 8 + j)
+    persons(2)
+    for j in range(1, 8 - SBLK):
+        block(tab(256 * j, 256 * j + 256), "lo", j)
 
-    ts(W("mu"), W("pari"), 1024.0, 1535.0, A.is_ge, A.mult)
-    ts(W("ta"), W("pari"), 2.0, None, A.mult)
-    ts(W("tb"), W("pari"), 1792.0, -1535.0, A.is_ge, A.mult)
-    ts(W("mu"), W("mu"), 1.0, None, A.add)
-    tt(W("td"), W("ta"), W("tb"), A.add)
-    tt(W("te"), W("mu"), W("swi"), A.mult)
-    ts(R("tab", 0, NF, 2), R("wb", NS, NS + NF, 2), col("rt", 3), None, A.add)
-    tt(W("q0"), W("td"), W("te"), A.add)
-    ts(R("tab", 1, NF, 2), R("wb", NS + 1, NS + NF, 2), col("rt", 3), None, A.subtract)
-    cp(W("uq"), W("q0"))
+    def pieces(t):
+        return ((0, FIRST[t]), (FIRST[t], NC))
+    founders = lambda lo, hi: (R("wb", W1 + lo, W1 + hi), tab(lo, hi))
+    for lo, hi in pieces(0):
+        ts(PS(3, lo, hi), W("pari", lo, hi), 2.0, None, A.mult)
+    cp(tab(NF, NF + 1024), R("tb", 0, 1024))
+    for lo, hi in pieces(0):
+        tt(W("q0", lo, hi), PS(3, lo, hi), W("swi", lo, hi), A.add)
+    ts(tab(NF + 1024, NF + 2048), R("tb", 0, 1024), col("hc", 4), None, A.add)
+    act(*founders(0, NF - GSELF), AF.Copy)
+    for lo, hi in pieces(0):
+        cp(W("uq", lo, hi), W("q0", lo, hi))
 
+    zc = lambda s, c=15: R("zz", s * ZW + c, s * ZW + c + 128, 16)
     iota(R("zz", 0, 6 * ZW), [[0, 6 * ZW]], 0, 0)
-    iota(R("idn", 512, 512 + ZW), [[0, ZW]], 0, 0)
-    iota(W("tg0"), [[NP, 2], [16, KC]], 0, 0)
-    zc = lambda s: R("zz", s * ZW + 15, s * ZW + 143, 16)
+    iota(R("idn", 128 * I0, 128 * I0 + ZW), [[0, ZW]], 0, 0)
+    ident = lambda k, v: asel(ID(k), ID(I0), [[-1, 128]], A.not_equal, v, 0, 1)
+    diag = lambda k: asel(ID(k), ID(k), [[-1, 128]], A.is_equal, 0.0, 0, 1)
     for n in range(2):
-        for s, rows in ((ZA1, (0, 1)), (ZP, (2, 3)), (ZA, (4, 1))):
+        for s, rows in ((ZA, (0, 1)), (ZC, (0, 2))):
             asel(zc(s), zc(s), [[-16, 8]], A.not_equal, (256.0, 1.0)[n], -rows[n], 1)
+    if GSELF:
+        gcopy(*founders(NF - GSELF, NF))
+    for k, v in ((I1, 1.0), (IH, 0.5), (IMH, -0.5)):
+        ident(k, v)
+    for e in range(2):
+        gcopy(R("xb", FS + e, FS + NF, 2), R("xb", FA + 1 - e, FA + NF, 2))
+    for n in range(2):
         for s, v in ((ZSP, 1.0), (ZSM, -1.0)):
             asel(zc(s), zc(s), [[16, 8]], A.is_gt, (v, 0.0)[n], 16 * n, -1)
-    asel(zc(ZG), zc(ZG), [[-16, 8]], A.not_equal, 1.0, -2, 1)
-    for k, v in enumerate((1.0, 0.5, -0.5)):
-        asel(ID(k), ID(4), [[-1, 128]], A.not_equal, v, 0, 1)
-    for b in range(2):
-        asel(R("yp", b, NP, 2), R("phs", 768 * b, 768 * b + 768), [[0, 768]], A.is_ge, 0.0, 0, 0)
-    asel(ID(3), ID(0), [[0, 8], [-1, 16]], A.is_ge, 0.0, 1, 0)
-    asel(R("z8", 0, ZW, 1, 8), R("idn", 512, 512 + ZW, 1, 8), [[1, ZW]], A.not_equal, 1.0, -15, -16)
+    asel(ID(I01), ID(I1), [[0, 8], [-1, 16]], A.is_ge, 0.0, 1, 0)
+    for c in (14, 15):
+        gcopy(zc(ZB, c), zc(ZSP))
 
     def late(c):
         if c == 0:
-            ts(R("gen1", 0, KC), R("geni", 0, KC), 1, None, A.bitwise_and)
-            ts(W("uk"), W("kdi"), -float(NF), None, A.add)
-            cp(R("genf", 0, KC), R("gen1", 0, KC))
-        else:
-            act(R("genb", 0, KC), R("genf", 0, KC), AF.Copy)
-            act(W("tgt"), W("tg0"), AF.Identity, col("cs", 9))
-            dma("y", T.g8[0:8, :], T.genb[:], [R("genb", 0, KC)], [R("g8", 0, NP)])
+            iota(ID(ID64), [[0, 8], [-64, 16]], 0, 0)
+            for r, (v, k, u) in enumerate(((16384.0, IK, -1024.0), (64.0, IKK, -64.0 * NF), (1.0, I2, 2.0))):
+                asel(zc(ZU), zc(ZU), [[-16, 8]], A.not_equal, v, -r, 1)
+                ident(k, u)
+            gcopy(zc(ZU, 14), zc(ZU))
+            diag(ID64)
+            ident(IM, -1.0)
+            return
+        iota(ID(IODD), [[0, 64], [1, 2]], 0, 0)
+        z8 = R("z8", 0, ZW, 1, 8)
+        asel(z8, R("idn", 128 * I0, 128 * I0 + ZW, 1, 8), [[1, ZW]], A.not_equal, 1.0, -15, -16)
+        diag(IODD)
+        asel(z8, z8, [[1, ZW]], A.not_equal, 1.0, -14, -16)
+        for e in range(2):
+            asel(R("idn", 128 * ISW + e, 128 * ISW + 128, 2), R("idn", 128 * I0, 128 * I0 + 64), [[-2, 64]], A.not_equal, 1.0, e - 1, 1)
+        iota(W("tg0"), [[16, NC]], NF, 0)
 
-    def stage(win, off, dst, lo, split, zs, take, before, mid=None):
-        a, b = split
-        part = lambda q, c0, c1: gather(q, R(dst, lo + 16 * c0, lo + 16 * c1), win, R(off, c0, c1))
-        part("v", 0, a)
-        part("s", a, KC)
-        if zs is not None:
-            mm(wrap(PS(3, 0, KC), zs, dst, lo, KC))
-        if before:
-            before()
-        if mid:
-            mid()
-        part("v", KC, KC + b)
-        part("s", KC + b, 192)
-        if zs is None:
-            return None
-        mm(wrap(PS(4, 0, KC), zs, dst, lo + NP, KC))
-        take(0)
-        return lambda: take(1)
+    def stages(todo):
+        wait, nb = [], 0
+        for k, (w, off, dst, lo, share, zs, flip, take, extra) in enumerate(todo):
+            for n in range(len(CUTS) - 1):
+                c0, c1 = CUTS[n], CUTS[n + 1]
+                while wait and wait[0][0] < k and wait[0][1] <= n + LEAD:
+                    wait.pop(0)[2]()
+                a = c0 + share * (c1 - c0) // 128 * 2
+                gather("v", R(dst, lo + 16 * c0, lo + 16 * a), w, R(off, c0, a))
+                gather("s", R(dst, lo + 16 * a, lo + 16 * c1), w, R(off, a, c1))
+                if extra and n in extra:
+                    extra[n]()
+                if zs is not None:
+                    o = PS(3 + nb % 3, 0, c1 - c0)
+                    nb += 1
+                    mm(wrap(o, zs, dst, lo + 16 * c0, c1 - c0, flip))
+                    wait.append((k, n, lambda o=o, c0=c0, c1=c1, take=take: take(o, c0, c1)))
+        for x in wait:
+            x[2]()
 
-    WA, WA1, PB = R("wb", NS, 8192), R("wb", 0, NS + NF), NS + NF
-    to = lambda name: (lambda h: cp(H[h](name), PS(3 + h, 0, KC)))
+    to = lambda name: (lambda o, c0, c1: cp(W(name, c0, c1), o))
 
-    def take4(h):
-        ts(H[h]("u4c"), PS(3 + h, 0, KC), -float(NS), 0.0, A.add, A.max)
-        cp(H[h]("u4"), PS(3 + h, 0, KC))
+    def take4(o, c0, c1):
+        ts(W("u4c", c0, c1), o, NF - 1.0, None, A.min)
+        cp(W("u4", c0, c1), o)
 
     near = [c for c in T.cores if c != core and c in topo.cores_of(core)]
     far = [c for c in T.cores if c not in topo.cores_of(core)]
@@ -262,20 +286,20 @@ def rank_program(g, core, T, topo):
     n_eng, n_all = len(topo.engines(core, far[0])), len(topo.engines(core, near[0]))
     sent = [0]
     ids = lambda cs: [DstId(rid=topo.addr(c, core)[0], pnc=topo.addr(c, core)[1]) for c in cs]
-    slot = lambda t, n: R("land%d" % t, 192 * n, 192 * n + 192)
+    slot = lambda t, n: R("land%d" % t, NC * n, NC * n + NC)
 
     def send_base():
-        vs, land = H[0]("vs2"), T.land2[:, KC * rank:KC * rank + KC]
-        for (lo, hi, tok, eq, ew) in recs[vs[0]]:
-            need("g", tok)
-        g.remote_dma_fused([RemoteDMATransfer(dst_ids=ids(cs), dma_engine_mask=m, remote_sem=T.sem.arr2, srcs=[ap(vs)], dsts=[land] * len(cs))
+        vs = W("vs2")
+        for x in recs[vs[0]]:
+            need("g", x[2])
+        g.remote_dma_fused([RemoteDMATransfer(dst_ids=ids(cs), dma_engine_mask=m, remote_sem=T.sem.arr2, srcs=[ap(vs)], dsts=[ap(slot(2, rank))] * len(cs))
                             for cs, m in ((far, far_mask), (near, near_mask))], local_sem=T.sem.sent)
         sent[0] += 2 * n_eng
 
     def exchange(t):
         vs = W("vs%d" % t)
-        for (lo, hi, tok, eq, ew) in recs[vs[0]]:
-            need("g", tok)
+        for x in recs[vs[0]]:
+            need("g", x[2])
         cs = [c for c in line if c != core]
         g.remote_dma_fused([RemoteDMATransfer(dst_ids=ids(cs), dma_engine_mask=far_mask, remote_sem=T.sem["arr%d" % t], srcs=[ap(vs)],
                                               dsts=[ap(slot(t, me))] * len(cs))], local_sem=T.sem.sent)
@@ -286,148 +310,176 @@ def rank_program(g, core, T, topo):
         sent[0] += n_eng + n_all
 
     def match(t):
-        XW, bank, ring = R("xb", NS, 8192), {}, {}
-        last = [x for x in MATCH if x[0] in "BV" or x == "AD.0"][-1]
+        held, free = {}, [3, 4, 5, 6]
+        last = [x for x in MATCH if x[0] == "V" or x[:2] == "AD"][-1]
+        copies = {int(x[-2]) + n: x[-2:] for x in MATCH if x[0] == "C" for n in range(int(x[-1]))}
 
-        def mx(dst, off, lo, n):
-            z = (lo + NP) % NS
-            gather("v", dst, XW, R("up", off + lo // 16, off + (lo + n) // 16), R("xc", z, z + n))
+        def take(key, n):
+            if key not in held:
+                held[key] = min((b for b in free if n == 1 or b + 1 in free), key=lambda b: max(free.index(b + i) for i in range(n)))
+                for i in range(n):
+                    free.remove(held[key] + i)
+            return held[key]
+
+        def drop(key, n):
+            free.extend(range(held[key], held[key] + n))
         for step in MATCH:
             k, c = (step.split(".") + ["0"])[:2]
+            if k in ("d", "sg", "ab", "nz", "n"):
+                kind, w, lo = c[0], int(c[2]), 512 * int(c[1])
+                st = 1 if kind == "b" else 2
+                blk = lambda n, e=0, st=1: R(n + kind, lo + e, lo + 512 * w, st)
+                if k == "n":
+                    for e in range(st):
+                        tt(blk("n", e, st), PS(0, lo // st, (lo + 512 * w) // st), blk("m", e, st), A.not_equal)
+                elif k == "d":
+                    for h in range(w):
+                        b, a = take(c, w) + h, lo + 512 * h
+                        mm([(PS(b, 0, 512), ID(IH), R("m" + kind, a, a + 512))]
+                           + [(PS(b, e, 512, st), ID(IMH), R("phs", a // st, (a + 512) // st)) for e in range(st)])
+                elif k == "sg":
+                    act(blk("s"), PS(held[c], 0, 512 * w), AF.Sign)
+                    drop(c, w)
+                elif k == "ab":
+                    act(blk("n"), blk("s"), AF.Abs)
+                else:
+                    ts(blk("n"), blk("s"), 0.0, None, A.not_equal)
+                continue
+            if k in ("C", "Cv"):
+                o, a = R("gw", 512 * int(c[0]), 512 * (int(c[0]) + int(c[1]))), PS(held["C" + c], 0, 512 * int(c[1]))
+                act(o, a, AF.Copy) if k == "C" else cp(o, a)
+                drop("C" + c, int(c[1]))
+                continue
             c = int(c)
-            ch = lambda n, w=512: R(n, w * c, w * c + w)
-            y = 512 * (c % 3)
+            ch = lambda n, lo=0, w=512: R(n, lo + w * c, lo + w * c + w)
+            e = c % 2
             if k in ("X", "Xv"):
-                o = R("xb", PB + 512 * c, PB + 512 * c + 512)
-                gather("s" if k == "X" else "v", o, R("xb", 0, NS + NF), ch("u4", 32))
-                dma("y", ap(ch("xc")), ap(o), [o], [ch("xc")])
-            elif k == "H":
-                mm([(PS(5 + c, 0, 512), ID(0), R("xb", PB + y, PB + y + 512))])
-            elif k == "UP":
-                cp(R("up", 0, 384), PS(7, 0, 384))
+                gather("s" if k == "X" else "v", ch("xb", XS), R("xb", FA, FA + NW), ch("u4", 0, 32))
+            elif k == "T":
+                dma("y", ap(ch("xc")), ap(ch("xb", XS)), [ch("xb", XS)], [ch("xc")])
+            elif k == "Tg":
+                gcopy(ch("xc"), ch("xb", XS))
+            elif k == "Ts":
+                gather("s", ch("xc"), R("xb", FA, FA + NW), ch("u4", 0, 32))
             elif k == "L":
                 if t == 0:
                     late(c)
+            elif k == "H":
+                mm([(PS(7 if c == 2 else take(step, 1), 0, 512), ID(I1), R("xb", XS + 1024 * c, XS + 1024 * c + 1024, 2))])
             elif k == "M":
-                if c < 3:
-                    tt(ch("mx"), PS(5 + c, 0, 512), R("xb", PB + NP + y, PB + NP + y + 512), A.max)
-                else:
-                    mx(ch("mx"), 192, 512 * (c - 3), 512)
-            elif k == "M1":
-                mx(ch("m1", 768), 0, 768 * c, 768)
-            elif k == "d":
-                bank[c] = PS(3 + len(bank) % 2, 0, 512)
-                mm([(bank[c], ID(1), ch("mx")), (bank[c], ID(2), R("yp", y, y + 512))])
-            elif k == "sg":
-                act(ch("sg"), bank[c], AF.Sign)
-            elif k == "ab":
-                act(ch("ne"), ch("sg"), AF.Abs)
-            elif k == "n":
-                tt(ch("ne"), PS(0, y, y + 512), ch("mx"), A.not_equal)
-            elif k == "n1":
-                y = 768 * (c % 2)
-                tt(ch("ne1", 768), PS(0, y, y + 768), ch("m1", 768), A.not_equal)
-            elif k == "G":
-                lo, b = 768 * (c // 2), c % 2
-                o = ring[c] = PS((5, 6, 3, 4)[len(ring) % 4], 0, 384)
-                mm([(o, ID(3), R("wb", PB + lo + b, PB + lo + 768, 2)), (o, Z(ZSP, 2), R("ne", lo % NP + b, lo % NP + 768, 2)),
-                    (o, Z(ZSM, 2), R("ne", NP + lo + b, NP + lo + 768, 2))])
-            elif k == "C":
-                e, h, b = c // 4, c // 2 % 2, c % 2
-                lo = 2 * (768 * b + 384 * h) + e
-                act(R("gw", lo, lo + 767, 2), ring[c], AF.Copy)
+                tt(ch("mb"), PS(7 if c == 2 else held["H.%d" % c], 0, 512), R("xb", XS + 1024 * c + 1, XS + 1024 * c + 1024, 2), A.max)
+                if c < 2:
+                    drop("H.%d" % c, 1)
+            elif k in ("A1", "A2"):
+                gather("v", ch("m" + k[1]), R("xb", FS, FS + NW), ch("uq" if k == "A1" else "u2", 0, 32), ch("xc"))
             elif k == "Z":
+                mm([(PS(7, 0, NC), Z(ZB, 2 * r + 1), R("nb", r, NP, 8)) for r in range(8)], True, t == 0)
+            elif k in ("Y", "Yv"):
                 if t == 0:
-                    mm(wrap(PS(7, 0, KC), ZSP, "ne", 0, KC))
-                    act(H[0]("vs2"), PS(7, 0, KC), AF.Copy)
+                    act(W("vs2"), PS(7, 0, NC), AF.Copy) if k == "Y" else cp(W("vs2"), PS(7, 0, NC))
                     send_base()
-                mm([(PS(7, 0, 192), ID(4), W("yp"))], True, False)
-            elif k == "B":
-                if t:
-                    mm(wrap(PS(7, KC * c, KC * c + KC), ZSP, "ne", 0, KC), False, step == last)
-            elif k == "V":
-                c0, n = ((0, KC), (KC, 48), (KC + 48, 48))[c]
-                mm(wrap(PS(7, c0, c0 + n), ZSM, "ne1", 16 * c0, n), False, step == last)
-            elif k == "K":
-                gather("s", ch("go", 768), R("gw", 0, NS), ch("uk", 48))
+                    mm([(PS(7, 0, NC), ID(I0), W("one"))], True, False)
+            elif k == "G":
+                b = take("C" + copies[c], int(copies[c][1])) + c - int(copies[c][0])
+                mm([(PS(b, 0, 512), ID(I01), ch("wb", W1 + NF))] + [(PS(b, n, 512, 2), Z(ZSP, 2), ch("nb", 0, 256)) for n in range(2)]
+                   + [(PS(b, 0, 512), Z(ZSM, 2), ch("n2"))])
+            elif k in ("K", "Kv"):
+                lo = 96 * e + 48 * (c // 2)
+                gather("s" if k == "K" else "v", ch("go", 0, 768), R("gw", 0, NS), R("uk", lo, lo + 48))
+            elif k == "U0":
+                b = take(step, 1)
+                mm([(PS(b, 0, NC), ID(m), W("one")) for m in (ID64, IKK)] + [(PS(b, 96 * n, 96 * n + 96), ID(IK), H("lo", c)) for n in range(2)], True, False)
             elif k == "U":
-                kk, b = c // 2, c % 2
-                for n, zs in enumerate((ZA1, ZG)):
-                    mm([(PS(3 + 2 * kk + n, 0, KC), Z(zs, 2 * a + b), R("go", 768 * c + a, 768 * c + 768, 8)) for a in range(8)], b == 0, b == 1)
-            elif k == "mk":
-                for e in range(2):
-                    tt(R("mk", 192 * c + KC * e, 192 * c + KC * e + KC), PS(3 + 2 * c, 0, KC), H[e]("tgt"), A.is_equal)
-            elif k == "ck":
-                for e in range(2):
-                    lo = 192 * c + KC * e
-                    tt(R("ck", lo, lo + KC), PS(4 + 2 * c, 0, KC), R("mk", lo, lo + KC), A.mult)
+                mm([(PS(held["U0.%d" % (c // 2)], 96 * e, 96 * e + 96), Z(ZU, 2 * r + 1), R("go", 768 * c + r, 768 * c + 768, 8)) for r in range(8)], False, e == 1)
+            elif k == "cl":
+                for n, v in enumerate((16.0, 32.0)):
+                    ts(R("ck", NC * (2 * c + n), NC * (2 * c + n + 1)), PS(held["U0.%d" % c], 0, NC), -v, v, A.max, A.min)
+                drop("U0.%d" % c, 1)
             elif k == "AD":
-                if c == 0:
-                    mm([(PS(7, 0, 192), ID(0), ch("ck", 192))], False, step == last)
-                else:
-                    tt(W("vs%d" % t), PS(7, 0, 192), ch("ck", 192), A.add)
+                mm([(PS(7, 96 * c, 96 * c + 96), ID((I2, IM)[n // 2]), R("ck", 384 * c + 96 * n, 384 * c + 96 * n + 96)) for n in range(4)], False, step == last)
+            elif k == "V":
+                mm(wrap(PS(7, 64 * c, 64 * c + 64), ZSM, "n1", 1024 * c, 64), False, step == last)
+            elif k == "E":
+                cp(W("vs%d" % t), PS(7, 0, NC))
+
+    def odd(b):
+        mm([(PS(b, 0, NC), R("z8", 14 - 2 * r, 142 - 2 * r, 1, 8), R("g8", r, NP, 8, 8)) for r in range(8)])
 
     def decide(t):
-        P = lambda b, e: PS(b, KC * e, KC * e + KC)
-        others = [r for r in range(len(T.cores)) if r != rank]
-        mm([(PS(3, 0, 192), ID(0), W("vs%d" % t))], True, False)
+        def add(xs, start=False, stop=False, sym=False):
+            for b, m in ((3, I1 if sym else ISW), (4, I1)):
+                mm([(PS(b, 0, NC), ID(m), x) for x in xs], start, stop)
+        add([W("vs%d" % t)], True)
+        mm([(PS(3, 0, NC), ID(IODD), W("one"))], False, False)
         if t == 0:
+            others = [r for r in range(len(T.cores)) if r != rank]
             need("t", ("arr2", n_eng * len(others), {}))
-            mm([(P(3, e), ID(0), x) for e in range(2) for x in [H[0]("vs2")] + [R("land2", KC * r, KC * r + KC) for r in others]], False, False)
+            add([W("vs2")] + [slot(2, r) for r in others], sym=True)
         need("t", ("arr%d" % t, n_eng * (len(line) - 1), {}))
-        mm([(PS(3, 0, 192), ID(0), slot(t, n)) for n in range(len(line)) if n != me], False, False)
+        add([slot(t, n) for n in range(len(line)) if n != me])
         need("t", ("sib%d" % t, n_all, {}))
-        mm([(PS(3, 0, 192), ID(0), slot(t, len(line)))], False, True)
-        qn = "q%d" % (t + 1)
-        for e in range(2):
-            tt(H[e]("thr"), P(3, 1 - e), R("big", 192 * t + KC * e, 192 * t + KC * e + KC), A.max)
-        for e in range(2):
-            tt(P(4, e), P(3, e), H[e]("thr"), (A.is_ge, A.is_gt)[e])
-        for e in range(2):
-            tt(P(5, e), P(4, e), H[e]("dl"), A.mult)
-        for e in range(2):
-            tt(H[e](qn), P(5, e), H[e]("q%d" % t), A.add)
-        for e in range(2):
-            cp(H[e]("uq"), H[e](qn))
+        add([slot(t, len(line))], stop=True)
+        old, qn = ("swi", "b1")[t], "q%d" % (t + 1)
+        for fn in (lambda lo, hi: tt(W("thr", lo, hi), PS(3, lo, hi), W("big", lo, hi), A.max),
+                   lambda lo, hi: tt(PS(5, lo, hi), PS(4, lo, hi), W("thr", lo, hi), A.is_ge),
+                   lambda lo, hi: tt(PS(6, lo, hi), PS(5, lo, hi), W(old, lo, hi), A.not_equal),
+                   lambda lo, hi: tt(W(qn, lo, hi), PS(6, lo, hi), W("par2", lo, hi), A.add),
+                   lambda lo, hi: cp(W("uq", lo, hi), W(qn, lo, hi))):
+            for lo, hi in pieces(t + 1):
+                fn(lo, hi)
 
-    for t in range(3):
-        for e, q in enumerate("sv"):
-            gather(q, R("wb", PB + NP * e, PB + NP * e + NP), R("tab", 0, 5120), H[e]("uq"))
-        if t < 2:
-            mm(wrap(PS(7, 0, 192), ZP, "wb", PB, 192))
-        rest = stage(WA, "uq", "wb", 0, SPLIT["b"], ZA1, to("u2"), None)
-        if t == 2:
-            rest = stage(WA1, "u2", "wb", PB, SPLIT["f"], ZA, to("u4"), rest)
+    def split_gather(w, off, dst, lo, a):
+        gather("s", R(dst, lo, lo + 16 * a), w, R(off, 0, a))
+        gather("v", R(dst, lo + 16 * a, lo + NS), w, R(off, a, NC))
 
-            def put(h):
-                cp(H[h]("yao"), PS(3 + h, 0, KC))
-                dma("y", T.ya[h::2, :], ap(H[h]("yao")), [H[h]("yao")], [])
-                if h == 0:
-                    tt(W("yso"), W("q2"), W("qhi"), A.is_equal)
-                    for e in range(2):
-                        dma("s", T.ys[e::2, :], ap(H[e]("yso")), [H[e]("yso")], [])
-            stage(WA, "u4", "w4", 0, SPLIT["g"], ZA, put, rest)()
-            break
-        rest = stage(WA1, "u2", "w4", 0, SPLIT["c"], ZA1, take4, rest)
+    def observed():
+        for b in range(3):
+            mm([(PS(b, 0, 512), ID(I1), R("phs", 512 * b, 512 * b + 512))])
 
-        def partners():
-            mm(wrap(PS(7, 192, 384), ZP, "wb", 0, 192))
-            if t == 0:
-                for b in range(3):
-                    mm([(PS(b, 0, 512), ID(0), R("yp", 512 * b, 512 * b + 512))])
-        stage(R("xb", NS, NS + NF), "u4c", "xb", 0, SPLIT["d"], None, None, rest, partners)
+    def parity():
+        cp(R("genb", 0, 96), R("gen1", 0, 96))
+        dma("y", T.g8[0:8, :], T.genb[:], [R("genb", 0, 96)], [R("g8", 0, NP)])
+        ts(W("uk"), W("kdi"), -float(NF), None, A.add)
+
+    for t in range(2):
+        split_gather(win(TAB), "uq", "wb", W1 + NF, FIRST[t])
+        stages([(win(W1), "uq", "wb", TAB + NF, SHARE["p2"], ZA, 0, to("u2"), None),
+                (win(TAB), "u2", "w4", 0, SHARE["p4"], ZC, 1, take4, None),
+                (R("xb", FA, FA + NF), "u4c", "xb", X1, SHARE["x1"], None, 0, None,
+                 None if t else {0: observed, 1: lambda: ts(R("gen1", 0, 96), R("geni", 0, 96), 1, None, A.bitwise_and), 2: parity})])
         match(t)
         exchange(t)
+        for n in range(3):
+            persons(n)
+        odd(5)
         if t == 0:
-            tt(W("qhi"), W("td"), W("mu"), A.add)
-            tt(W("qsum"), W("td"), W("qhi"), A.add)
-            mm([(PS(4, 0, KC), R("z8", 15 - i, 143 - i, 1, 8), R("g8", 768 * (i % 2) + i // 2, 768 * (i % 2) + 768, 8, 8)) for i in range(16)])
-        ts(W("tc"), W("q%d" % t), -2.0, None, A.mult)
-        tt(W("dl"), W("qsum"), W("tc"), A.add)
-        if t == 0:
-            for n, (m, c) in enumerate(((-999.0, 1000.0), (-1000.0, 1000.0), (999.0, 1.0), (1000.0, 0.0))):
-                ts(R("big", KC * n, KC * n + KC), PS(4, 0, KC), m, c, A.mult, A.add)
+            cp(col("cs", 0), col("i2", 0))
+            ts(W("par2"), W("pari"), 2.0, None, A.mult)
+            ts(W("tg"), W("tg0"), col("cs", 0), None, A.add)
+            ts(W("big"), PS(5, 0, NC), -999.0, 1000.0, A.mult, A.add)
+            tt(W("rd"), W("tg"), W("q0"), A.subtract)
+            ts(PS(6, 0, NC), PS(5, 0, NC), -1.0, 1.0, A.mult, A.add)
+            tt(W("stay"), PS(6, 0, NC), W("rd"), A.mult)
+        else:
+            tt(W("rd"), W("q1"), W("stay"), A.add)
+            tt(W("b1"), W("q1"), W("par2"), A.subtract)
+            cp(W("ur"), W("rd"))
+            ts(W("big"), PS(5, 0, NC), 999.0, 1.0, A.mult, A.add)
+            split_gather(win(TAB), "ur", "wb", W1 + NF, NC - SHARE["r"])
         decide(t)
+
+    def switches():
+        cp(W("b2"), PS(6, 0, NC))
+        dma("y", T.ys[:], T.b2[:], [W("b2")], [])
+
+    def put(o, c0, c1):
+        cp(W("yao", c0, c1), o)
+        if c1 >= CUTS[-2]:
+            c0 = c0 if c1 == NC else 0
+            dma("y", T.ya[:, c0:c1], ap(W("yao", c0, c1)), [W("yao", c0, c1)], [])
+    stages([(win(W1), "uq", "wb", TAB + NF, SHARE["n1"], ZA, 0, to("u2"), {2: switches}),
+            (win(TAB), "u2", "wb", W1 + NF, SHARE["n2"], ZA, 0, to("u4"), None),
+            (win(W1), "u4", "w4", 0, SHARE["n4"], ZA, 0, put, None)])
 
     g.wait_ge(T.sem.sent, sent[0])
     for q in QUEUES:

@@ -4,9 +4,9 @@ from concourse.mybir import AluOpType as A, ActivationFunctionType as AF
 NF, NP, NS, NW, NC = 2048, 1536, 3072, 5120, 192
 BF, F32, I32, U16 = "bfloat16", "float32", "int32", "uint16"
 ZW = 144
-ZA, ZC, ZSP, ZSM, ZU, ZB = range(6)
-I1, IH, IMH, I01, I2, IM, IK, IKK, ID64, IODD, ISW, I0 = range(12)
-TAB, W1 = 0, NW
+ZA, ZSP, ZSM, ZU, ZB = range(5)
+I1, IH, IMH, I02, I2, IM, IK, IKK, ID64, IODD, ISW, I0 = range(12)
+W1, W2 = 0, NW
 FS, XS, FA, X1 = 0, NF, NW, NW + NF
 
 
@@ -15,31 +15,32 @@ def _sb(n, d):
 
 
 SCRATCH = {
-    "wb": _sb(2 * NW, BF), "tb": _sb(1024, BF), "w4": _sb(NS, BF), "xb": _sb(2 * NW, BF), "xc": _sb(NS, BF), "phs": _sb(NP, BF),
+    "wb": _sb(2 * NW, BF), "w4": _sb(NS, BF), "xb": _sb(2 * NW, BF), "xc": _sb(NS, BF), "phs": _sb(NP, BF),
     "mb": _sb(NP, BF), "m2": _sb(NS, BF), "m1": _sb(NS, BF), "nb": _sb(NP, BF), "n2": _sb(NS, BF), "n1": _sb(NS, BF),
     "sb": _sb(NP, BF), "s1": _sb(NS, BF), "s2": _sb(NS, BF), "gw": _sb(NS, BF), "go": _sb(NS, BF), "ck": _sb(4 * NC, BF),
     "pari": _sb(NC, I32), "swi": _sb(NC, I32), "kdi": _sb(NC, I32), "geni": _sb(96, I32), "gen1": _sb(96, I32), "genb": _sb(96, BF),
-    "g8": _sb(NP, BF), "par2": _sb(NC, F32), "q0": _sb(NC, F32), "q1": _sb(NC, F32), "q2": _sb(NC, F32), "b1": _sb(NC, F32), "b2": _sb(NC, F32),
-    "big": _sb(NC, F32), "thr": _sb(NC, F32), "tg0": _sb(NC, F32), "tg": _sb(NC, F32), "rd": _sb(NC, F32), "stay": _sb(NC, F32), "yao": _sb(NC, F32),
-    "uq": _sb(NC, U16), "u2": _sb(NC, U16), "u4": _sb(NC, U16), "u4c": _sb(NC, U16), "uk": _sb(NC, U16), "ur": _sb(NC, U16),
+    "pp": _sb(NC, I32), "pt": _sb(NC, I32), "rows": _sb(8 * NC, BF), "g8": _sb(NP, BF),
+    "par2": _sb(NC, F32), "q0": _sb(NC, F32), "q1": _sb(NC, F32), "v1": _sb(NC, F32), "sb0": _sb(NC, F32), "stp": _sb(NC, F32), "dp": _sb(NC, F32),
+    "p0": _sb(NC, F32), "p1": _sb(NC, F32), "p2": _sb(NC, F32), "b2": _sb(NC, F32),
+    "big": _sb(NC, F32), "thr": _sb(NC, F32), "tg0": _sb(NC, F32), "rd": _sb(NC, F32), "yao": _sb(NC, F32),
+    "uq": _sb(NC, U16), "up": _sb(NC, U16), "u2": _sb(NC, U16), "u4": _sb(NC, U16), "u4c": _sb(NC, U16), "uk": _sb(NC, U16),
     "vs0": _sb(NC, BF), "vs1": _sb(NC, BF), "vs2": _sb(NC, BF),
     "land0": _sb(5 * NC, BF), "land1": _sb(5 * NC, BF), "land2": _sb(8 * NC, BF),
-    "i1": _sb(4, I32), "i2": _sb(4, I32), "rt": _sb(4, F32), "cs": _sb(4, F32), "hc": _sb(12, F32),
-    "one": _sb(256, BF), "lo": _sb(256, BF), "lx": _sb(256, BF), "zz": _sb(6 * ZW, BF), "z8": _sb(ZW, BF), "idn": _sb(11 * 128 + ZW, BF),
+    "i1": _sb(2, I32), "i2": _sb(2, I32), "rt": _sb(2, F32), "cs": _sb(2, F32), "hc": _sb(8, F32),
+    "one": _sb(256, BF), "lo": _sb(256, BF), "zz": _sb(6 * ZW, BF), "z8": _sb(ZW, BF), "idn": _sb(11 * 128 + ZW, BF),
     "ps": ("psum", [128, 4096], F32),
 }
 QUEUES = ["v", "s", "t", "g"]
-NDMA = 24
+NDMA = 30
 SEMAPHORES = ["c_" + q for q in QUEUES] + ["d%d" % i for i in range(NDMA)] + ["arr0", "arr1", "arr2", "sib0", "sib1", "sent"]
 
 CUTS = (0, 64, 128, 192)
-FIRST = (96, 96, 96)
-SHARE = {"p2": 32, "p4": 30, "x1": 30, "n1": 30, "n2": 30, "n4": 32, "r": 90}
+SHARE = {"p2": 32, "p4": 30, "x1": 30, "n1": 30, "n2": 30, "n4": 32}
 LEAD = 1
-SBLK, GSELF = 3, 1536
-MATCH = ("L.0 L.1 X.1 X.3 X.5 Xv.0 X.4 T.0 Xv.2 T.1 H.0 H.1 M.0 M.1 T.2 d.b11 sg.b11 n.b01 ab.b11 A2.0 H.2 A2.1 d.201 T.3 T.4 sg.201 ab.201 A2.2 M.2 "
-         "T.5 d.211 A2.3 d.221 n.b21 n.231 sg.211 sg.221 A2.4 G.0 Z ab.211 ab.221 A2.5 G.3 n.241 n.251 Y C.31 G.1 C.02 A1.0 A1.3 G.2 G.4 C.21 C.41 "
-         "A1.1 A1.5 G.5 A1.2 C.51 K.0 K.1 U0.1 U0.0 U.0 U.1 A1.4 n.122 n.102 V.1 K.2 n.142 cl.0 U.2 V.0 K.3 U.3 V.2 cl.1 AD.0 AD.1 E").split()
+HS = (0, 128, 192)
+MATCH = ("L.0 L.1 Xv.0 X.1 T.0 Xv.2 H.0 X.3 M.0 T.1 H.1 M.1 X.4 T.2 T.3 T.4 d.b11 X.5 n.b01 H.2 A2.0 M.2 P.1 B2.1 A2.3 d.201 sg.b11 n.211 d.b21 T.5 P.3 "
+         "ab.b11 sg.201 sg.b21 ab.201 ab.b21 P.0 d.221 G.0 B2.4 G.1 sg.221 ab.221 Z n.231 C.11 P.2 n.241 G.2 C.01 P.4 G.3 n.251 G.4 P.5 Y G.5 C.21 C.31 "
+         "C.41 C.51 B1.2 B1.0 n.122 B1.4 U0.0 K.0 K.1 U0.1 U.0 V.1 n.102 U.1 n.142 cl.0 V.0 K.2 U.2 K.3 U.3 V.2 cl.1 AD.0 AD.1 E").split()
 
 
 def rank_program(g, core, T, topo):
@@ -52,8 +53,8 @@ def rank_program(g, core, T, topo):
     recs = {}
     ndma = [0]
 
-    def R(name, lo, hi, step=1, p=128):
-        return (name, lo, hi, step, p)
+    def R(name, lo, hi, step=1, p=128, row=None):
+        return (name, lo, hi, step, p, row)
 
     def ap(r):
         return T[r[0]][0:r[4], r[1]:r[2]:r[3]] if r[3] > 1 else T[r[0]][0:r[4], r[1]:r[2]]
@@ -70,8 +71,8 @@ def rank_program(g, core, T, topo):
         deps = {}
         for rs, w in ((reads, False), (writes, True)):
             for r in rs:
-                for (lo, hi, tok, eq, ew, st) in recs.get(r[0], []):
-                    hit = lo < r[2] and r[1] < hi and (w or ew) and not (st == r[3] and (lo - r[1]) % st)
+                for (lo, hi, tok, eq, ew, st, row) in recs.get(r[0], []):
+                    hit = lo < r[2] and r[1] < hi and (w or ew) and not (st == r[3] and (lo - r[1]) % st) and (row == r[5] or None in (row, r[5]))
                     if r[0] == "ps":
                         if eq != q:
                             hit = lo // 512 <= (r[2] - 1) // 512 and r[1] // 512 <= (hi - 1) // 512
@@ -95,11 +96,11 @@ def rank_program(g, core, T, topo):
             for r in rs:
                 l = recs.setdefault(r[0], [])
                 if w and r[3] == 1 and r[0] != "ps":
-                    l[:] = [x for x in l if not (r[1] <= x[0] and x[1] <= r[2])]
+                    l[:] = [x for x in l if not (r[1] <= x[0] and x[1] <= r[2] and r[5] in (None, x[6]))]
                 elif r[0] == "ps":
                     l[:] = [x for x in l if not (x[3] == q and r[1] // 512 <= x[0] // 512 and (x[1] - 1) // 512 <= (r[2] - 1) // 512
                                                  and (q == "t" or known[q].get(x[2][0], 0) >= x[2][1]))]
-                l.append((r[1], r[2], tok, "dma" if dma else q, w, r[3]))
+                l.append((r[1], r[2], tok, "dma" if dma else q, w, r[3], r[5]))
         return tok
 
     def ts(out, in0, s1, s2, o0, o1=None):
@@ -115,10 +116,13 @@ def rank_program(g, core, T, topo):
     def cp(out, a):
         return op("v", lambda: g.vector.tensor_copy(ap(out), ap(a)), [a], [out])
 
+    def fill(out, v):
+        return op("v", lambda: g.vector.memset(ap(out), v), [], [out])
+
     def act(out, a, f, bias=None, scale=None):
         kw = {}
         if bias is not None:
-            kw["bias"] = ap(bias)
+            kw["bias"] = ap(bias) if isinstance(bias, tuple) else bias
         if scale is not None:
             kw["scale"] = ap(scale) if isinstance(scale, tuple) else scale
         return op("s", lambda: g.scalar.activation(ap(out), ap(a), f, **kw), [a] + [x for x in (bias, scale) if isinstance(x, tuple)], [out])
@@ -167,76 +171,81 @@ def rank_program(g, core, T, topo):
         return [(out, Z(s, i ^ flip), R(src, lo + i, lo + 16 * n, 16)) for i in range(16)]
 
     W = lambda n, lo=0, hi=NC: R(n, lo, hi)
-    H = lambda n, h: R(n, 96 * h, 96 * h + 96)
     win = lambda base: R("wb", base, base + NW)
+    row = lambda n, lo=0, hi=NC: R("rows", NC * n + lo, NC * n + hi)
+    L = lambda n: PS(3 + n // 2, NC * (n % 2), NC * (n % 2) + NC)
+
+    def spread(q, r, n):
+        dma(q, T.wb[r::16, W1 + NF:W1 + NW], ap(row(n)), [row(n)], [R("wb", W1 + NF, W1 + NW, 1, 128, r)])
 
     dma("y", T.pari[:], T.par[:], [], [W("pari")])
     dma("s", T.swi[:], T.sw[:], [], [W("swi")])
+    iota(R("i1", 0, 2), [[-1, 2]], 16, 1, False)
+    blank = lambda n: fill(R("wb", W1 + NF + 768 * n, W1 + NF + 768 * n + 768), 0.0)
+    fill(R("one", 0, 256), 1.0)
+    blank(0)
+    ts(R("i2", 0, 2), R("i1", 0, 2), 15, None, A.bitwise_and)
+    op("v", lambda: g.vector.tensor_tensor_scan(T.lo[:], T.one[:], T.one[:], -1.0, A.add, A.mult), [R("one", 0, 256)], [R("lo", 0, 256)])
+    blank(1)
+    ts(R("rt", 0, 2), R("i2", 0, 2), 0.0, None, A.is_equal)
+    blank(2)
+    ts(R("hc", 0, 8), R("lo", 0, 8), col("rt", 0), 256.0, A.mult, A.mult)
+    blank(3)
+    for j in range(2):
+        ts(R("wb", W1 + 256 * j, W1 + 256 * j + 256), R("lo", 0, 256), col("rt", 1), col("hc", j), A.mult, A.add)
+    act(R("wb", W1 + 512, W1 + 1024), R("wb", W1, W1 + 512), AF.Identity, col("hc", 2))
+    act(R("wb", W1 + 1024, W1 + NF), R("wb", W1, W1 + 1024), AF.Identity, col("hc", 4))
+
+    ts(row(0), W("pari"), 2.0, None, A.mult)
+    ts(L(0), W("pari"), 2.0, None, A.mult)
+    ts(L(1), W("pari"), 1024.0, None, A.is_ge)
+    spread("y", 0, 0)
+    cp(row(2), W("swi"))
+    tt(row(1), L(0), row(0), A.subtract)
+    spread("y", 2, 2)
+    ts(W("pt"), W("pari"), 3, None, A.arith_shift_right)
+    spread("y", 1, 1)
+    ts(L(2), W("pari"), 382.0, 1920.0, A.mult, A.add)
+    ts(W("sb0"), W("swi"), 191.0, None, A.mult)
+    ts(W("v1"), W("pt"), -3071.0, None, A.mult)
+    tt(L(3), L(2), W("sb0"), A.add)
+    tt(W("q0"), L(0), W("swi"), A.add)
+    pieces = lambda *fns: [fn(lo, hi) for fn in fns for lo, hi in ((0, 96), (96, NC))]
+    part = lambda r, lo, hi: R(r[0], r[1] + lo, r[1] + hi)
+    pieces(lambda lo, hi: tt(W("rd", lo, hi), part(L(3), lo, hi), W("v1", lo, hi), A.add))
+    cp(W("uq"), W("q0"))
+    pieces(lambda lo, hi: tt(part(L(4), lo, hi), part(L(1), lo, hi), W("rd", lo, hi), A.mult),
+           lambda lo, hi: tt(W("p0", lo, hi), part(L(4), lo, hi), W("q0", lo, hi), A.add),
+           lambda lo, hi: cp(W("up", lo, hi), W("p0", lo, hi)))
+    act(R("wb", W2, W2 + 1024), R("wb", W1, W1 + 1024), AF.Copy)
     dma("y", ap(R("xb", FA, FA + NF)), T.fa[:], [], [R("xb", FA, FA + NF)])
-    dma("y", T.geni[:], T.gen[:], [], [R("geni", 0, 96)])
     dma("y", T.phs[:], T.ph[:], [], [R("phs", 0, NP)])
+    dma("y", T.geni[:], T.gen[:], [], [R("geni", 0, 96)])
     dma("y", T.kdi[:], T.kd[:], [], [W("kdi")])
 
-    iota(R("i1", 0, 4), [[-1, 4]], 16, 1, False)
-    op("v", lambda: g.vector.memset(T.one[:], 1.0), [], [R("one", 0, 256)])
-    ts(R("i2", 0, 3, 2), R("i1", 0, 3, 2), 15, None, A.bitwise_and)
-    ts(col("i2", 1), col("i1", 1), 14, None, A.bitwise_and)
-    op("v", lambda: g.vector.tensor_tensor_scan(T.lo[:], T.one[:], T.one[:], -1.0, A.add, A.mult), [R("one", 0, 256)], [R("lo", 0, 256)])
-    ts(R("rt", 0, 3), R("i2", 0, 3), 0.0, None, A.is_equal)
-    ts(R("hc", 0, 12), R("lo", 0, 12), col("rt", 0), None, A.mult)
-    ts(R("lx", 0, 256, 2), R("lo", 0, 256, 2), col("rt", 2), None, A.add)
-    ts(R("lx", 1, 256, 2), R("lo", 1, 256, 2), col("rt", 2), None, A.subtract)
-    tab = lambda lo, hi: R("wb", TAB + lo, TAB + hi)
-    block = lambda o, src, j: ts(o, R(src, 0, 256), col("rt", 1), col("hc", j), A.mult, A.add)
-    persons = lambda n: act(tab(NF + 1024 * n, NF + 1024 * n + 1024), R("tb", 0, 1024), AF.Identity, col("hc", 4 * n))
-    for j in range(8 - SBLK, 8):
-        act(tab(256 * j, 256 * j + 256), R("lo", 0, 256), AF.Identity, col("hc", j), col("rt", 1))
-    block(tab(0, 256), "lo", 0)
-    for j in range(4):
-        block(R("tb", 256 * j, 256 * j + 256), "lx", 8 + j)
-    persons(2)
-    for j in range(1, 8 - SBLK):
-        block(tab(256 * j, 256 * j + 256), "lo", j)
-
-    def pieces(t):
-        return ((0, FIRST[t]), (FIRST[t], NC))
-    founders = lambda lo, hi: (R("wb", W1 + lo, W1 + hi), tab(lo, hi))
-    for lo, hi in pieces(0):
-        ts(PS(3, lo, hi), W("pari", lo, hi), 2.0, None, A.mult)
-    cp(tab(NF, NF + 1024), R("tb", 0, 1024))
-    for lo, hi in pieces(0):
-        tt(W("q0", lo, hi), PS(3, lo, hi), W("swi", lo, hi), A.add)
-    ts(tab(NF + 1024, NF + 2048), R("tb", 0, 1024), col("hc", 4), None, A.add)
-    act(*founders(0, NF - GSELF), AF.Copy)
-    for lo, hi in pieces(0):
-        cp(W("uq", lo, hi), W("q0", lo, hi))
-
     zc = lambda s, c=15: R("zz", s * ZW + c, s * ZW + c + 128, 16)
-    iota(R("zz", 0, 6 * ZW), [[0, 6 * ZW]], 0, 0)
+    iota(R("zz", 0, 5 * ZW), [[0, 5 * ZW]], 0, 0)
     iota(R("idn", 128 * I0, 128 * I0 + ZW), [[0, ZW]], 0, 0)
     ident = lambda k, v: asel(ID(k), ID(I0), [[-1, 128]], A.not_equal, v, 0, 1)
     diag = lambda k: asel(ID(k), ID(k), [[-1, 128]], A.is_equal, 0.0, 0, 1)
-    for n in range(2):
-        for s, rows in ((ZA, (0, 1)), (ZC, (0, 2))):
-            asel(zc(s), zc(s), [[-16, 8]], A.not_equal, (256.0, 1.0)[n], -rows[n], 1)
-    if GSELF:
-        gcopy(*founders(NF - GSELF, NF))
-    for k, v in ((I1, 1.0), (IH, 0.5), (IMH, -0.5)):
+    rows = lambda s, n, v: asel(zc(s), zc(s), [[16, 8]], A.is_gt, v, n, -1)
+    for s, n, v in ((ZA, 0, 1.0), (ZSP, 0, 1.0), (ZSM, 0, -1.0), (ZA, 3, 0.0), (ZSP, 16, 0.0), (ZSM, 16, 0.0)):
+        rows(s, n, v)
+    ident(I1, 1.0)
+    gcopy(R("wb", W2 + 1024, W2 + NF), R("wb", W1 + 1024, W1 + NF))
+    for k, v in ((IH, 0.5), (IMH, -0.5)):
         ident(k, v)
-    for e in range(2):
-        gcopy(R("xb", FS + e, FS + NF, 2), R("xb", FA + 1 - e, FA + NF, 2))
-    for n in range(2):
-        for s, v in ((ZSP, 1.0), (ZSM, -1.0)):
-            asel(zc(s), zc(s), [[16, 8]], A.is_gt, (v, 0.0)[n], 16 * n, -1)
-    asel(ID(I01), ID(I1), [[0, 8], [-1, 16]], A.is_ge, 0.0, 1, 0)
+    asel(ID(I02), ID(I1), [[0, 8], [-1, 16]], A.is_ge, 0.0, 2, 0)
     for c in (14, 15):
         gcopy(zc(ZB, c), zc(ZSP))
+    for e in range(2):
+        gcopy(R("xb", FS + e, FS + NF, 2), R("xb", FA + 1 - e, FA + NF, 2))
 
     def late(c):
         if c == 0:
             iota(ID(ID64), [[0, 8], [-64, 16]], 0, 0)
-            for r, (v, k, u) in enumerate(((16384.0, IK, -1024.0), (64.0, IKK, -64.0 * NF), (1.0, I2, 2.0))):
-                asel(zc(ZU), zc(ZU), [[-16, 8]], A.not_equal, v, -r, 1)
+            for n, v, k, u in ((0, 64.0, IK, -1024.0), (3, 1.0, IKK, -64.0 * NF), (4, 0.0, I2, 2.0)):
+                rows(ZU, n, v)
                 ident(k, u)
             gcopy(zc(ZU, 14), zc(ZU))
             diag(ID64)
@@ -264,7 +273,7 @@ def rank_program(g, core, T, topo):
                 if extra and n in extra:
                     extra[n]()
                 if zs is not None:
-                    o = PS(3 + nb % 3, 0, c1 - c0)
+                    o = PS((3, 4, 6)[nb % 3], 0, c1 - c0)
                     nb += 1
                     mm(wrap(o, zs, dst, lo + 16 * c0, c1 - c0, flip))
                     wait.append((k, n, lambda o=o, c0=c0, c1=c1, take=take: take(o, c0, c1)))
@@ -273,9 +282,13 @@ def rank_program(g, core, T, topo):
 
     to = lambda name: (lambda o, c0, c1: cp(W(name, c0, c1), o))
 
-    def take4(o, c0, c1):
-        ts(W("u4c", c0, c1), o, NF - 1.0, None, A.min)
-        cp(W("u4", c0, c1), o)
+    def partners(t):
+        bank = lambda n: PS((5, 7, 5)[n], CUTS[n], CUTS[n + 1])
+        lists = lambda ns: [mm(wrap(bank(n), ZA, "w4", 16 * CUTS[n], CUTS[n + 1] - CUTS[n], 1)) for n in ns]
+        casts = lambda ns: [cp(W("u4", CUTS[n], CUTS[n + 1]), bank(n)) for n in ns]
+        return {0: lambda: lists((0, 1)),
+                1: lambda: (casts((0,)), lists((2,)), t or ts(R("gen1", 0, 96), R("geni", 0, 96), 1, None, A.bitwise_and)),
+                2: lambda: (casts((1, 2)), t or (observed(), parity()))}
 
     near = [c for c in T.cores if c != core and c in topo.cores_of(core)]
     far = [c for c in T.cores if c not in topo.cores_of(core)]
@@ -353,12 +366,12 @@ def rank_program(g, core, T, topo):
             c = int(c)
             ch = lambda n, lo=0, w=512: R(n, lo + w * c, lo + w * c + w)
             e = c % 2
+            h0, h1 = HS[c // 2:c // 2 + 2] if k in ("K", "Kv", "U") else HS[e:e + 2]
+            hn = h1 - h0
             if k in ("X", "Xv"):
                 gather("s" if k == "X" else "v", ch("xb", XS), R("xb", FA, FA + NW), ch("u4", 0, 32))
             elif k == "T":
                 dma("y", ap(ch("xc")), ap(ch("xb", XS)), [ch("xb", XS)], [ch("xc")])
-            elif k == "Tg":
-                gcopy(ch("xc"), ch("xb", XS))
             elif k == "Ts":
                 gather("s", ch("xc"), R("xb", FA, FA + NW), ch("u4", 0, 32))
             elif k == "L":
@@ -370,8 +383,9 @@ def rank_program(g, core, T, topo):
                 tt(ch("mb"), PS(7 if c == 2 else held["H.%d" % c], 0, 512), R("xb", XS + 1024 * c + 1, XS + 1024 * c + 1024, 2), A.max)
                 if c < 2:
                     drop("H.%d" % c, 1)
-            elif k in ("A1", "A2"):
-                gather("v", ch("m" + k[1]), R("xb", FS, FS + NW), ch("uq" if k == "A1" else "u2", 0, 32), ch("xc"))
+            elif k in ("A1", "A2", "B1", "B2"):
+                n = c + 1 + (k[0] == "B")
+                gather("v", R("m" + k[1], 512 * c, 512 * n), R("xb", FS, FS + NW), R("uq" if k[1] == "1" else "u2", 32 * c, 32 * n), R("xc", 512 * c, 512 * n))
             elif k == "Z":
                 mm([(PS(7, 0, NC), Z(ZB, 2 * r + 1), R("nb", r, NP, 8)) for r in range(8)], True, t == 0)
             elif k in ("Y", "Yv"):
@@ -379,31 +393,31 @@ def rank_program(g, core, T, topo):
                     act(W("vs2"), PS(7, 0, NC), AF.Copy) if k == "Y" else cp(W("vs2"), PS(7, 0, NC))
                     send_base()
                     mm([(PS(7, 0, NC), ID(I0), W("one"))], True, False)
-            elif k == "G":
+            elif k in ("P", "G"):
                 b = take("C" + copies[c], int(copies[c][1])) + c - int(copies[c][0])
-                mm([(PS(b, 0, 512), ID(I01), ch("wb", W1 + NF))] + [(PS(b, n, 512, 2), Z(ZSP, 2), ch("nb", 0, 256)) for n in range(2)]
-                   + [(PS(b, 0, 512), Z(ZSM, 2), ch("n2"))])
+                if k == "P":
+                    mm([(PS(b, i, 512, 16), ID(I02), R("wb", W1 + NF + NC * i + 32 * c, W1 + NF + NC * i + 32 * c + 32)) for i in range(16)], True, False)
+                else:
+                    mm([(PS(b, n, 512, 2), Z(ZSP, 3), ch("nb", 0, 256)) for n in range(2)] + [(PS(b, 0, 512), Z(ZSM, 3), ch("n2"))], False, True)
             elif k in ("K", "Kv"):
-                lo = 96 * e + 48 * (c // 2)
-                gather("s" if k == "K" else "v", ch("go", 0, 768), R("gw", 0, NS), R("uk", lo, lo + 48))
+                gather("s" if k == "K" else "v", R("go", NP * e + 8 * h0, NP * e + 8 * h1), R("gw", 0, NS), R("uk", 96 * e + h0 // 2, 96 * e + h1 // 2))
             elif k == "U0":
                 b = take(step, 1)
-                mm([(PS(b, 0, NC), ID(m), W("one")) for m in (ID64, IKK)] + [(PS(b, 96 * n, 96 * n + 96), ID(IK), H("lo", c)) for n in range(2)], True, False)
+                mm([(PS(b, 0, 2 * hn), ID(m), R("one", 0, 2 * hn)) for m in (ID64, IKK)]
+                   + [(PS(b, hn * x, hn * x + hn), ID(IK), R("lo", h0, h1)) for x in range(2)], True, False)
             elif k == "U":
-                mm([(PS(held["U0.%d" % (c // 2)], 96 * e, 96 * e + 96), Z(ZU, 2 * r + 1), R("go", 768 * c + r, 768 * c + 768, 8)) for r in range(8)], False, e == 1)
+                mm([(PS(held["U0.%d" % (c // 2)], hn * e, hn * e + hn), Z(ZU, 2 * r + 1), R("go", NP * e + 8 * h0 + r, NP * e + 8 * h1, 8)) for r in range(8)],
+                   False, e == 1)
             elif k == "cl":
-                for n, v in enumerate((16.0, 32.0)):
-                    ts(R("ck", NC * (2 * c + n), NC * (2 * c + n + 1)), PS(held["U0.%d" % c], 0, NC), -v, v, A.max, A.min)
+                for x, v in enumerate((16.0, 32.0)):
+                    ts(R("ck", 4 * h0 + 2 * hn * x, 4 * h0 + 2 * hn * (x + 1)), PS(held["U0.%d" % c], 0, 2 * hn), -v, v, A.max, A.min)
                 drop("U0.%d" % c, 1)
             elif k == "AD":
-                mm([(PS(7, 96 * c, 96 * c + 96), ID((I2, IM)[n // 2]), R("ck", 384 * c + 96 * n, 384 * c + 96 * n + 96)) for n in range(4)], False, step == last)
+                mm([(PS(7, h0, h1), ID((I2, IM)[x // 2]), R("ck", 4 * h0 + hn * x, 4 * h0 + hn * x + hn)) for x in range(4)], False, step == last)
             elif k == "V":
                 mm(wrap(PS(7, 64 * c, 64 * c + 64), ZSM, "n1", 1024 * c, 64), False, step == last)
             elif k == "E":
                 cp(W("vs%d" % t), PS(7, 0, NC))
-
-    def odd(b):
-        mm([(PS(b, 0, NC), R("z8", 14 - 2 * r, 142 - 2 * r, 1, 8), R("g8", r, NP, 8, 8)) for r in range(8)])
 
     def decide(t):
         def add(xs, start=False, stop=False, sym=False):
@@ -419,18 +433,17 @@ def rank_program(g, core, T, topo):
         add([slot(t, n) for n in range(len(line)) if n != me])
         need("t", ("sib%d" % t, n_all, {}))
         add([slot(t, len(line))], stop=True)
-        old, qn = ("swi", "b1")[t], "q%d" % (t + 1)
-        for fn in (lambda lo, hi: tt(W("thr", lo, hi), PS(3, lo, hi), W("big", lo, hi), A.max),
-                   lambda lo, hi: tt(PS(5, lo, hi), PS(4, lo, hi), W("thr", lo, hi), A.is_ge),
-                   lambda lo, hi: tt(PS(6, lo, hi), PS(5, lo, hi), W(old, lo, hi), A.not_equal),
-                   lambda lo, hi: tt(W(qn, lo, hi), PS(6, lo, hi), W("par2", lo, hi), A.add),
-                   lambda lo, hi: cp(W("uq", lo, hi), W(qn, lo, hi))):
-            for lo, hi in pieces(t + 1):
-                fn(lo, hi)
-
-    def split_gather(w, off, dst, lo, a):
-        gather("s", R(dst, lo, lo + 16 * a), w, R(off, 0, a))
-        gather("v", R(dst, lo + 16 * a, lo + NS), w, R(off, a, NC))
+        pieces(lambda lo, hi: tt(W("thr", lo, hi), PS(3, lo, hi), W("big", lo, hi), A.max),
+               lambda lo, hi: tt(PS(5, lo, hi), PS(4, lo, hi), W("thr", lo, hi), A.is_ge))
+        if t == 0:
+            pieces(lambda lo, hi: tt(row(4, lo, hi), PS(5, lo, hi), row(2, lo, hi), A.not_equal))
+            spread("y", 2, 4)
+        pieces(lambda lo, hi: tt(PS(6, lo, hi), PS(5, lo, hi), W("dp", lo, hi), A.mult),
+               lambda lo, hi: tt(W("p%d" % (t + 1), lo, hi), PS(6, lo, hi), W("p%d" % t, lo, hi), A.add),
+               lambda lo, hi: cp(W("up", lo, hi), W("p%d" % (t + 1), lo, hi)))
+        if t == 0:
+            tt(W("q1"), row(4), W("par2"), A.add)
+            cp(W("uq"), W("q1"))
 
     def observed():
         for b in range(3):
@@ -442,34 +455,37 @@ def rank_program(g, core, T, topo):
         ts(W("uk"), W("kdi"), -float(NF), None, A.add)
 
     for t in range(2):
-        split_gather(win(TAB), "uq", "wb", W1 + NF, FIRST[t])
-        stages([(win(W1), "uq", "wb", TAB + NF, SHARE["p2"], ZA, 0, to("u2"), None),
-                (win(TAB), "u2", "w4", 0, SHARE["p4"], ZC, 1, take4, None),
-                (R("xb", FA, FA + NF), "u4c", "xb", X1, SHARE["x1"], None, 0, None,
-                 None if t else {0: observed, 1: lambda: ts(R("gen1", 0, 96), R("geni", 0, 96), 1, None, A.bitwise_and), 2: parity})])
+        stages([(win(W1), "up", "wb", W2 + NF, SHARE["p2"], ZA, 0, to("u2"), None),
+                (win(W2), "u2", "w4", 0, SHARE["p4"], ZA, 0, lambda o, c0, c1: ts(W("u4c", c0, c1), o, NF - 1.0, None, A.min), None),
+                (R("xb", FA, FA + NF), "u4c", "xb", X1, SHARE["x1"], None, 0, None, partners(t))])
         match(t)
         exchange(t)
-        for n in range(3):
-            persons(n)
-        odd(5)
+        mm([(L(4), R("z8", 14 - 2 * r, 142 - 2 * r, 1, 8), R("g8", r, NP, 8, 8)) for r in range(8)])
         if t == 0:
+            ts(L(6), W("pari"), 1024.0, 191.0, A.is_ge, A.mult)
             cp(col("cs", 0), col("i2", 0))
             ts(W("par2"), W("pari"), 2.0, None, A.mult)
-            ts(W("tg"), W("tg0"), col("cs", 0), None, A.add)
-            ts(W("big"), PS(5, 0, NC), -999.0, 1000.0, A.mult, A.add)
-            tt(W("rd"), W("tg"), W("q0"), A.subtract)
-            ts(PS(6, 0, NC), PS(5, 0, NC), -1.0, 1.0, A.mult, A.add)
-            tt(W("stay"), PS(6, 0, NC), W("rd"), A.mult)
+            ts(L(8), row(2), -2.0, 1.0, A.mult, A.add)
+            ts(W("stp"), L(6), 1.0, None, A.add)
+            ts(W("big"), L(4), -999.0, 1000.0, A.mult, A.add)
+            tt(W("dp"), L(8), W("stp"), A.mult)
         else:
-            tt(W("rd"), W("q1"), W("stay"), A.add)
-            tt(W("b1"), W("q1"), W("par2"), A.subtract)
-            cp(W("ur"), W("rd"))
-            ts(W("big"), PS(5, 0, NC), 999.0, 1.0, A.mult, A.add)
-            split_gather(win(TAB), "ur", "wb", W1 + NF, NC - SHARE["r"])
+            ts(L(6), W("tg0"), col("cs", 0), None, A.add)
+            ts(L(8), row(4), -2.0, 1.0, A.mult, A.add)
+            tt(W("rd"), L(6), W("q1"), A.subtract)
+            ts(L(7), L(4), -1.0, 1.0, A.mult, A.add)
+            tt(W("dp"), L(8), W("stp"), A.mult)
+            tt(L(9), L(7), W("rd"), A.mult)
+            ts(W("big"), L(4), 999.0, 1.0, A.mult, A.add)
+            tt(L(6), L(9), W("par2"), A.add)
+            cp(row(6), L(6))
+            spread("y", 0, 6)
+            tt(row(7), L(6), row(6), A.subtract)
+            spread("s", 1, 7)
         decide(t)
 
     def switches():
-        cp(W("b2"), PS(6, 0, NC))
+        tt(W("b2"), PS(5, 0, NC), row(4), A.not_equal)
         dma("y", T.ys[:], T.b2[:], [W("b2")], [])
 
     def put(o, c0, c1):
@@ -477,8 +493,8 @@ def rank_program(g, core, T, topo):
         if c1 >= CUTS[-2]:
             c0 = c0 if c1 == NC else 0
             dma("y", T.ya[:, c0:c1], ap(W("yao", c0, c1)), [W("yao", c0, c1)], [])
-    stages([(win(W1), "uq", "wb", TAB + NF, SHARE["n1"], ZA, 0, to("u2"), {2: switches}),
-            (win(TAB), "u2", "wb", W1 + NF, SHARE["n2"], ZA, 0, to("u4"), None),
+    stages([(win(W1), "up", "wb", W2 + NF, SHARE["n1"], ZA, 0, to("u2"), {2: switches}),
+            (win(W2), "u2", "wb", W1 + NF, SHARE["n2"], ZA, 0, to("u4"), None),
             (win(W1), "u4", "w4", 0, SHARE["n4"], ZA, 0, put, None)])
 
     g.wait_ge(T.sem.sent, sent[0])

@@ -4,10 +4,11 @@ from concourse.mybir import AluOpType as A, ActivationFunctionType as AF
 NF, NP, NS, NW, NC = 2048, 1536, 3072, 5120, 192
 BF, F32, I32, U16 = "bfloat16", "float32", "int32", "uint16"
 ZW = 144
-ZA, ZSP, ZSM, ZU, ZB = range(5)
-I1, IH, IMH, I02, I2, IM, IK, IKK, ID64, IODD, ISW, I0 = range(12)
+ZA, ZSP, ZSM, ZU, ZB, ZV, ZGP, ZGM, ZP = range(9)
+I1, IM, I191, I16, IH, IMH, I2, IK, IN, I02, ID64, IODD, ISW, I0 = range(14)
 W1, W2 = 0, NW
 FS, XS, FA, X1 = 0, NF, NW, NW + NF
+R0, R1, DL, SW1, Q0, Q1, A1, A2, MR, SG = range(10)
 
 
 def _sb(n, d):
@@ -17,36 +18,68 @@ def _sb(n, d):
 SCRATCH = {
     "wb": _sb(2 * NW, BF), "w4": _sb(NS, BF), "xb": _sb(2 * NW, BF), "xc": _sb(NS, BF), "phs": _sb(NP, BF),
     "mb": _sb(NP, BF), "m2": _sb(NS, BF), "m1": _sb(NS, BF), "nb": _sb(NP, BF), "n2": _sb(NS, BF), "n1": _sb(NS, BF),
-    "sb": _sb(NP, BF), "s1": _sb(NS, BF), "s2": _sb(NS, BF), "gw": _sb(NS, BF), "go": _sb(NS, BF), "ck": _sb(4 * NC, BF),
+    "sb": _sb(NP, BF), "s1": _sb(NS, BF), "s2": _sb(NS, BF), "gw": _sb(NS + 16, BF), "go": _sb(NS, BF), "pl": _sb(NS, BF), "ck": _sb(4 * NC, BF),
     "pari": _sb(NC, I32), "swi": _sb(NC, I32), "kdi": _sb(NC, I32), "geni": _sb(96, I32), "gen1": _sb(96, I32), "genb": _sb(96, BF),
-    "pp": _sb(NC, I32), "pt": _sb(NC, I32), "rows": _sb(8 * NC, BF), "g8": _sb(NP, BF),
-    "par2": _sb(NC, F32), "q0": _sb(NC, F32), "q1": _sb(NC, F32), "v1": _sb(NC, F32), "sb0": _sb(NC, F32), "stp": _sb(NC, F32), "dp": _sb(NC, F32),
-    "p0": _sb(NC, F32), "p1": _sb(NC, F32), "p2": _sb(NC, F32), "b2": _sb(NC, F32),
-    "big": _sb(NC, F32), "thr": _sb(NC, F32), "tg0": _sb(NC, F32), "rd": _sb(NC, F32), "yao": _sb(NC, F32),
-    "uq": _sb(NC, U16), "up": _sb(NC, U16), "u2": _sb(NC, U16), "u4": _sb(NC, U16), "u4c": _sb(NC, U16), "uk": _sb(NC, U16),
+    "pa": _sb(NC, I32), "pb": _sb(NC, I32), "rows": _sb(10 * NC, BF), "g8": _sb(NP, BF),
+    "stp": _sb(NC, F32), "dp": _sb(NC, F32), "p0": _sb(NC, F32), "p1": _sb(NC, F32), "p2": _sb(NC, F32), "b2": _sb(NC, F32),
+    "big": _sb(NC, F32), "thr": _sb(NC, F32), "tk": _sb(NC, F32), "rd": _sb(NC, F32), "re": _sb(NC, F32), "yao": _sb(NC, F32), "ukf": _sb(NC, F32),
+    "uq": _sb(NC, U16), "up": _sb(NC, U16), "u2": _sb(NC, U16), "u4": _sb(NC, U16), "u4c": _sb(NC, U16), "uk0": _sb(NC, U16), "uk1": _sb(NC, U16),
     "vs0": _sb(NC, BF), "vs1": _sb(NC, BF), "vs2": _sb(NC, BF),
-    "land0": _sb(5 * NC, BF), "land1": _sb(5 * NC, BF), "land2": _sb(8 * NC, BF),
-    "i1": _sb(2, I32), "i2": _sb(2, I32), "rt": _sb(2, F32), "cs": _sb(2, F32), "hc": _sb(8, F32),
-    "one": _sb(256, BF), "lo": _sb(256, BF), "zz": _sb(6 * ZW, BF), "z8": _sb(ZW, BF), "idn": _sb(11 * 128 + ZW, BF),
+    "land0": _sb(5 * NC, BF), "land1": _sb(5 * NC, BF), "land2": _sb(5 * NC, BF),
+    "i1": _sb(2, I32), "i2": _sb(2, I32), "rt": _sb(2, F32), "cs": _sb(8, F32), "hi": _sb(16, F32), "hc": _sb(16, F32),
+    "one": _sb(256, BF), "lo": _sb(256, BF), "zz": _sb(9 * ZW + 16, BF), "z8": _sb(ZW, BF), "idn": _sb(13 * 128 + ZW, BF),
     "ps": ("psum", [128, 4096], F32),
 }
-QUEUES = ["v", "s", "t", "g"]
-NDMA = 30
-SEMAPHORES = ["c_" + q for q in QUEUES] + ["d%d" % i for i in range(NDMA)] + ["arr0", "arr1", "arr2", "sib0", "sib1", "sent"]
 
 CUTS = (0, 64, 128, 192)
-SHARE = {"p2": 32, "p4": 30, "x1": 30, "n1": 30, "n2": 30, "n4": 32}
-LEAD = 1
-HS = (0, 128, 192)
-MATCH = ("L.0 L.1 Xv.0 X.1 T.0 Xv.2 H.0 X.3 M.0 T.1 H.1 M.1 X.4 T.2 T.3 T.4 d.b11 X.5 n.b01 H.2 A2.0 M.2 P.1 B2.1 A2.3 d.201 sg.b11 n.211 d.b21 T.5 P.3 "
-         "ab.b11 sg.201 sg.b21 ab.201 ab.b21 P.0 d.221 G.0 B2.4 G.1 sg.221 ab.221 Z n.231 C.11 P.2 n.241 G.2 C.01 P.4 G.3 n.251 G.4 P.5 Y G.5 C.21 C.31 "
-         "C.41 C.51 B1.2 B1.0 n.122 B1.4 U0.0 K.0 K.1 U0.1 U.0 V.1 n.102 U.1 n.142 cl.0 V.0 K.2 U.2 K.3 U.3 V.2 cl.1 AD.0 AD.1 E").split()
+SHARE = {"p0": 32, "p2": 32, "p4": 30, "x1": 30, "n1": 30, "n2": 30, "n4": 32}
+LEAD = 64
+HS = ((0, 96, 144, 192),) * 2
+VB = ((0, 96, 192), (0, 96, 192), (0, 192))
+LAST = ((0, 96, 28), (96, 144, 24), (144, 192, 24))
+SUMS = ((3, 4), (1, 2))
+PIECES = 2
+GZ = 256
+MATCH = (("L.0 X.1 Xv.0 Xv.2 X.3 H.0 T.0 P.11 M.0 X.5 T.1 T.2 P.01 H.1 n.b01 X.4 T.3 M.1 Q1.4 T.4 T.5 H.2 A2.0 d.b11 M.2 d.201 B2.1 sg.b11 D1.4 L.1 L.2 sg.201 "
+          "P.21 n.211 d.b21 ab.201 n.221 ab.b11 G.1 A2.3 G.0 sg.b21 G.2 B2.4 C.01 P.41 C.11 P.31 n.231 ab.b21 P.51 n.251 C.21 G.3 n.241 G.5 C.31 B1.0 U0.0 G.4 "
+          "C.51 Z.0 C.41 n.102 K.00 A1.2 K.01 U.00 n.121 U0.2 U0.1 Z.1 A1.3 K.20 U.01 V.03 K.10 cl.0 n.131 K.11 AD.0 U.10 E.0 U.20 n.142 K.21 V.31 U.11 U.21 "
+          "cl.1 V.42 cl.2 AD.1 AD.2 E.1").split(),
+         ("X.1 Xv.0 P.11 Xv.2 X.3 H.0 T.0 T.1 M.0 X.5 H.1 T.2 P.31 M.1 X.4 n.b01 A2.0 P2.5 H.2 T.3 T.4 d.b11 M.2 Q1.4 d.201 F2.5 B2.1 sg.201 D1.4 A2.3 sg.b11 "
+          "P.21 n.211 ab.201 P.01 n.222 ab.b11 G.1 G.0 A2.4 C.11 G.3 C.01 G.2 n.b21 P.41 n.241 C.31 P.51 Q.0 Q.1 n.251 C.21 G.4 B1.0 G.5 C.41 Z.0 Z.1 C.51 "
+          "A1.2 K.01 n.102 n.121 K.00 U.01 n.142 V.03 K.11 U.00 A1.3 K.10 V.42 E.0 K.21 n.131 U.10 U.11 K.20 U.21 V.31 U.20 E.1").split())
+QUEUES = ["v", "s", "t", "g"]
+NDMA = 34
+SEMAPHORES = (["c_" + q for q in QUEUES] + ["d%d" % i for i in range(NDMA)] + ["sent"]
+              + ["%s%d%d" % (n, t, b) for n in ("arr", "sib") for t in range(3) for b in range(3)]
+              + ["%s%d%d" % (n, t, b) for n in ("hin", "hout") for t in range(2) for b in range(6)])
+
+
+def folds(t):
+    return [(x[1], 512 * int(x[-1]), 512 * (int(x[-1]) + 1 + (x[0] == "D"))) for x in MATCH[t] if x[0] in "FD"]
+
+
+def helper_of(c, T, topo):
+    return [h for h in topo.cores_of(c) if h not in T.cores and topo.die(h) == topo.die(c)][0]
+
+
+def hand_back(g, core, T, topo):
+    for c in T.cores:
+        if helper_of(c, T, topo) == core:
+            n, sent = len(topo.engines(core, c)), 0
+            rid, pid = topo.addr(c, core)
+            for t in range(2):
+                for k, (kind, lo, hi) in enumerate(folds(t)):
+                    g.wait_ge(T.sem["hin%d%d" % (t, k)], n)
+                    g.remote_dma(T["m" + kind][:, lo:hi], T["mn"[t] + kind][:, lo:hi], T.sem["hout%d%d" % (t, k)], T.sem.sent, pid, rid, topo.mask(core, c))
+                    sent += n
+            if sent:
+                g.wait_ge(T.sem.sent, sent)
 
 
 def rank_program(g, core, T, topo):
     rank = T.rank_of(core)
     if rank is None:
-        return
+        return hand_back(g, core, T, topo)
     Q = {"v": g.vector, "s": g.scalar, "t": g.tensor, "g": g, "y": g.sync}
     cnt = {q: 0 for q in QUEUES}
     known = {q: {} for q in Q}
@@ -67,7 +100,7 @@ def rank_program(g, core, T, topo):
                 if known[q].get(k, 0) < v:
                     known[q][k] = v
 
-    def op(q, fn, reads, writes, dma=False):
+    def op(q, fn, reads, writes, dma=False, done=None):
         deps = {}
         for rs, w in ((reads, False), (writes, True)):
             for r in rs:
@@ -83,7 +116,9 @@ def rank_program(g, core, T, topo):
         for tok in sorted(deps.values(), key=lambda t: t[0] == "c_" + q):
             need(q, tok)
         ins = fn()
-        if dma:
+        if done:
+            tok = done + (dict(known[q]),)
+        elif dma:
             name = "d%d" % ndma[0]
             ndma[0] += 1
             ins.then_inc(T.sem[name], 16)
@@ -100,7 +135,7 @@ def rank_program(g, core, T, topo):
                 elif r[0] == "ps":
                     l[:] = [x for x in l if not (x[3] == q and r[1] // 512 <= x[0] // 512 and (x[1] - 1) // 512 <= (r[2] - 1) // 512
                                                  and (q == "t" or known[q].get(x[2][0], 0) >= x[2][1]))]
-                l.append((r[1], r[2], tok, "dma" if dma else q, w, r[3], r[5]))
+                l.append((r[1], r[2], tok, "dma" if dma or done else q, w, r[3], r[5]))
         return tok
 
     def ts(out, in0, s1, s2, o0, o1=None):
@@ -173,159 +208,186 @@ def rank_program(g, core, T, topo):
     W = lambda n, lo=0, hi=NC: R(n, lo, hi)
     win = lambda base: R("wb", base, base + NW)
     row = lambda n, lo=0, hi=NC: R("rows", NC * n + lo, NC * n + hi)
-    L = lambda n: PS(3 + n // 2, NC * (n % 2), NC * (n % 2) + NC)
+    L = lambda n, lo=0, hi=NC: PS(3 + n // 2, NC * (n % 2) + lo, NC * (n % 2) + hi)
+    slots = lambda out, o: ts(out, o, float(NF), None, A.add)
 
     def spread(q, r, n):
         dma(q, T.wb[r::16, W1 + NF:W1 + NW], ap(row(n)), [row(n)], [R("wb", W1 + NF, W1 + NW, 1, 128, r)])
 
     dma("y", T.pari[:], T.par[:], [], [W("pari")])
-    dma("s", T.swi[:], T.sw[:], [], [W("swi")])
+    dma("y", T.swi[:], T.sw[:], [], [W("swi")])
+    dma("y", T.geni[:], T.gen[:], [], [R("geni", 0, 96)])
+    dma("y", T.kdi[:], T.kd[:], [], [W("kdi")])
     iota(R("i1", 0, 2), [[-1, 2]], 16, 1, False)
-    blank = lambda n: fill(R("wb", W1 + NF + 768 * n, W1 + NF + 768 * n + 768), 0.0)
+    iota(R("hi", 0, 16), [[16, 16]], -128, 0)
+    persons = lambda lo, hi: R("wb", W1 + NF + lo, W1 + NF + hi)
     fill(R("one", 0, 256), 1.0)
-    blank(0)
+    fill(persons(0, 256), 0.0)
     ts(R("i2", 0, 2), R("i1", 0, 2), 15, None, A.bitwise_and)
     op("v", lambda: g.vector.tensor_tensor_scan(T.lo[:], T.one[:], T.one[:], -1.0, A.add, A.mult), [R("one", 0, 256)], [R("lo", 0, 256)])
-    blank(1)
     ts(R("rt", 0, 2), R("i2", 0, 2), 0.0, None, A.is_equal)
-    blank(2)
-    ts(R("hc", 0, 8), R("lo", 0, 8), col("rt", 0), 256.0, A.mult, A.mult)
-    blank(3)
+    act(persons(256, 512), persons(0, 256), AF.Copy)
+    act(persons(512, 1024), persons(0, 512), AF.Copy)
+    fill(persons(1024, 1280), 0.0)
+    ts(R("hc", 0, 16), R("hi", 0, 16), col("rt", 0), None, A.mult)
+    fill(persons(1280, 1536), 0.0)
     for j in range(2):
         ts(R("wb", W1 + 256 * j, W1 + 256 * j + 256), R("lo", 0, 256), col("rt", 1), col("hc", j), A.mult, A.add)
-    act(R("wb", W1 + 512, W1 + 1024), R("wb", W1, W1 + 512), AF.Identity, col("hc", 2))
-    act(R("wb", W1 + 1024, W1 + NF), R("wb", W1, W1 + 1024), AF.Identity, col("hc", 4))
+    fill(persons(1536, NS - GZ), 0.0)
+    act(R("wb", W1 + 512, W1 + 1024), R("wb", W1, W1 + 512), AF.Identity, col("hc", 10))
+    act(R("wb", W1 + 1024, W1 + NF), R("wb", W1, W1 + 1024), AF.Identity, col("hc", 12))
 
-    ts(row(0), W("pari"), 2.0, None, A.mult)
-    ts(L(0), W("pari"), 2.0, None, A.mult)
-    ts(L(1), W("pari"), 1024.0, None, A.is_ge)
-    spread("y", 0, 0)
-    cp(row(2), W("swi"))
-    tt(row(1), L(0), row(0), A.subtract)
-    spread("y", 2, 2)
-    ts(W("pt"), W("pari"), 3, None, A.arith_shift_right)
-    spread("y", 1, 1)
-    ts(L(2), W("pari"), 382.0, 1920.0, A.mult, A.add)
-    ts(W("sb0"), W("swi"), 191.0, None, A.mult)
-    ts(W("v1"), W("pt"), -3071.0, None, A.mult)
-    tt(L(3), L(2), W("sb0"), A.add)
-    tt(W("q0"), L(0), W("swi"), A.add)
-    pieces = lambda *fns: [fn(lo, hi) for fn in fns for lo, hi in ((0, 96), (96, NC))]
-    part = lambda r, lo, hi: R(r[0], r[1] + lo, r[1] + hi)
-    pieces(lambda lo, hi: tt(W("rd", lo, hi), part(L(3), lo, hi), W("v1", lo, hi), A.add))
-    cp(W("uq"), W("q0"))
-    pieces(lambda lo, hi: tt(part(L(4), lo, hi), part(L(1), lo, hi), W("rd", lo, hi), A.mult),
-           lambda lo, hi: tt(W("p0", lo, hi), part(L(4), lo, hi), W("q0", lo, hi), A.add),
-           lambda lo, hi: cp(W("up", lo, hi), W("p0", lo, hi)))
+    zc = lambda s, c=15: R("zz", s * ZW + c, s * ZW + c + 128, 16)
+    ident = lambda k, v: asel(ID(k), ID(I0), [[-1, 128]], A.not_equal, v, 0, 1)
+    diag = lambda k: asel(ID(k), ID(k), [[-1, 128]], A.is_equal, 0.0, 0, 1)
+    rows = lambda s, n, v, c=15: asel(zc(s, c), zc(s, c), [[16, 8]], A.is_gt, v, n, -1)
+    clear = lambda s0, s1: iota(R("zz", s0 * ZW, s1 * ZW), [[0, (s1 - s0) * ZW]], 0, 0)
+    iota(R("idn", 128 * I0, 128 * I0 + ZW), [[0, ZW]], 0, 0)
+    if GZ:
+        iota(persons(NS - GZ, NS), [[0, GZ]], 0, 0)
+    for k, v in ((I1, 1.0), (I191, 191.0)):
+        ident(k, v)
+    clear(ZA, ZA + 1)
+    ident(I16, 16.0)
+    for n, v in ((0, 16.0), (1, 1.0), (3, 0.0)):
+        rows(ZA, n, v)
+
+    ts(W("pb"), W("pari"), 7, None, A.bitwise_and)
+    ts(W("pa"), W("pari"), 3, None, A.arith_shift_right)
+    ts(L(0), W("pb"), 2.0, None, A.mult)
+    ts(row(R0), W("pa"), -128.0, None, A.add)
+    spread("y", 0, R0)
+    tt(row(R1), L(0), W("swi"), A.add)
+    spread("y", 1, R1)
+    ts(L(2), W("pari"), 1024.0, None, A.is_ge)
+    ts(row(A1), row(R0), 0.0, None, A.max)
+    tt(row(MR), L(2), row(R1), A.mult)
+    ts(row(A2), row(R0), 0.0, 16.0, A.min, A.mult)
+    place = lambda o: [(o, ID(k), row(n)) for k, n in ((I1, R1), (I1, A1), (I191, MR), (I1, A2))]
+    mm(place(PS(0, 0, NC)))
+    mm([(PS(1, 0, NC), ID(k), row(n)) for k, n in ((I16, R0), (I1, R1))])
+    ts(R("gen1", 0, 96), R("geni", 0, 96), 1, None, A.bitwise_and)
+    ts(W("uk0"), W("kdi"), 16.0 - NF, None, A.add)
+    cp(R("genb", 0, 96), R("gen1", 0, 96))
+    fill(R("gw", 0, 16), 0.0)
+    slots(W("up"), PS(0, 0, NC))
+    slots(W("uq"), PS(1, 0, NC))
     act(R("wb", W2, W2 + 1024), R("wb", W1, W1 + 1024), AF.Copy)
     dma("y", ap(R("xb", FA, FA + NF)), T.fa[:], [], [R("xb", FA, FA + NF)])
     dma("y", T.phs[:], T.ph[:], [], [R("phs", 0, NP)])
-    dma("y", T.geni[:], T.gen[:], [], [R("geni", 0, 96)])
-    dma("y", T.kdi[:], T.kd[:], [], [W("kdi")])
+    dma("y", T.g8[0:8, :], T.genb[:], [R("genb", 0, 96)], [R("g8", 0, NP)])
 
-    zc = lambda s, c=15: R("zz", s * ZW + c, s * ZW + c + 128, 16)
-    iota(R("zz", 0, 5 * ZW), [[0, 5 * ZW]], 0, 0)
-    iota(R("idn", 128 * I0, 128 * I0 + ZW), [[0, ZW]], 0, 0)
-    ident = lambda k, v: asel(ID(k), ID(I0), [[-1, 128]], A.not_equal, v, 0, 1)
-    diag = lambda k: asel(ID(k), ID(k), [[-1, 128]], A.is_equal, 0.0, 0, 1)
-    rows = lambda s, n, v: asel(zc(s), zc(s), [[16, 8]], A.is_gt, v, n, -1)
-    for s, n, v in ((ZA, 0, 1.0), (ZSP, 0, 1.0), (ZSM, 0, -1.0), (ZA, 3, 0.0), (ZSP, 16, 0.0), (ZSM, 16, 0.0)):
-        rows(s, n, v)
-    ident(I1, 1.0)
     gcopy(R("wb", W2 + 1024, W2 + NF), R("wb", W1 + 1024, W1 + NF))
+    clear(ZSP, ZV)
     for k, v in ((IH, 0.5), (IMH, -0.5)):
         ident(k, v)
+    for s, n, v in ((ZSP, 0, 1.0), (ZSM, 0, -1.0), (ZSP, 16, 0.0), (ZSM, 16, 0.0)):
+        rows(s, n, v)
+    for e in range(2):
+        gcopy(R("xb", FS + e, FS + NF, 2), R("xb", FA + 1 - e, FA + NF, 2))
     asel(ID(I02), ID(I1), [[0, 8], [-1, 16]], A.is_ge, 0.0, 2, 0)
     for c in (14, 15):
         gcopy(zc(ZB, c), zc(ZSP))
-    for e in range(2):
-        gcopy(R("xb", FS + e, FS + NF, 2), R("xb", FA + 1 - e, FA + NF, 2))
 
     def late(c):
         if c == 0:
             iota(ID(ID64), [[0, 8], [-64, 16]], 0, 0)
-            for n, v, k, u in ((0, 64.0, IK, -1024.0), (3, 1.0, IKK, -64.0 * NF), (4, 0.0, I2, 2.0)):
-                rows(ZU, n, v)
+            rows(ZU, 0, 1024.0)
+            for n, v, k, u in ((1, 64.0, IK, -1024.0), (3, 1.0, I2, 2.0), (4, 0.0, IM, -1.0)):
                 ident(k, u)
-            gcopy(zc(ZU, 14), zc(ZU))
+                rows(ZU, n, v)
             diag(ID64)
-            ident(IM, -1.0)
-            return
-        iota(ID(IODD), [[0, 64], [1, 2]], 0, 0)
-        z8 = R("z8", 0, ZW, 1, 8)
-        asel(z8, R("idn", 128 * I0, 128 * I0 + ZW, 1, 8), [[1, ZW]], A.not_equal, 1.0, -15, -16)
-        diag(IODD)
-        asel(z8, z8, [[1, ZW]], A.not_equal, 1.0, -14, -16)
-        for e in range(2):
-            asel(R("idn", 128 * ISW + e, 128 * ISW + 128, 2), R("idn", 128 * I0, 128 * I0 + 64), [[-2, 64]], A.not_equal, 1.0, e - 1, 1)
-        iota(W("tg0"), [[16, NC]], NF, 0)
+            gcopy(zc(ZU, 14), zc(ZU))
+        elif c == 1:
+            iota(ID(IODD), [[0, 64], [1, 2]], 0, 0)
+            z8 = R("z8", 0, ZW, 1, 8)
+            asel(z8, R("idn", 128 * I0, 128 * I0 + ZW, 1, 8), [[1, ZW]], A.not_equal, 1.0, -15, -16)
+            diag(IODD)
+            asel(z8, z8, [[1, ZW]], A.not_equal, 1.0, -14, -16)
+            for e in range(2):
+                asel(R("idn", 128 * ISW + e, 128 * ISW + 128, 2), R("idn", 128 * I0, 128 * I0 + 64), [[-2, 64]], A.not_equal, 1.0, e - 1, 1)
+        elif c == 2:
+            ident(IN, -32.0)
+        else:
+            clear(ZV, ZP + 1)
+            one_row = ((ZV, 14, 4, -1.0), (ZV, 15, 3, 1.0), (ZP, 15, 5, 64.0), (ZP, 16, 5, -64.0), (ZP, 17, 5, 1.0), (ZP, 18, 5, -1.0),
+                       (ZV, 14, 6, 32.0), (ZV, 15, 5, -32.0))
+            for part in (one_row[:6], one_row[6:]):
+                for d in range(2):
+                    for s, c, n, v in part:
+                        rows(s, n + d, 0.0 if d else v, c)
+            for s, c, z in ((ZGP, 15, ZSP), (ZGP, 16, ZSM), (ZGM, 15, ZSM), (ZGM, 16, ZSP)):
+                gcopy(zc(s, c), zc(z))
 
-    def stages(todo):
+    def even(name):
+        return [(c0, c1, SHARE[name] * (c1 - c0) // 128 * 2) for c0, c1 in zip(CUTS, CUTS[1:])]
+
+    def stages(todo, banks):
         wait, nb = [], 0
-        for k, (w, off, dst, lo, share, zs, flip, take, extra) in enumerate(todo):
-            for n in range(len(CUTS) - 1):
-                c0, c1 = CUTS[n], CUTS[n + 1]
-                while wait and wait[0][0] < k and wait[0][1] <= n + LEAD:
+        for k, (w, off, dst, lo, cuts, zs, take, extra) in enumerate(todo):
+            for n, (c0, c1, share) in enumerate(cuts):
+                while wait and wait[0][0] < k and wait[0][1] < c1 + LEAD:
                     wait.pop(0)[2]()
-                a = c0 + share * (c1 - c0) // 128 * 2
+                a = c0 + share
                 gather("v", R(dst, lo + 16 * c0, lo + 16 * a), w, R(off, c0, a))
                 gather("s", R(dst, lo + 16 * a, lo + 16 * c1), w, R(off, a, c1))
                 if extra and n in extra:
                     extra[n]()
                 if zs is not None:
-                    o = PS((3, 4, 6)[nb % 3], 0, c1 - c0)
+                    o = PS(banks[nb % 3], 0, c1 - c0)
                     nb += 1
-                    mm(wrap(o, zs, dst, lo + 16 * c0, c1 - c0, flip))
-                    wait.append((k, n, lambda o=o, c0=c0, c1=c1, take=take: take(o, c0, c1)))
+                    mm(wrap(o, zs, dst, lo + 16 * c0, c1 - c0))
+                    wait.append((k, c0, lambda o=o, c0=c0, c1=c1, take=take: take(o, c0, c1)))
         for x in wait:
             x[2]()
 
-    to = lambda name: (lambda o, c0, c1: cp(W(name, c0, c1), o))
+    to = lambda name: (lambda o, c0, c1: slots(W(name, c0, c1), o))
 
     def partners(t):
         bank = lambda n: PS((5, 7, 5)[n], CUTS[n], CUTS[n + 1])
         lists = lambda ns: [mm(wrap(bank(n), ZA, "w4", 16 * CUTS[n], CUTS[n + 1] - CUTS[n], 1)) for n in ns]
-        casts = lambda ns: [cp(W("u4", CUTS[n], CUTS[n + 1]), bank(n)) for n in ns]
+        casts = lambda ns: [slots(W("u4", CUTS[n], CUTS[n + 1]), bank(n)) for n in ns]
         return {0: lambda: lists((0, 1)),
-                1: lambda: (casts((0,)), lists((2,)), t or ts(R("gen1", 0, 96), R("geni", 0, 96), 1, None, A.bitwise_and)),
-                2: lambda: (casts((1, 2)), t or (observed(), parity()))}
+                1: lambda: (casts((0,)), lists((2,))),
+                2: lambda: (casts((1, 2)), observed())}
 
     near = [c for c in T.cores if c != core and c in topo.cores_of(core)]
-    far = [c for c in T.cores if c not in topo.cores_of(core)]
     line = [c for c in T.cores if topo.die(c) == topo.die(core)]
+    others = [c for c in line if c != core]
     me = line.index(core)
-    far_mask = topo.mask(core, far[0])
-    near_mask = topo.mask(core, near[0]) & ~far_mask
-    n_eng, n_all = len(topo.engines(core, far[0])), len(topo.engines(core, near[0]))
+    n_far, n_all = len(topo.engines(core, others[0])), len(topo.engines(core, near[0]))
     sent = [0]
     ids = lambda cs: [DstId(rid=topo.addr(c, core)[0], pnc=topo.addr(c, core)[1]) for c in cs]
-    slot = lambda t, n: R("land%d" % t, NC * n, NC * n + NC)
+    slot = lambda t, n, lo, hi: R("land%d" % t, NC * n + lo, NC * n + hi)
+    landed = lambda t, lo, hi: [slot(t, n, lo, hi) for n in range(len(line)) if n != me]
 
-    def send_base():
-        vs = W("vs2")
-        for x in recs[vs[0]]:
-            need("g", x[2])
-        g.remote_dma_fused([RemoteDMATransfer(dst_ids=ids(cs), dma_engine_mask=m, remote_sem=T.sem.arr2, srcs=[ap(vs)], dsts=[ap(slot(2, rank))] * len(cs))
-                            for cs, m in ((far, far_mask), (near, near_mask))], local_sem=T.sem.sent)
-        sent[0] += 2 * n_eng
+    def remote(cs, sem, srcs, dst, reads, writes=(), done=None, alu=0, spare=0):
+        mask = topo.mask(core, cs[0]) & ~spare
+        sent[0] += bin(mask).count("1")
+        tr = RemoteDMATransfer(dst_ids=ids(cs), dma_engine_mask=mask, remote_sem=T.sem[sem], srcs=[ap(x) for x in srcs], dsts=[ap(dst)] * len(cs), alu_op=alu)
+        op("g", lambda: g.remote_dma_fused([tr], local_sem=T.sem.sent), reads, list(writes), done=done or ("sent", 10 ** 6))
 
-    def exchange(t):
-        vs = W("vs%d" % t)
-        for x in recs[vs[0]]:
-            need("g", x[2])
-        cs = [c for c in line if c != core]
-        g.remote_dma_fused([RemoteDMATransfer(dst_ids=ids(cs), dma_engine_mask=far_mask, remote_sem=T.sem["arr%d" % t], srcs=[ap(vs)],
-                                              dsts=[ap(slot(t, me))] * len(cs))], local_sem=T.sem.sent)
-        need("g", ("arr%d" % t, n_eng * len(cs), {}))
-        g.remote_dma_fused([RemoteDMATransfer(dst_ids=ids(near), dma_engine_mask=topo.mask(core, near[0]), remote_sem=T.sem["sib%d" % t],
-                                              srcs=[ap(vs)] + [ap(slot(t, n)) for n in range(len(line)) if n != me],
-                                              dsts=[ap(slot(t, len(line)))], alu_op=1)], local_sem=T.sem.sent)
-        sent[0] += n_eng + n_all
+    def send(t, b):
+        lo, hi = VB[t][b:b + 2]
+        remote(others, "arr%d%d" % (t, b), [W("vs%d" % t, lo, hi)], slot(t, me, lo, hi), [W("vs%d" % t, lo, hi)])
+
+    def fold(t, b):
+        lo, hi = VB[t][b:b + 2]
+        need("g", ("arr%d%d" % (t, b), n_far * len(others), {}))
+        remote(near, "sib%d%d" % (t, b), [W("vs%d" % t, lo, hi)] + landed(t, lo, hi), slot(t, len(line), lo, hi), [], alu=1,
+               spare=topo.mask(core, others[0]) if hi < NC or t == 2 else 0)
+    n_sib = lambda hi: n_all - n_far if hi < NC else n_all
+    early = "Y" in MATCH[0]
+
+    seen = sorted({(int(x[3]) + h) // (1 if x[2] == "b" else 2) for m in MATCH for x in m if x[:2] == "n." for h in range(int(x[4]))})
 
     def match(t):
-        held, free = {}, [3, 4, 5, 6]
-        last = [x for x in MATCH if x[0] == "V" or x[:2] == "AD"][-1]
-        copies = {int(x[-2]) + n: x[-2:] for x in MATCH if x[0] == "C" for n in range(int(x[-1]))}
+        held, free = {}, [b for b in range(7) if b not in seen]
+        order, plain = MATCH[t], {"1": "pl", "2": "w4"}
+        vb = lambda c: max(b for b in range(len(VB[t]) - 1) if VB[t][b] <= c)
+        first = {"V": lambda c: 32 * int(c[0]), "U": lambda c: HS[t][int(c[0])], "AD": lambda c: HS[t][int(c[0])]}
+        last = {vb(first[k](c)): k + "." + c for k, c in (x.split(".") for x in order if "." in x) if k in ("V", "U" if t else "AD")}
+        copies = {int(x[2]) + n: x[2:] for x in order if x[:2] == "P." for n in range(int(x[3]))}
 
         def take(key, n):
             if key not in held:
@@ -336,7 +398,8 @@ def rank_program(g, core, T, topo):
 
         def drop(key, n):
             free.extend(range(held[key], held[key] + n))
-        for step in MATCH:
+        votes = lambda lo, hi: PS(take("votes%d" % vb(lo), 1) if vb(lo) else 7, lo, hi)
+        for step in order:
             k, c = (step.split(".") + ["0"])[:2]
             if k in ("d", "sg", "ab", "nz", "n"):
                 kind, w, lo = c[0], int(c[2]), 512 * int(c[1])
@@ -358,144 +421,195 @@ def rank_program(g, core, T, topo):
                 else:
                     ts(blk("n"), blk("s"), 0.0, None, A.not_equal)
                 continue
-            if k in ("C", "Cv"):
-                o, a = R("gw", 512 * int(c[0]), 512 * (int(c[0]) + int(c[1]))), PS(held["C" + c], 0, 512 * int(c[1]))
-                act(o, a, AF.Copy) if k == "C" else cp(o, a)
-                drop("C" + c, int(c[1]))
+            if k in ("P", "C", "V"):
+                c0, w = int(c[0]), int(c[1])
+                if k == "P":
+                    for b in range(c0, c0 + w):
+                        lo = W1 + NF + 32 * b
+                        mm([(PS(take("C" + c, w) + b - c0, i, 512, 16), Z(ZP, 3) if t else ID(I02), R("wb", lo + NC * i, lo + NC * i + 32)) for i in range(16)],
+                           True, False)
+                elif k == "C":
+                    act(R("gw", 16 + 512 * c0, 16 + 512 * (c0 + w)), PS(held["C" + c], 0, 512 * w), *((AF.Relu, col("cs", 2)) if t else (AF.Copy,)))
+                    drop("C" + c, w)
+                else:
+                    mm(wrap(votes(32 * c0, 32 * (c0 + w)), ZSM, "n1", 512 * c0, 32 * w), False, step in last.values())
+                continue
+            if k in ("K", "Kv", "U"):
+                b, e = int(c[0]), int(c[1])
+                h0, h1 = HS[t][b:b + 2]
+                lo, hi = NP * e + 8 * h0, NP * e + 8 * h1
+                if k != "U":
+                    gather("s" if k == "K" else "v", R("go", lo, hi), R("gw", 0, NS + 16), R("uk%d" % t, lo // 16, hi // 16))
+                elif t:
+                    mm([(votes(h0, h1), Z(ZV, 2 * r + 1), R("go", lo + r, hi, 8)) for r in range(8)], False, step in last.values())
+                else:
+                    mm([(PS(held["U0.%d" % b], (h1 - h0) * e, (h1 - h0) * (e + 1)), Z(ZU, 2 * r + 1), R("go", lo + r, hi, 8)) for r in range(8)], False, e == 1)
                 continue
             c = int(c)
             ch = lambda n, lo=0, w=512: R(n, lo + w * c, lo + w * c + w)
-            e = c % 2
-            h0, h1 = HS[c // 2:c // 2 + 2] if k in ("K", "Kv", "U") else HS[e:e + 2]
+            h0, h1 = HS[t][c:c + 2] if k in ("U0", "cl", "AD") else VB[t][c:c + 2] if k in ("Z", "E", "Es") else (0, NC)
             hn = h1 - h0
+            wide = lambda n, lo=0: R(n, lo + 512 * c, lo + 512 * (c + 1 + (k[0] in "BQD")))
             if k in ("X", "Xv"):
                 gather("s" if k == "X" else "v", ch("xb", XS), R("xb", FA, FA + NW), ch("u4", 0, 32))
             elif k == "T":
                 dma("y", ap(ch("xc")), ap(ch("xb", XS)), [ch("xb", XS)], [ch("xc")])
-            elif k == "Ts":
-                gather("s", ch("xc"), R("xb", FA, FA + NW), ch("u4", 0, 32))
             elif k == "L":
-                if t == 0:
-                    late(c)
+                late(c)
+            elif k == "Q":
+                spread("y", c, (Q0, Q1)[c])
             elif k == "H":
                 mm([(PS(7 if c == 2 else take(step, 1), 0, 512), ID(I1), R("xb", XS + 1024 * c, XS + 1024 * c + 1024, 2))])
             elif k == "M":
                 tt(ch("mb"), PS(7 if c == 2 else held["H.%d" % c], 0, 512), R("xb", XS + 1024 * c + 1, XS + 1024 * c + 1024, 2), A.max)
                 if c < 2:
                     drop("H.%d" % c, 1)
-            elif k in ("A1", "A2", "B1", "B2"):
-                n = c + 1 + (k[0] == "B")
-                gather("v", R("m" + k[1], 512 * c, 512 * n), R("xb", FS, FS + NW), R("uq" if k[1] == "1" else "u2", 32 * c, 32 * n), R("xc", 512 * c, 512 * n))
-            elif k == "Z":
-                mm([(PS(7, 0, NC), Z(ZB, 2 * r + 1), R("nb", r, NP, 8)) for r in range(8)], True, t == 0)
-            elif k in ("Y", "Yv"):
-                if t == 0:
-                    act(W("vs2"), PS(7, 0, NC), AF.Copy) if k == "Y" else cp(W("vs2"), PS(7, 0, NC))
-                    send_base()
-                    mm([(PS(7, 0, NC), ID(I0), W("one"))], True, False)
-            elif k in ("P", "G"):
-                b = take("C" + copies[c], int(copies[c][1])) + c - int(copies[c][0])
-                if k == "P":
-                    mm([(PS(b, i, 512, 16), ID(I02), R("wb", W1 + NF + NC * i + 32 * c, W1 + NF + NC * i + 32 * c + 32)) for i in range(16)], True, False)
+            elif k in ("A1", "A2", "B1", "B2", "P1", "Q1", "P2", "Q2"):
+                o = wide(plain[k[1]] if k[0] in "PQ" else "m" + k[1])
+                off = R("uq" if k[1] == "1" else "u2", o[1] // 16, o[2] // 16)
+                gather("s", o, R("xb", FS, FS + NW), off, None if k[0] in "PQ" else wide("xc"))
+            elif k in ("F1", "D1", "F2", "D2"):
+                n, srcs = folds(t).index((k[1],) + wide("")[1:3]), [wide(plain[k[1]]), wide("xb", XS)]
+                remote([helper_of(core, T, topo)], "hin%d%d" % (t, n), srcs, wide("mn"[t] + k[1]), srcs, [wide("m" + k[1])], ("hout%d%d" % (t, n), n_all), 2)
+            elif k == "G":
+                b = held["C" + copies[c]] + c - int(copies[c][0])
+                mm([(PS(b, n, 512, 2), Z((ZSP, ZGP)[t], 3), ch("nb", 0, 256)) for n in range(2)] + [(PS(b, 0, 512), Z((ZSM, ZGM)[t], 3), ch("n2"))], False, True)
+            elif k in ("Y", "Z"):
+                o = votes(h0, h1)
+                if t == 0 and k == "Z" and early:
+                    mm([(o, ID(I0), W("one", h0, h1))], True, False)
                 else:
-                    mm([(PS(b, n, 512, 2), Z(ZSP, 3), ch("nb", 0, 256)) for n in range(2)] + [(PS(b, 0, 512), Z(ZSM, 3), ch("n2"))], False, True)
-            elif k in ("K", "Kv"):
-                gather("s" if k == "K" else "v", R("go", NP * e + 8 * h0, NP * e + 8 * h1), R("gw", 0, NS), R("uk", 96 * e + h0 // 2, 96 * e + h1 // 2))
+                    mm([(o, Z(ZB, 2 * r + 1), R("nb", 8 * h0 + r, 8 * h1, 8)) for r in range(8)], True, k == "Y")
+            elif k == "Yc":
+                act(W("vs2"), PS(7, 0, NC), AF.Copy)
+                send(2, 0)
+            elif k == "Yf":
+                fold(2, 0)
             elif k == "U0":
                 b = take(step, 1)
-                mm([(PS(b, 0, 2 * hn), ID(m), R("one", 0, 2 * hn)) for m in (ID64, IKK)]
+                mm([(PS(b, 0, 2 * hn), ID(ID64), R("one", 0, 2 * hn))]
                    + [(PS(b, hn * x, hn * x + hn), ID(IK), R("lo", h0, h1)) for x in range(2)], True, False)
-            elif k == "U":
-                mm([(PS(held["U0.%d" % (c // 2)], hn * e, hn * e + hn), Z(ZU, 2 * r + 1), R("go", NP * e + 8 * h0 + r, NP * e + 8 * h1, 8)) for r in range(8)],
-                   False, e == 1)
             elif k == "cl":
                 for x, v in enumerate((16.0, 32.0)):
                     ts(R("ck", 4 * h0 + 2 * hn * x, 4 * h0 + 2 * hn * (x + 1)), PS(held["U0.%d" % c], 0, 2 * hn), -v, v, A.max, A.min)
                 drop("U0.%d" % c, 1)
             elif k == "AD":
-                mm([(PS(7, h0, h1), ID((I2, IM)[x // 2]), R("ck", 4 * h0 + hn * x, 4 * h0 + hn * x + hn)) for x in range(4)], False, step == last)
-            elif k == "V":
-                mm(wrap(PS(7, 64 * c, 64 * c + 64), ZSM, "n1", 1024 * c, 64), False, step == last)
-            elif k == "E":
-                cp(W("vs%d" % t), PS(7, 0, NC))
+                mm([(votes(h0, h1), ID((I2, IM)[x // 2]), R("ck", 4 * h0 + hn * x, 4 * h0 + hn * x + hn)) for x in range(4)], False, step in last.values())
+            elif k in ("E", "Es"):
+                cp(W("vs%d" % t, h0, h1), votes(h0, h1)) if k == "E" else act(W("vs%d" % t, h0, h1), votes(h0, h1), AF.Copy)
+                send(t, c)
+        for b in range(len(VB[t]) - 1):
+            fold(t, b)
 
-    def decide(t):
-        def add(xs, start=False, stop=False, sym=False):
-            for b, m in ((3, I1 if sym else ISW), (4, I1)):
-                mm([(PS(b, 0, NC), ID(m), x) for x in xs], start, stop)
-        add([W("vs%d" % t)], True)
-        mm([(PS(3, 0, NC), ID(IODD), W("one"))], False, False)
-        if t == 0:
-            others = [r for r in range(len(T.cores)) if r != rank]
-            need("t", ("arr2", n_eng * len(others), {}))
-            add([W("vs2")] + [slot(2, r) for r in others], sym=True)
-        need("t", ("arr%d" % t, n_eng * (len(line) - 1), {}))
-        add([slot(t, n) for n in range(len(line)) if n != me])
-        need("t", ("sib%d" % t, n_all, {}))
-        add([slot(t, len(line))], stop=True)
-        pieces(lambda lo, hi: tt(W("thr", lo, hi), PS(3, lo, hi), W("big", lo, hi), A.max),
-               lambda lo, hi: tt(PS(5, lo, hi), PS(4, lo, hi), W("thr", lo, hi), A.is_ge))
-        if t == 0:
-            pieces(lambda lo, hi: tt(row(4, lo, hi), PS(5, lo, hi), row(2, lo, hi), A.not_equal))
-            spread("y", 2, 4)
-        pieces(lambda lo, hi: tt(PS(6, lo, hi), PS(5, lo, hi), W("dp", lo, hi), A.mult),
-               lambda lo, hi: tt(W("p%d" % (t + 1), lo, hi), PS(6, lo, hi), W("p%d" % t, lo, hi), A.add),
-               lambda lo, hi: cp(W("up", lo, hi), W("p%d" % (t + 1), lo, hi)))
-        if t == 0:
-            tt(W("q1"), row(4), W("par2"), A.add)
-            cp(W("uq"), W("q1"))
+    def add(t, b, xs, start=False, stop=False, sym=False):
+        for k, m in zip(SUMS[b], (I1 if sym else ISW, I1)):
+            mm([(PS(k, *VB[t][b:b + 2]), ID(m), x) for x in xs], start, stop)
+
+    def own(t, b):
+        lo, hi = VB[t][b:b + 2]
+        add(t, b, [W("vs%d" % t, lo, hi)], True)
+        mm([(PS(SUMS[b][0], lo, hi), ID(IODD), W("one", lo, hi))], False, False)
+        if t == 0 and early:
+            need("t", ("arr20", n_far * len(others), {}))
+            need("t", ("sib20", n_sib(0), {}))
+            add(t, b, [W("vs2", lo, hi), slot(2, len(line), lo, hi)] + landed(2, lo, hi), sym=True)
+
+    def decide(t, b):
+        lo, hi = VB[t][b:b + 2]
+        cut = lambda n: [(lo + (hi - lo) * k // n, lo + (hi - lo) * (k + 1) // n) for k in range(n)]
+        pieces = lambda *fns: [fn(x, y) for fn in fns for x, y in cut(PIECES if hi - lo < NC else 2)]
+        need("t", ("arr%d%d" % (t, b), n_far * len(others), {}))
+        add(t, b, landed(t, lo, hi))
+        need("t", ("sib%d%d" % (t, b), n_sib(hi), {}))
+        add(t, b, [slot(t, len(line), lo, hi)], stop=True)
+        change = [lambda x, y: tt(W("thr", x, y), PS(SUMS[b][0], x, y), W("big", x, y), A.max),
+                  lambda x, y: tt(PS(5, x, y), PS(SUMS[b][1], x, y), W("thr", x, y), A.is_ge)]
+        move = [lambda x, y: tt(PS(6, x, y), *((PS(5, x, y), W("dp", x, y)) if t else (L(7, x, y), row(DL, x, y))), A.mult),
+                lambda x, y: tt(W("p%d" % (t + 1), x, y), PS(6, x, y), W("p%d" % t, x, y), A.add),
+                lambda x, y: cp(W("up", x, y), W("p%d" % (t + 1), x, y))]
+        if t:
+            return pieces(*change, *move)
+        change.append(lambda x, y: tt(row(DL, x, y), PS(5, x, y), row(SG, x, y), A.mult))
+        if hi < NC:
+            return pieces(*change)
+        for f, h in zip(change, move):
+            f(lo, hi)
+            if f is change[-1]:
+                spread("y", 2, DL)
+                mm([(L(9), ID(k), row(n)) for k, n in ((I16, R0), (I1, R1), (I1, DL))])
+            h(0, lo)
+        for f, (x, y) in zip(move, ((0, lo), (lo, hi), (0, 0))):
+            f(lo, hi)
+            tt(row(SW1, x, y), PS(5, x, y), W("swi", x, y), A.not_equal) if y else slots(W("uq"), L(9))
+
+    def true_kids():
+        mm([(PS(0, 96 * k, 96 * k + 96), ID(IN), W("lo", 0, 96)) for k in range(2)], True, False)
+        mm(wrap(PS(0, 0, NC), ZA, "go", 0, NC), False, True)
+        act(W("b2"), PS(0, 0, NC), AF.Abs, col("cs", 1))
+        ts(L(8), W("b2"), 1.0, None, A.is_lt)
+        tt(W("rd"), L(8), W("kdi"), A.mult)
+        ts(W("uk1"), W("rd"), 16.0 - NF, None, A.add)
 
     def observed():
-        for b in range(3):
+        for b in seen:
             mm([(PS(b, 0, 512), ID(I1), R("phs", 512 * b, 512 * b + 512))])
 
-    def parity():
-        cp(R("genb", 0, 96), R("gen1", 0, 96))
-        dma("y", T.g8[0:8, :], T.genb[:], [R("genb", 0, 96)], [R("g8", 0, NP)])
-        ts(W("uk"), W("kdi"), -float(NF), None, A.add)
+    def columns():
+        ts(col("cs", 7), col("i2", 0), -1.0, None, A.mult)
+        for n, (r, v) in enumerate(((3, -32.0), (4, 32.0), (6, 1.0))):
+            ts(col("cs", 3 + n), col("i2", 0), float(r), v, A.is_equal, A.mult)
+        cp(col("cs", 0), col("i2", 0))
+        tt(col("cs", 6), col("cs", 3), col("cs", 4), A.add)
+        ts(col("cs", 1), col("i2", 0), -2.0, -0.5, A.mult, A.add)
+        tt(col("cs", 2), col("cs", 5), col("cs", 6), A.add)
 
     for t in range(2):
-        stages([(win(W1), "up", "wb", W2 + NF, SHARE["p2"], ZA, 0, to("u2"), None),
-                (win(W2), "u2", "w4", 0, SHARE["p4"], ZA, 0, lambda o, c0, c1: ts(W("u4c", c0, c1), o, NF - 1.0, None, A.min), None),
-                (R("xb", FA, FA + NF), "u4c", "xb", X1, SHARE["x1"], None, 0, None, partners(t))])
+        stages([(win(W1), "up", "wb", W2 + NF, even("p2" if t else "p0"), ZA, to("u2"), {2: lambda: t and spread("y", 5, SW1)}),
+                (win(W2), "u2", "w4", 0, even("p4"), ZA, lambda o, c0, c1: ts(W("u4c", c0, c1), o, float(NF), NF - 1.0, A.add, A.min), None),
+                (R("xb", FA, FA + NF), "u4c", "xb", X1, even("x1"), None, None, partners(t))], (3, 4, 6))
         match(t)
-        exchange(t)
         mm([(L(4), R("z8", 14 - 2 * r, 142 - 2 * r, 1, 8), R("g8", r, NP, 8, 8)) for r in range(8)])
         if t == 0:
-            ts(L(6), W("pari"), 1024.0, 191.0, A.is_ge, A.mult)
-            cp(col("cs", 0), col("i2", 0))
-            ts(W("par2"), W("pari"), 2.0, None, A.mult)
-            ts(L(8), row(2), -2.0, 1.0, A.mult, A.add)
-            ts(W("stp"), L(6), 1.0, None, A.add)
-            ts(W("big"), L(4), -999.0, 1000.0, A.mult, A.add)
-            tt(W("dp"), L(8), W("stp"), A.mult)
+            late(3)
+            mm(place(L(6)))
+            columns()
+            ts(W("re"), W("pari"), 1024.0, 191.0, A.is_ge, A.mult)
+            ts(row(SG), W("swi"), -2.0, 1.0, A.mult, A.add)
+            act(W("dp"), row(R1), AF.Identity, col("cs", 7))
+            tt(W("thr"), row(R0), W("lo"), A.subtract)
+            act(W("big"), L(4), AF.Identity, 1000.0, -999.0)
+            tt(L(8), L(4), W("thr"), A.mult)
+            tt(L(9), L(4), W("dp"), A.mult)
+            act(W("p0"), L(6), AF.Identity, float(NF))
+            tt(row(Q0), L(8), W("lo"), A.add)
+            ts(row(Q1), L(9), col("cs", 0), None, A.add)
+            act(L(7), W("re"), AF.Identity, 1.0)
+            true_kids()
+            act(W("stp"), W("re"), AF.Identity, 1.0)
+        for b in range(len(VB[t]) - 1):
+            own(t, b)
+        if t == 0:
+            decide(0, 0)
+            decide(0, 1)
         else:
-            ts(L(6), W("tg0"), col("cs", 0), None, A.add)
-            ts(L(8), row(4), -2.0, 1.0, A.mult, A.add)
-            tt(W("rd"), L(6), W("q1"), A.subtract)
-            ts(L(7), L(4), -1.0, 1.0, A.mult, A.add)
+            act(L(8), row(SW1), AF.Identity, 1.0, -2.0)
+            act(W("big"), L(4), AF.Identity, 1.0, 999.0)
             tt(W("dp"), L(8), W("stp"), A.mult)
-            tt(L(9), L(7), W("rd"), A.mult)
-            ts(W("big"), L(4), 999.0, 1.0, A.mult, A.add)
-            tt(L(6), L(9), W("par2"), A.add)
-            cp(row(6), L(6))
-            spread("y", 0, 6)
-            tt(row(7), L(6), row(6), A.subtract)
-            spread("s", 1, 7)
-        decide(t)
+            decide(1, 0)
 
     def switches():
-        tt(W("b2"), PS(5, 0, NC), row(4), A.not_equal)
+        tt(W("b2"), PS(5, 0, NC), row(SW1), A.not_equal)
         dma("y", T.ys[:], T.b2[:], [W("b2")], [])
 
     def put(o, c0, c1):
-        cp(W("yao", c0, c1), o)
+        slots(W("yao", c0, c1), o)
         if c1 >= CUTS[-2]:
             c0 = c0 if c1 == NC else 0
             dma("y", T.ya[:, c0:c1], ap(W("yao", c0, c1)), [W("yao", c0, c1)], [])
-    stages([(win(W1), "up", "wb", W2 + NF, SHARE["n1"], ZA, 0, to("u2"), {2: switches}),
-            (win(W2), "u2", "wb", W1 + NF, SHARE["n2"], ZA, 0, to("u4"), None),
-            (win(W1), "u4", "w4", 0, SHARE["n4"], ZA, 0, put, None)])
+    split = len(VB[1]) > 2
+    stages([(win(W1), "up", "wb", W2 + NF, LAST if split else even("n1"), ZA, to("u2"), {0: lambda: split and decide(1, 1), len(LAST) - 1: switches}),
+            (win(W2), "u2", "wb", W1 + NF, even("n2"), ZA, to("u4"), None),
+            (win(W1), "u4", "w4", 0, even("n4"), ZA, put, None)], (0, 1, 2))
 
     g.wait_ge(T.sem.sent, sent[0])
     for q in QUEUES:

from concourse.bass import DstId, RemoteDMATransfer
from concourse.mybir import AluOpType as A, ActivationFunctionType as AF

NF, NP, NS, NW, NC = 2048, 1536, 3072, 5120, 192
BF, F32, I32, U16 = "bfloat16", "float32", "int32", "uint16"
ZW = 144
ZA, ZSP, ZSM, ZU, ZB, ZV, ZGP, ZGM, ZP = range(9)
I1, IM, I191, I16, IH, IMH, I2, IK, IN, I02, ID64, IODD, ISW, I0 = range(14)
W1, W2 = 0, NW
FS, XS, FA, X1 = 0, NF, NW, NW + NF
R0, R1, DL, SW1, Q0, Q1, A1, A2, MR, SG = range(10)


def _sb(n, d):
    return ("sbuf", [128, n], d)


SCRATCH = {
    "wb": _sb(2 * NW, BF), "w4": _sb(NS, BF), "xb": _sb(2 * NW, BF), "xc": _sb(NS, BF), "phs": _sb(NP, BF),
    "mb": _sb(NP, BF), "m2": _sb(NS, BF), "m1": _sb(NS, BF), "nb": _sb(NP, BF), "n2": _sb(NS, BF), "n1": _sb(NS, BF),
    "sb": _sb(NP, BF), "s1": _sb(NS, BF), "s2": _sb(NS, BF), "gw": _sb(NS + 16, BF), "go": _sb(NS, BF), "pl": _sb(NS, BF), "ck": _sb(4 * NC, BF),
    "pari": _sb(NC, I32), "swi": _sb(NC, I32), "kdi": _sb(NC, I32), "geni": _sb(96, I32), "gen1": _sb(96, I32), "genb": _sb(96, BF),
    "pa": _sb(NC, I32), "pb": _sb(NC, I32), "rows": _sb(10 * NC, BF), "g8": _sb(NP, BF),
    "stp": _sb(NC, F32), "dp": _sb(NC, F32), "p0": _sb(NC, F32), "p1": _sb(NC, F32), "p2": _sb(NC, F32), "b2": _sb(NC, F32),
    "big": _sb(NC, F32), "thr": _sb(NC, F32), "tk": _sb(NC, F32), "rd": _sb(NC, F32), "re": _sb(NC, F32), "yao": _sb(NC, F32), "ukf": _sb(NC, F32),
    "uq": _sb(NC, U16), "up": _sb(NC, U16), "u2": _sb(NC, U16), "u4": _sb(NC, U16), "u4c": _sb(NC, U16), "uk0": _sb(NC, U16), "uk1": _sb(NC, U16),
    "vs0": _sb(NC, BF), "vs1": _sb(NC, BF), "vs2": _sb(NC, BF),
    "land0": _sb(5 * NC, BF), "land1": _sb(5 * NC, BF), "land2": _sb(5 * NC, BF),
    "i1": _sb(2, I32), "i2": _sb(2, I32), "rt": _sb(2, F32), "cs": _sb(8, F32), "hi": _sb(16, F32), "hc": _sb(16, F32),
    "one": _sb(256, BF), "lo": _sb(256, BF), "zz": _sb(9 * ZW + 16, BF), "z8": _sb(ZW, BF), "idn": _sb(13 * 128 + ZW, BF),
    "ps": ("psum", [128, 4096], F32),
}

CUTS = (0, 64, 128, 192)
SHARE = {"p0": 32, "p2": 32, "p4": 30, "x1": 30, "n1": 30, "n2": 30, "n4": 32}
LEAD = 64
HS = ((0, 96, 144, 192),) * 2
VB = ((0, 96, 192), (0, 96, 192), (0, 192))
LAST = ((0, 96, 28), (96, 144, 24), (144, 192, 24))
SUMS = ((3, 4), (1, 2))
PIECES = 2
GZ = 256
MATCH = (("L.0 X.1 Xv.0 Xv.2 X.3 H.0 T.0 P.11 M.0 X.5 T.1 T.2 P.01 H.1 n.b01 X.4 T.3 M.1 Q1.4 T.4 T.5 H.2 A2.0 d.b11 M.2 d.201 B2.1 sg.b11 D1.4 L.1 L.2 sg.201 "
          "P.21 n.211 d.b21 ab.201 n.221 ab.b11 G.1 A2.3 G.0 sg.b21 G.2 B2.4 C.01 P.41 C.11 P.31 n.231 ab.b21 P.51 n.251 C.21 G.3 n.241 G.5 C.31 B1.0 U0.0 G.4 "
          "C.51 Z.0 C.41 n.102 K.00 A1.2 K.01 U.00 n.121 U0.2 U0.1 Z.1 A1.3 K.20 U.01 V.03 K.10 cl.0 n.131 K.11 AD.0 U.10 E.0 U.20 n.142 K.21 V.31 U.11 U.21 "
          "cl.1 V.42 cl.2 AD.1 AD.2 E.1").split(),
         ("X.1 Xv.0 P.11 Xv.2 X.3 H.0 T.0 T.1 M.0 X.5 H.1 T.2 P.31 M.1 X.4 n.b01 A2.0 P2.5 H.2 T.3 T.4 d.b11 M.2 Q1.4 d.201 F2.5 B2.1 sg.201 D1.4 A2.3 sg.b11 "
          "P.21 n.211 ab.201 P.01 n.222 ab.b11 G.1 G.0 A2.4 C.11 G.3 C.01 G.2 n.b21 P.41 n.241 C.31 P.51 Q.0 Q.1 n.251 C.21 G.4 B1.0 G.5 C.41 Z.0 Z.1 C.51 "
          "A1.2 K.01 n.102 n.121 K.00 U.01 n.142 V.03 K.11 U.00 A1.3 K.10 V.42 E.0 K.21 n.131 U.10 U.11 K.20 U.21 V.31 U.20 E.1").split())
QUEUES = ["v", "s", "t", "g"]
NDMA = 34
SEMAPHORES = (["c_" + q for q in QUEUES] + ["d%d" % i for i in range(NDMA)] + ["sent"]
              + ["%s%d%d" % (n, t, b) for n in ("arr", "sib") for t in range(3) for b in range(3)]
              + ["%s%d%d" % (n, t, b) for n in ("hin", "hout") for t in range(2) for b in range(6)])


def folds(t):
    return [(x[1], 512 * int(x[-1]), 512 * (int(x[-1]) + 1 + (x[0] == "D"))) for x in MATCH[t] if x[0] in "FD"]


def helper_of(c, T, topo):
    return [h for h in topo.cores_of(c) if h not in T.cores and topo.die(h) == topo.die(c)][0]


def hand_back(g, core, T, topo):
    for c in T.cores:
        if helper_of(c, T, topo) == core:
            n, sent = len(topo.engines(core, c)), 0
            rid, pid = topo.addr(c, core)
            for t in range(2):
                for k, (kind, lo, hi) in enumerate(folds(t)):
                    g.wait_ge(T.sem["hin%d%d" % (t, k)], n)
                    g.remote_dma(T["m" + kind][:, lo:hi], T["mn"[t] + kind][:, lo:hi], T.sem["hout%d%d" % (t, k)], T.sem.sent, pid, rid, topo.mask(core, c))
                    sent += n
            if sent:
                g.wait_ge(T.sem.sent, sent)


def rank_program(g, core, T, topo):
    rank = T.rank_of(core)
    if rank is None:
        return hand_back(g, core, T, topo)
    Q = {"v": g.vector, "s": g.scalar, "t": g.tensor, "g": g, "y": g.sync}
    cnt = {q: 0 for q in QUEUES}
    known = {q: {} for q in Q}
    recs = {}
    ndma = [0]

    def R(name, lo, hi, step=1, p=128, row=None):
        return (name, lo, hi, step, p, row)

    def ap(r):
        return T[r[0]][0:r[4], r[1]:r[2]:r[3]] if r[3] > 1 else T[r[0]][0:r[4], r[1]:r[2]]

    def need(q, tok):
        if known[q].get(tok[0], 0) < tok[1]:
            Q[q].wait_ge(T.sem[tok[0]], tok[1])
            known[q][tok[0]] = tok[1]
            for k, v in tok[2].items():
                if known[q].get(k, 0) < v:
                    known[q][k] = v

    def op(q, fn, reads, writes, dma=False, done=None):
        deps = {}
        for rs, w in ((reads, False), (writes, True)):
            for r in rs:
                for (lo, hi, tok, eq, ew, st, row) in recs.get(r[0], []):
                    hit = lo < r[2] and r[1] < hi and (w or ew) and not (st == r[3] and (lo - r[1]) % st) and (row == r[5] or None in (row, r[5]))
                    if r[0] == "ps":
                        if eq != q:
                            hit = lo // 512 <= (r[2] - 1) // 512 and r[1] // 512 <= (hi - 1) // 512
                        elif q == "t":
                            hit = False
                    if hit and deps.get(tok[0], (0, 0))[1] < tok[1]:
                        deps[tok[0]] = tok
        for tok in sorted(deps.values(), key=lambda t: t[0] == "c_" + q):
            need(q, tok)
        ins = fn()
        if done:
            tok = done + (dict(known[q]),)
        elif dma:
            name = "d%d" % ndma[0]
            ndma[0] += 1
            ins.then_inc(T.sem[name], 16)
            tok = (name, 16, dict(known[q]))
        else:
            cnt[q] += 1
            ins.then_inc(T.sem["c_" + q], 1)
            tok = ("c_" + q, cnt[q], dict(known[q]))
        for rs, w in ((reads, False), (writes, True)):
            for r in rs:
                l = recs.setdefault(r[0], [])
                if w and r[3] == 1 and r[0] != "ps":
                    l[:] = [x for x in l if not (r[1] <= x[0] and x[1] <= r[2] and r[5] in (None, x[6]))]
                elif r[0] == "ps":
                    l[:] = [x for x in l if not (x[3] == q and r[1] // 512 <= x[0] // 512 and (x[1] - 1) // 512 <= (r[2] - 1) // 512
                                                 and (q == "t" or known[q].get(x[2][0], 0) >= x[2][1]))]
                l.append((r[1], r[2], tok, "dma" if dma or done else q, w, r[3], r[5]))
        return tok

    def ts(out, in0, s1, s2, o0, o1=None):
        rd = [in0] + [s for s in (s1, s2) if isinstance(s, tuple)]
        a1, a2 = [ap(s) if isinstance(s, tuple) else s for s in (s1, s2)]
        if o1 is None:
            return op("v", lambda: g.vector.tensor_scalar(ap(out), ap(in0), a1, None, o0), rd, [out])
        return op("v", lambda: g.vector.tensor_scalar(ap(out), ap(in0), a1, a2, o0, o1), rd, [out])

    def tt(out, a, b, o):
        return op("v", lambda: g.vector.tensor_tensor(ap(out), ap(a), ap(b), o), [a, b], [out])

    def cp(out, a):
        return op("v", lambda: g.vector.tensor_copy(ap(out), ap(a)), [a], [out])

    def fill(out, v):
        return op("v", lambda: g.vector.memset(ap(out), v), [], [out])

    def act(out, a, f, bias=None, scale=None):
        kw = {}
        if bias is not None:
            kw["bias"] = ap(bias) if isinstance(bias, tuple) else bias
        if scale is not None:
            kw["scale"] = ap(scale) if isinstance(scale, tuple) else scale
        return op("s", lambda: g.scalar.activation(ap(out), ap(a), f, **kw), [a] + [x for x in (bias, scale) if isinstance(x, tuple)], [out])

    def gather(q, out, win, off, other=None):
        src = lambda: ap(win).indirect(ap(off))
        if other is not None:
            return op("v", lambda: g.vector.tensor_tensor(ap(out), src(), ap(other), A.max), [win, off, other], [out])
        if q == "v":
            return op("v", lambda: g.vector.tensor_copy(ap(out), src()), [win, off], [out])
        return op("s", lambda: g.scalar.activation(ap(out), src(), AF.Copy), [win, off], [out])

    def mm(items, start=True, stop=True):
        def fn():
            for n, (o, l, r) in enumerate(items):
                ins = g.tensor.matmul(ap(o), ap(l), ap(r), start and n == 0, stop and n == len(items) - 1)
            return ins
        return op("t", fn, [x for it in items for x in it[1:]], [it[0] for it in items])

    def iota(out, pat, base, cm, small=True):
        kw = {"allow_small_or_imprecise_dtypes": True} if small else {}
        return op("g", lambda: g.iota(ap(out), pat, base, cm, **kw), [], [out])

    def asel(out, a, pat, cmp, fill, base, cm):
        return op("g", lambda: g.affine_select(ap(out), ap(a), pat, cmp, fill, base, cm), [a], [out])

    def gcopy(out, a):
        return asel(out, a, [[0, len(range(a[1], a[2], a[3]))]], A.is_ge, 0.0, 0, 0)

    def dma(q, out, in_, reads, writes):
        return op(q, lambda: Q[q].dma_start(out, in_), reads, writes, dma=True)

    def PS(b, lo, hi, step=1):
        return R("ps", 512 * b + lo, 512 * b + hi, step)

    def Z(s, i):
        return R("zz", s * ZW + 15 - i, s * ZW + 143 - i)

    def ID(k):
        return R("idn", 128 * k, 128 * k + 128)

    def col(name, k):
        return R(name, k, k + 1)

    def wrap(out, s, src, lo, n, flip=0):
        return [(out, Z(s, i ^ flip), R(src, lo + i, lo + 16 * n, 16)) for i in range(16)]

    W = lambda n, lo=0, hi=NC: R(n, lo, hi)
    win = lambda base: R("wb", base, base + NW)
    row = lambda n, lo=0, hi=NC: R("rows", NC * n + lo, NC * n + hi)
    L = lambda n, lo=0, hi=NC: PS(3 + n // 2, NC * (n % 2) + lo, NC * (n % 2) + hi)
    slots = lambda out, o: ts(out, o, float(NF), None, A.add)

    def spread(q, r, n):
        dma(q, T.wb[r::16, W1 + NF:W1 + NW], ap(row(n)), [row(n)], [R("wb", W1 + NF, W1 + NW, 1, 128, r)])

    dma("y", T.pari[:], T.par[:], [], [W("pari")])
    dma("y", T.swi[:], T.sw[:], [], [W("swi")])
    dma("y", T.geni[:], T.gen[:], [], [R("geni", 0, 96)])
    dma("y", T.kdi[:], T.kd[:], [], [W("kdi")])
    iota(R("i1", 0, 2), [[-1, 2]], 16, 1, False)
    iota(R("hi", 0, 16), [[16, 16]], -128, 0)
    persons = lambda lo, hi: R("wb", W1 + NF + lo, W1 + NF + hi)
    fill(R("one", 0, 256), 1.0)
    fill(persons(0, 256), 0.0)
    ts(R("i2", 0, 2), R("i1", 0, 2), 15, None, A.bitwise_and)
    op("v", lambda: g.vector.tensor_tensor_scan(T.lo[:], T.one[:], T.one[:], -1.0, A.add, A.mult), [R("one", 0, 256)], [R("lo", 0, 256)])
    ts(R("rt", 0, 2), R("i2", 0, 2), 0.0, None, A.is_equal)
    act(persons(256, 512), persons(0, 256), AF.Copy)
    act(persons(512, 1024), persons(0, 512), AF.Copy)
    fill(persons(1024, 1280), 0.0)
    ts(R("hc", 0, 16), R("hi", 0, 16), col("rt", 0), None, A.mult)
    fill(persons(1280, 1536), 0.0)
    for j in range(2):
        ts(R("wb", W1 + 256 * j, W1 + 256 * j + 256), R("lo", 0, 256), col("rt", 1), col("hc", j), A.mult, A.add)
    fill(persons(1536, NS - GZ), 0.0)
    act(R("wb", W1 + 512, W1 + 1024), R("wb", W1, W1 + 512), AF.Identity, col("hc", 10))
    act(R("wb", W1 + 1024, W1 + NF), R("wb", W1, W1 + 1024), AF.Identity, col("hc", 12))

    zc = lambda s, c=15: R("zz", s * ZW + c, s * ZW + c + 128, 16)
    ident = lambda k, v: asel(ID(k), ID(I0), [[-1, 128]], A.not_equal, v, 0, 1)
    diag = lambda k: asel(ID(k), ID(k), [[-1, 128]], A.is_equal, 0.0, 0, 1)
    rows = lambda s, n, v, c=15: asel(zc(s, c), zc(s, c), [[16, 8]], A.is_gt, v, n, -1)
    clear = lambda s0, s1: iota(R("zz", s0 * ZW, s1 * ZW), [[0, (s1 - s0) * ZW]], 0, 0)
    iota(R("idn", 128 * I0, 128 * I0 + ZW), [[0, ZW]], 0, 0)
    if GZ:
        iota(persons(NS - GZ, NS), [[0, GZ]], 0, 0)
    for k, v in ((I1, 1.0), (I191, 191.0)):
        ident(k, v)
    clear(ZA, ZA + 1)
    ident(I16, 16.0)
    for n, v in ((0, 16.0), (1, 1.0), (3, 0.0)):
        rows(ZA, n, v)

    ts(W("pb"), W("pari"), 7, None, A.bitwise_and)
    ts(W("pa"), W("pari"), 3, None, A.arith_shift_right)
    ts(L(0), W("pb"), 2.0, None, A.mult)
    ts(row(R0), W("pa"), -128.0, None, A.add)
    spread("y", 0, R0)
    tt(row(R1), L(0), W("swi"), A.add)
    spread("y", 1, R1)
    ts(L(2), W("pari"), 1024.0, None, A.is_ge)
    ts(row(A1), row(R0), 0.0, None, A.max)
    tt(row(MR), L(2), row(R1), A.mult)
    ts(row(A2), row(R0), 0.0, 16.0, A.min, A.mult)
    place = lambda o: [(o, ID(k), row(n)) for k, n in ((I1, R1), (I1, A1), (I191, MR), (I1, A2))]
    mm(place(PS(0, 0, NC)))
    mm([(PS(1, 0, NC), ID(k), row(n)) for k, n in ((I16, R0), (I1, R1))])
    ts(R("gen1", 0, 96), R("geni", 0, 96), 1, None, A.bitwise_and)
    ts(W("uk0"), W("kdi"), 16.0 - NF, None, A.add)
    cp(R("genb", 0, 96), R("gen1", 0, 96))
    fill(R("gw", 0, 16), 0.0)
    slots(W("up"), PS(0, 0, NC))
    slots(W("uq"), PS(1, 0, NC))
    act(R("wb", W2, W2 + 1024), R("wb", W1, W1 + 1024), AF.Copy)
    dma("y", ap(R("xb", FA, FA + NF)), T.fa[:], [], [R("xb", FA, FA + NF)])
    dma("y", T.phs[:], T.ph[:], [], [R("phs", 0, NP)])
    dma("y", T.g8[0:8, :], T.genb[:], [R("genb", 0, 96)], [R("g8", 0, NP)])

    gcopy(R("wb", W2 + 1024, W2 + NF), R("wb", W1 + 1024, W1 + NF))
    clear(ZSP, ZV)
    for k, v in ((IH, 0.5), (IMH, -0.5)):
        ident(k, v)
    for s, n, v in ((ZSP, 0, 1.0), (ZSM, 0, -1.0), (ZSP, 16, 0.0), (ZSM, 16, 0.0)):
        rows(s, n, v)
    for e in range(2):
        gcopy(R("xb", FS + e, FS + NF, 2), R("xb", FA + 1 - e, FA + NF, 2))
    asel(ID(I02), ID(I1), [[0, 8], [-1, 16]], A.is_ge, 0.0, 2, 0)
    for c in (14, 15):
        gcopy(zc(ZB, c), zc(ZSP))

    def late(c):
        if c == 0:
            iota(ID(ID64), [[0, 8], [-64, 16]], 0, 0)
            rows(ZU, 0, 1024.0)
            for n, v, k, u in ((1, 64.0, IK, -1024.0), (3, 1.0, I2, 2.0), (4, 0.0, IM, -1.0)):
                ident(k, u)
                rows(ZU, n, v)
            diag(ID64)
            gcopy(zc(ZU, 14), zc(ZU))
        elif c == 1:
            iota(ID(IODD), [[0, 64], [1, 2]], 0, 0)
            z8 = R("z8", 0, ZW, 1, 8)
            asel(z8, R("idn", 128 * I0, 128 * I0 + ZW, 1, 8), [[1, ZW]], A.not_equal, 1.0, -15, -16)
            diag(IODD)
            asel(z8, z8, [[1, ZW]], A.not_equal, 1.0, -14, -16)
            for e in range(2):
                asel(R("idn", 128 * ISW + e, 128 * ISW + 128, 2), R("idn", 128 * I0, 128 * I0 + 64), [[-2, 64]], A.not_equal, 1.0, e - 1, 1)
        elif c == 2:
            ident(IN, -32.0)
        else:
            clear(ZV, ZP + 1)
            one_row = ((ZV, 14, 4, -1.0), (ZV, 15, 3, 1.0), (ZP, 15, 5, 64.0), (ZP, 16, 5, -64.0), (ZP, 17, 5, 1.0), (ZP, 18, 5, -1.0),
                       (ZV, 14, 6, 32.0), (ZV, 15, 5, -32.0))
            for part in (one_row[:6], one_row[6:]):
                for d in range(2):
                    for s, c, n, v in part:
                        rows(s, n + d, 0.0 if d else v, c)
            for s, c, z in ((ZGP, 15, ZSP), (ZGP, 16, ZSM), (ZGM, 15, ZSM), (ZGM, 16, ZSP)):
                gcopy(zc(s, c), zc(z))

    def even(name):
        return [(c0, c1, SHARE[name] * (c1 - c0) // 128 * 2) for c0, c1 in zip(CUTS, CUTS[1:])]

    def stages(todo, banks):
        wait, nb = [], 0
        for k, (w, off, dst, lo, cuts, zs, take, extra) in enumerate(todo):
            for n, (c0, c1, share) in enumerate(cuts):
                while wait and wait[0][0] < k and wait[0][1] < c1 + LEAD:
                    wait.pop(0)[2]()
                a = c0 + share
                gather("v", R(dst, lo + 16 * c0, lo + 16 * a), w, R(off, c0, a))
                gather("s", R(dst, lo + 16 * a, lo + 16 * c1), w, R(off, a, c1))
                if extra and n in extra:
                    extra[n]()
                if zs is not None:
                    o = PS(banks[nb % 3], 0, c1 - c0)
                    nb += 1
                    mm(wrap(o, zs, dst, lo + 16 * c0, c1 - c0))
                    wait.append((k, c0, lambda o=o, c0=c0, c1=c1, take=take: take(o, c0, c1)))
        for x in wait:
            x[2]()

    to = lambda name: (lambda o, c0, c1: slots(W(name, c0, c1), o))

    def partners(t):
        bank = lambda n: PS((5, 7, 5)[n], CUTS[n], CUTS[n + 1])
        lists = lambda ns: [mm(wrap(bank(n), ZA, "w4", 16 * CUTS[n], CUTS[n + 1] - CUTS[n], 1)) for n in ns]
        casts = lambda ns: [slots(W("u4", CUTS[n], CUTS[n + 1]), bank(n)) for n in ns]
        return {0: lambda: lists((0, 1)),
                1: lambda: (casts((0,)), lists((2,))),
                2: lambda: (casts((1, 2)), observed())}

    near = [c for c in T.cores if c != core and c in topo.cores_of(core)]
    line = [c for c in T.cores if topo.die(c) == topo.die(core)]
    others = [c for c in line if c != core]
    me = line.index(core)
    n_far, n_all = len(topo.engines(core, others[0])), len(topo.engines(core, near[0]))
    sent = [0]
    ids = lambda cs: [DstId(rid=topo.addr(c, core)[0], pnc=topo.addr(c, core)[1]) for c in cs]
    slot = lambda t, n, lo, hi: R("land%d" % t, NC * n + lo, NC * n + hi)
    landed = lambda t, lo, hi: [slot(t, n, lo, hi) for n in range(len(line)) if n != me]

    def remote(cs, sem, srcs, dst, reads, writes=(), done=None, alu=0, spare=0):
        mask = topo.mask(core, cs[0]) & ~spare
        sent[0] += bin(mask).count("1")
        tr = RemoteDMATransfer(dst_ids=ids(cs), dma_engine_mask=mask, remote_sem=T.sem[sem], srcs=[ap(x) for x in srcs], dsts=[ap(dst)] * len(cs), alu_op=alu)
        op("g", lambda: g.remote_dma_fused([tr], local_sem=T.sem.sent), reads, list(writes), done=done or ("sent", 10 ** 6))

    def send(t, b):
        lo, hi = VB[t][b:b + 2]
        remote(others, "arr%d%d" % (t, b), [W("vs%d" % t, lo, hi)], slot(t, me, lo, hi), [W("vs%d" % t, lo, hi)])

    def fold(t, b):
        lo, hi = VB[t][b:b + 2]
        need("g", ("arr%d%d" % (t, b), n_far * len(others), {}))
        remote(near, "sib%d%d" % (t, b), [W("vs%d" % t, lo, hi)] + landed(t, lo, hi), slot(t, len(line), lo, hi), [], alu=1,
               spare=topo.mask(core, others[0]) if hi < NC or t == 2 else 0)
    n_sib = lambda hi: n_all - n_far if hi < NC else n_all
    early = "Y" in MATCH[0]

    seen = sorted({(int(x[3]) + h) // (1 if x[2] == "b" else 2) for m in MATCH for x in m if x[:2] == "n." for h in range(int(x[4]))})

    def match(t):
        held, free = {}, [b for b in range(7) if b not in seen]
        order, plain = MATCH[t], {"1": "pl", "2": "w4"}
        vb = lambda c: max(b for b in range(len(VB[t]) - 1) if VB[t][b] <= c)
        first = {"V": lambda c: 32 * int(c[0]), "U": lambda c: HS[t][int(c[0])], "AD": lambda c: HS[t][int(c[0])]}
        last = {vb(first[k](c)): k + "." + c for k, c in (x.split(".") for x in order if "." in x) if k in ("V", "U" if t else "AD")}
        copies = {int(x[2]) + n: x[2:] for x in order if x[:2] == "P." for n in range(int(x[3]))}

        def take(key, n):
            if key not in held:
                held[key] = min((b for b in free if n == 1 or b + 1 in free), key=lambda b: max(free.index(b + i) for i in range(n)))
                for i in range(n):
                    free.remove(held[key] + i)
            return held[key]

        def drop(key, n):
            free.extend(range(held[key], held[key] + n))
        votes = lambda lo, hi: PS(take("votes%d" % vb(lo), 1) if vb(lo) else 7, lo, hi)
        for step in order:
            k, c = (step.split(".") + ["0"])[:2]
            if k in ("d", "sg", "ab", "nz", "n"):
                kind, w, lo = c[0], int(c[2]), 512 * int(c[1])
                st = 1 if kind == "b" else 2
                blk = lambda n, e=0, st=1: R(n + kind, lo + e, lo + 512 * w, st)
                if k == "n":
                    for e in range(st):
                        tt(blk("n", e, st), PS(0, lo // st, (lo + 512 * w) // st), blk("m", e, st), A.not_equal)
                elif k == "d":
                    for h in range(w):
                        b, a = take(c, w) + h, lo + 512 * h
                        mm([(PS(b, 0, 512), ID(IH), R("m" + kind, a, a + 512))]
                           + [(PS(b, e, 512, st), ID(IMH), R("phs", a // st, (a + 512) // st)) for e in range(st)])
                elif k == "sg":
                    act(blk("s"), PS(held[c], 0, 512 * w), AF.Sign)
                    drop(c, w)
                elif k == "ab":
                    act(blk("n"), blk("s"), AF.Abs)
                else:
                    ts(blk("n"), blk("s"), 0.0, None, A.not_equal)
                continue
            if k in ("P", "C", "V"):
                c0, w = int(c[0]), int(c[1])
                if k == "P":
                    for b in range(c0, c0 + w):
                        lo = W1 + NF + 32 * b
                        mm([(PS(take("C" + c, w) + b - c0, i, 512, 16), Z(ZP, 3) if t else ID(I02), R("wb", lo + NC * i, lo + NC * i + 32)) for i in range(16)],
                           True, False)
                elif k == "C":
                    act(R("gw", 16 + 512 * c0, 16 + 512 * (c0 + w)), PS(held["C" + c], 0, 512 * w), *((AF.Relu, col("cs", 2)) if t else (AF.Copy,)))
                    drop("C" + c, w)
                else:
                    mm(wrap(votes(32 * c0, 32 * (c0 + w)), ZSM, "n1", 512 * c0, 32 * w), False, step in last.values())
                continue
            if k in ("K", "Kv", "U"):
                b, e = int(c[0]), int(c[1])
                h0, h1 = HS[t][b:b + 2]
                lo, hi = NP * e + 8 * h0, NP * e + 8 * h1
                if k != "U":
                    gather("s" if k == "K" else "v", R("go", lo, hi), R("gw", 0, NS + 16), R("uk%d" % t, lo // 16, hi // 16))
                elif t:
                    mm([(votes(h0, h1), Z(ZV, 2 * r + 1), R("go", lo + r, hi, 8)) for r in range(8)], False, step in last.values())
                else:
                    mm([(PS(held["U0.%d" % b], (h1 - h0) * e, (h1 - h0) * (e + 1)), Z(ZU, 2 * r + 1), R("go", lo + r, hi, 8)) for r in range(8)], False, e == 1)
                continue
            c = int(c)
            ch = lambda n, lo=0, w=512: R(n, lo + w * c, lo + w * c + w)
            h0, h1 = HS[t][c:c + 2] if k in ("U0", "cl", "AD") else VB[t][c:c + 2] if k in ("Z", "E", "Es") else (0, NC)
            hn = h1 - h0
            wide = lambda n, lo=0: R(n, lo + 512 * c, lo + 512 * (c + 1 + (k[0] in "BQD")))
            if k in ("X", "Xv"):
                gather("s" if k == "X" else "v", ch("xb", XS), R("xb", FA, FA + NW), ch("u4", 0, 32))
            elif k == "T":
                dma("y", ap(ch("xc")), ap(ch("xb", XS)), [ch("xb", XS)], [ch("xc")])
            elif k == "L":
                late(c)
            elif k == "Q":
                spread("y", c, (Q0, Q1)[c])
            elif k == "H":
                mm([(PS(7 if c == 2 else take(step, 1), 0, 512), ID(I1), R("xb", XS + 1024 * c, XS + 1024 * c + 1024, 2))])
            elif k == "M":
                tt(ch("mb"), PS(7 if c == 2 else held["H.%d" % c], 0, 512), R("xb", XS + 1024 * c + 1, XS + 1024 * c + 1024, 2), A.max)
                if c < 2:
                    drop("H.%d" % c, 1)
            elif k in ("A1", "A2", "B1", "B2", "P1", "Q1", "P2", "Q2"):
                o = wide(plain[k[1]] if k[0] in "PQ" else "m" + k[1])
                off = R("uq" if k[1] == "1" else "u2", o[1] // 16, o[2] // 16)
                gather("s", o, R("xb", FS, FS + NW), off, None if k[0] in "PQ" else wide("xc"))
            elif k in ("F1", "D1", "F2", "D2"):
                n, srcs = folds(t).index((k[1],) + wide("")[1:3]), [wide(plain[k[1]]), wide("xb", XS)]
                remote([helper_of(core, T, topo)], "hin%d%d" % (t, n), srcs, wide("mn"[t] + k[1]), srcs, [wide("m" + k[1])], ("hout%d%d" % (t, n), n_all), 2)
            elif k == "G":
                b = held["C" + copies[c]] + c - int(copies[c][0])
                mm([(PS(b, n, 512, 2), Z((ZSP, ZGP)[t], 3), ch("nb", 0, 256)) for n in range(2)] + [(PS(b, 0, 512), Z((ZSM, ZGM)[t], 3), ch("n2"))], False, True)
            elif k in ("Y", "Z"):
                o = votes(h0, h1)
                if t == 0 and k == "Z" and early:
                    mm([(o, ID(I0), W("one", h0, h1))], True, False)
                else:
                    mm([(o, Z(ZB, 2 * r + 1), R("nb", 8 * h0 + r, 8 * h1, 8)) for r in range(8)], True, k == "Y")
            elif k == "Yc":
                act(W("vs2"), PS(7, 0, NC), AF.Copy)
                send(2, 0)
            elif k == "Yf":
                fold(2, 0)
            elif k == "U0":
                b = take(step, 1)
                mm([(PS(b, 0, 2 * hn), ID(ID64), R("one", 0, 2 * hn))]
                   + [(PS(b, hn * x, hn * x + hn), ID(IK), R("lo", h0, h1)) for x in range(2)], True, False)
            elif k == "cl":
                for x, v in enumerate((16.0, 32.0)):
                    ts(R("ck", 4 * h0 + 2 * hn * x, 4 * h0 + 2 * hn * (x + 1)), PS(held["U0.%d" % c], 0, 2 * hn), -v, v, A.max, A.min)
                drop("U0.%d" % c, 1)
            elif k == "AD":
                mm([(votes(h0, h1), ID((I2, IM)[x // 2]), R("ck", 4 * h0 + hn * x, 4 * h0 + hn * x + hn)) for x in range(4)], False, step in last.values())
            elif k in ("E", "Es"):
                cp(W("vs%d" % t, h0, h1), votes(h0, h1)) if k == "E" else act(W("vs%d" % t, h0, h1), votes(h0, h1), AF.Copy)
                send(t, c)
        for b in range(len(VB[t]) - 1):
            fold(t, b)

    def add(t, b, xs, start=False, stop=False, sym=False):
        for k, m in zip(SUMS[b], (I1 if sym else ISW, I1)):
            mm([(PS(k, *VB[t][b:b + 2]), ID(m), x) for x in xs], start, stop)

    def own(t, b):
        lo, hi = VB[t][b:b + 2]
        add(t, b, [W("vs%d" % t, lo, hi)], True)
        mm([(PS(SUMS[b][0], lo, hi), ID(IODD), W("one", lo, hi))], False, False)
        if t == 0 and early:
            need("t", ("arr20", n_far * len(others), {}))
            need("t", ("sib20", n_sib(0), {}))
            add(t, b, [W("vs2", lo, hi), slot(2, len(line), lo, hi)] + landed(2, lo, hi), sym=True)

    def decide(t, b):
        lo, hi = VB[t][b:b + 2]
        cut = lambda n: [(lo + (hi - lo) * k // n, lo + (hi - lo) * (k + 1) // n) for k in range(n)]
        pieces = lambda *fns: [fn(x, y) for fn in fns for x, y in cut(PIECES if hi - lo < NC else 2)]
        need("t", ("arr%d%d" % (t, b), n_far * len(others), {}))
        add(t, b, landed(t, lo, hi))
        need("t", ("sib%d%d" % (t, b), n_sib(hi), {}))
        add(t, b, [slot(t, len(line), lo, hi)], stop=True)
        change = [lambda x, y: tt(W("thr", x, y), PS(SUMS[b][0], x, y), W("big", x, y), A.max),
                  lambda x, y: tt(PS(5, x, y), PS(SUMS[b][1], x, y), W("thr", x, y), A.is_ge)]
        move = [lambda x, y: tt(PS(6, x, y), *((PS(5, x, y), W("dp", x, y)) if t else (L(7, x, y), row(DL, x, y))), A.mult),
                lambda x, y: tt(W("p%d" % (t + 1), x, y), PS(6, x, y), W("p%d" % t, x, y), A.add),
                lambda x, y: cp(W("up", x, y), W("p%d" % (t + 1), x, y))]
        if t:
            return pieces(*change, *move)
        change.append(lambda x, y: tt(row(DL, x, y), PS(5, x, y), row(SG, x, y), A.mult))
        if hi < NC:
            return pieces(*change)
        for f, h in zip(change, move):
            f(lo, hi)
            if f is change[-1]:
                spread("y", 2, DL)
                mm([(L(9), ID(k), row(n)) for k, n in ((I16, R0), (I1, R1), (I1, DL))])
            h(0, lo)
        for f, (x, y) in zip(move, ((0, lo), (lo, hi), (0, 0))):
            f(lo, hi)
            tt(row(SW1, x, y), PS(5, x, y), W("swi", x, y), A.not_equal) if y else slots(W("uq"), L(9))

    def true_kids():
        mm([(PS(0, 96 * k, 96 * k + 96), ID(IN), W("lo", 0, 96)) for k in range(2)], True, False)
        mm(wrap(PS(0, 0, NC), ZA, "go", 0, NC), False, True)
        act(W("b2"), PS(0, 0, NC), AF.Abs, col("cs", 1))
        ts(L(8), W("b2"), 1.0, None, A.is_lt)
        tt(W("rd"), L(8), W("kdi"), A.mult)
        ts(W("uk1"), W("rd"), 16.0 - NF, None, A.add)

    def observed():
        for b in seen:
            mm([(PS(b, 0, 512), ID(I1), R("phs", 512 * b, 512 * b + 512))])

    def columns():
        ts(col("cs", 7), col("i2", 0), -1.0, None, A.mult)
        for n, (r, v) in enumerate(((3, -32.0), (4, 32.0), (6, 1.0))):
            ts(col("cs", 3 + n), col("i2", 0), float(r), v, A.is_equal, A.mult)
        cp(col("cs", 0), col("i2", 0))
        tt(col("cs", 6), col("cs", 3), col("cs", 4), A.add)
        ts(col("cs", 1), col("i2", 0), -2.0, -0.5, A.mult, A.add)
        tt(col("cs", 2), col("cs", 5), col("cs", 6), A.add)

    for t in range(2):
        stages([(win(W1), "up", "wb", W2 + NF, even("p2" if t else "p0"), ZA, to("u2"), {2: lambda: t and spread("y", 5, SW1)}),
                (win(W2), "u2", "w4", 0, even("p4"), ZA, lambda o, c0, c1: ts(W("u4c", c0, c1), o, float(NF), NF - 1.0, A.add, A.min), None),
                (R("xb", FA, FA + NF), "u4c", "xb", X1, even("x1"), None, None, partners(t))], (3, 4, 6))
        match(t)
        mm([(L(4), R("z8", 14 - 2 * r, 142 - 2 * r, 1, 8), R("g8", r, NP, 8, 8)) for r in range(8)])
        if t == 0:
            late(3)
            mm(place(L(6)))
            columns()
            ts(W("re"), W("pari"), 1024.0, 191.0, A.is_ge, A.mult)
            ts(row(SG), W("swi"), -2.0, 1.0, A.mult, A.add)
            act(W("dp"), row(R1), AF.Identity, col("cs", 7))
            tt(W("thr"), row(R0), W("lo"), A.subtract)
            act(W("big"), L(4), AF.Identity, 1000.0, -999.0)
            tt(L(8), L(4), W("thr"), A.mult)
            tt(L(9), L(4), W("dp"), A.mult)
            act(W("p0"), L(6), AF.Identity, float(NF))
            tt(row(Q0), L(8), W("lo"), A.add)
            ts(row(Q1), L(9), col("cs", 0), None, A.add)
            act(L(7), W("re"), AF.Identity, 1.0)
            true_kids()
            act(W("stp"), W("re"), AF.Identity, 1.0)
        for b in range(len(VB[t]) - 1):
            own(t, b)
        if t == 0:
            decide(0, 0)
            decide(0, 1)
        else:
            act(L(8), row(SW1), AF.Identity, 1.0, -2.0)
            act(W("big"), L(4), AF.Identity, 1.0, 999.0)
            tt(W("dp"), L(8), W("stp"), A.mult)
            decide(1, 0)

    def switches():
        tt(W("b2"), PS(5, 0, NC), row(SW1), A.not_equal)
        dma("y", T.ys[:], T.b2[:], [W("b2")], [])

    def put(o, c0, c1):
        slots(W("yao", c0, c1), o)
        if c1 >= CUTS[-2]:
            c0 = c0 if c1 == NC else 0
            dma("y", T.ya[:, c0:c1], ap(W("yao", c0, c1)), [W("yao", c0, c1)], [])
    split = len(VB[1]) > 2
    stages([(win(W1), "up", "wb", W2 + NF, LAST if split else even("n1"), ZA, to("u2"), {0: lambda: split and decide(1, 1), len(LAST) - 1: switches}),
            (win(W2), "u2", "wb", W1 + NF, even("n2"), ZA, to("u4"), None),
            (win(W1), "u4", "w4", 0, even("n4"), ZA, put, None)], (0, 1, 2))

    g.wait_ge(T.sem.sent, sent[0])
    for q in QUEUES:
        need("g", ("c_" + q, cnt[q], {}))
    for n in range(ndma[0]):
        need("g", ("d%d" % n, 16, {}))
